import numpy as np
import ml_dtypes


def mxq(x, axis, fmt="e4m3"):
    dtype, down = {"e4m3": (ml_dtypes.float8_e4m3fn, 7), "e5m2": (ml_dtypes.float8_e5m2, 14)}[fmt]
    v = np.moveaxis(np.asarray(x, np.float32).astype(ml_dtypes.bfloat16).astype(np.float64), axis, -1)
    blocks = v.reshape(v.shape[:-1] + (-1, 32))
    amax = np.abs(blocks).max(-1, keepdims=True)
    byte = np.maximum(np.where(amax > 0, np.frexp(amax)[1] - 1 + 127, 0) - down, 1)
    scale = np.exp2(byte - 127.0)
    codes = (blocks / scale).astype(np.float32).astype(dtype).astype(np.float64)
    return np.moveaxis((codes * scale).reshape(v.shape), -1, axis)


WIDE = False


def mx_kscale(k):
    if not WIDE:
        return np.ones(k)
    levels = np.array([10, -10, 5, -5, 0])
    if k % 512:
        return np.exp2(np.random.permutation(np.resize(levels, k // 32))).repeat(32)
    a = np.empty((k // 512, 16))
    for p in range(k // 512):
        a[p, :8] = np.random.permutation(np.resize(levels, 8))
        for g in range(8):
            far = levels[np.abs(levels - a[p, g]) >= 10]
            a[p, g + 8] = far[np.random.randint(len(far))]
    return np.exp2(a.ravel()).repeat(32)


def f64(x):
    return np.asarray(x).astype(np.float64)


def striped(idx):
    return np.tile(idx.reshape(-1, 16).T, (8, 1)).astype(np.uint16)


def unstriped(offs):
    return offs[:16].T.reshape(-1).astype(np.int64)


def pack_weight(w):
    k, n = w.shape
    w = f64(np.asarray(w, np.float32).astype(ml_dtypes.bfloat16)).reshape(k // 32, 32, n)
    amax = np.abs(w).max(1)
    byte = np.clip(np.where(amax > 0, np.frexp(amax)[1] - 1 + 127 - 7, 1), 1, 254)
    scaled = (w * np.exp2(127.0 - byte)[:, None, :]).reshape(k, n).astype(np.float32)
    words = np.ascontiguousarray(scaled.reshape(k // 512, 128, 4, n).transpose(0, 1, 3, 2)).astype(ml_dtypes.float8_e4m3fn).view(np.uint8)
    return words, np.ascontiguousarray(byte.astype(np.uint8).reshape(k // 512, 16, n))


def unpack_weight(words, scales):
    g, p, n, _ = words.shape
    vals = np.ascontiguousarray(words).view(ml_dtypes.float8_e4m3fn).astype(np.float64) * np.repeat(np.exp2(scales.astype(np.float64) - 127.0), 8, axis=1)[..., None]
    return vals.transpose(0, 1, 3, 2).reshape(g * 512, n)


def relu(v):
    return np.maximum(v, 0.0)


def gelu(v):
    return 0.5 * v * (1.0 + np.tanh(np.sqrt(2.0 / np.pi) * (v + 0.044715 * v**3)))


K, T, S, D, V, H, N, U = 512, 2048, 1024, 3, 512, 512, 256, 256
P = 2 ** 7


def setup_inputs():
    n = np.random.standard_normal
    s = mx_kscale(K)[:, None]
    u = mx_kscale(H)
    packed_w2 = pack_weight(n((H, N)) / np.sqrt(H) / u[:, None])
    return {
        "xT": (n((K, T)) * s).astype(np.float32),
        "w1": (n((K, H)) / np.sqrt(K) / s * u).astype(np.float32),
        "w2_words": packed_w2[0],
        "w2_scales": packed_w2[1],
        "gate": (np.tile(np.random.uniform(0.2, 1.0, (D, 1, V)) / np.sqrt(D), (1, P, 1))).astype(np.float32),
        "gate2": (np.tile(np.random.uniform(0.2, 1.0, (D, 1, U)) / np.sqrt(D), (1, P, 1))).astype(np.float32),
        "offs": striped(np.random.permutation(T)[:S]),
        "pos1": striped(np.random.permutation(S)[:V]),
        "pos2": striped(np.random.permutation(S)[:V]),
        "pos3": striped(np.random.permutation(S)[:V]),
        "nxt1": striped(np.random.permutation(V)[:U]),
        "nxt2": striped(np.random.permutation(V)[:U]),
        "nxt3": striped(np.random.permutation(V)[:U]),
    }


def reference(xT, w1, w2_words, w2_scales, gate, gate2, offs, pos1, pos2, pos3, nxt1, nxt2, nxt3):
    xq = mxq(f64(xT)[:, unstriped(offs)], 0, "e4m3")
    h = gelu(mxq(f64(w1), 0, "e4m3").T @ xq)
    z = h[:, unstriped(pos1)] * f64(gate)[0, :1] + h[:, unstriped(pos2)] * f64(gate)[1, :1] + h[:, unstriped(pos3)] * f64(gate)[2, :1]
    g = relu(unpack_weight(w2_words, w2_scales).T @ mxq(z, 0, "e4m3"))
    return g[:, unstriped(nxt1)] * f64(gate2)[0, :1] + g[:, unstriped(nxt2)] * f64(gate2)[1, :1] + g[:, unstriped(nxt3)] * f64(gate2)[2, :1]

@@ -1,0 +1,272 @@
+from contextlib import ExitStack
+
+import concourse.mybir as mybir
+from concourse.masks import make_identity
+
+K, T, S, D, V, H, N, U = 512, 2048, 1024, 3, 512, 512, 256, 256
+FLOPS = 2 * K * H * S + 2 * H * N * V
+
+F32 = mybir.dt.float32
+BF16 = mybir.dt.bfloat16
+I32 = mybir.dt.int32
+U32 = mybir.dt.uint32
+U16 = mybir.dt.uint16
+U8 = mybir.dt.uint8
+FP8X4 = mybir.dt.float8_e4m3fn_x4
+MULT = mybir.AluOpType.mult
+ADD = mybir.AluOpType.add
+GELU = mybir.ActivationFunctionType.Gelu_apprx_tanh
+RELU = mybir.ActivationFunctionType.Relu
+
+P = 128
+PACK = 4
+LINE = 4
+PIECE = 256
+PIECES = S // PIECE
+H_TILES = H // P
+M_TILES = N // P
+CHUNKS = (
+    ((512, "v"), (512, "s"), (512, "v"), (512, "v")),
+    ((512, "s"), (512, "s"), (512, "v"), (256, "s"), (256, "v")),
+)
+BLOCKS = V // P
+WIDE_TILES = 2
+
+
+def tile_picked_hop2_gelu_e_kernel(
+    tc, xT, w1, w2_words, w2_scales, gate, gate2, offs, pos1, pos2, pos3, nxt1, nxt2, nxt3, out
+):
+    nc = tc.nc
+
+    def copy(engine, dst, src):
+        if engine == "v":
+            nc.vector.tensor_copy(out=dst, in_=src)
+        else:
+            nc.scalar.copy(out=dst, in_=src)
+
+    with ExitStack() as ctx:
+        keep = ctx.enter_context(tc.tile_pool(name="keep", bufs=1))
+        ring = ctx.enter_context(tc.tile_pool(name="ring", bufs=2))
+        picked = ctx.enter_context(tc.tile_pool(name="picked", bufs=4))
+        h_psum = ctx.enter_context(tc.psum_pool(name="h_psum", bufs=2))
+        zt_psum = ctx.enter_context(tc.psum_pool(name="zt_psum", bufs=1))
+        z_psum = ctx.enter_context(tc.psum_pool(name="z_psum", bufs=1))
+        g_psum = ctx.enter_context(tc.psum_pool(name="g_psum", bufs=1))
+
+        def load_list(name, src):
+            tile = keep.tile(list(src.shape), U16, name=name)
+            nc.sync.dma_start(tile[:], src)
+            return tile
+
+        ident = keep.tile([P, P], F32, name="ident")
+        make_identity(nc, ident[:])
+        warm = keep.tile([P, 1], F32, name="warm")
+        nc.scalar.activation(warm[:], ident[:, 0:1], GELU)
+        w2_bytes = keep.tile([P, N], U8, name="w2_bytes", align_bytes=64)
+        nc.gpsimd.memset(w2_bytes[:], 0)
+
+        x_rows = xT.rearrange("(p j) c -> p j c", j=PACK)
+        words = [keep.tile([P, 2, PIECE], U32, name="words%d" % q) for q in range(PIECES)]
+        offs_t = None
+        for u in range(2):
+            pairs = keep.tile([P, T], U32, name="pairs%d" % u)
+            pairs_bf = pairs[:].bitcast(BF16)
+            c0 = 0
+            for n, (width, engine) in enumerate(CHUNKS[u]):
+                raw = keep.tile([P, 2, width], F32, name="raw%d_%d" % (u, n))
+                nc.sync.dma_start(raw[:], x_rows[:, 2 * u : 2 * u + 2, c0 : c0 + width])
+                copy(
+                    engine,
+                    pairs_bf[:, 2 * c0 : 2 * (c0 + width)].rearrange("p (c i e) -> p c e i", i=LINE, e=2),
+                    raw[:].rearrange("p e (c i) -> p c e i", i=LINE),
+                )
+                c0 = c0 + width
+            if u == 0:
+                offs_t = load_list("offs_t", offs)
+            for q in range(PIECES):
+                cols = slice(q * PIECE // 16, (q + 1) * PIECE // 16)
+                nc.vector.tensor_copy(out=words[q][:, u, :], in_=pairs[:].indirect(offs_t[:, cols]))
+
+        w_rows = w1.rearrange("(p j) c -> p j c", j=PACK)
+        w1_codes = keep.tile([P, H], U32, name="w1_codes", align_bytes=64)
+        w1_bytes = keep.tile([P, H], U8, name="w1_bytes", align_bytes=64)
+
+        def load_w1(c0, width):
+            raw = keep.tile([P, PACK, width], F32, name="w_raw%d" % c0)
+            nc.sync.dma_start(raw[:], w_rows[:, :, c0 : c0 + width])
+            return raw
+
+        def quantize_w1(raw, c0, width, engine, tag):
+            grouped = keep.tile([P, width * PACK], BF16, name="w_grouped%d" % c0, tag=tag, align_bytes=64)
+            copy(
+                engine,
+                grouped[:].rearrange("p (c i j) -> p c j i", i=LINE, j=PACK),
+                raw[:].rearrange("p j (c i) -> p c j i", i=LINE),
+            )
+            nc.vector.quantize_mx(
+                out=w1_codes[:, c0 : c0 + width].bitcast(FP8X4), scales=w1_bytes[:, c0 : c0 + width], in_=grouped[:]
+            )
+
+        w_raw0 = load_w1(0, P)
+        pos = [load_list("pos%d" % d, src) for d, src in enumerate((pos1, pos2, pos3))]
+        w_raw1 = load_w1(P, P)
+        w_raw2 = load_w1(2 * P, 2 * P)
+        gates = keep.tile([P, D, V], F32, name="gates")
+        for d in range(D):
+            nc.sync.dma_start(gates[:, d, :], gate[d])
+        w2_codes = keep.tile([P, N], U32, name="w2_codes", align_bytes=64)
+        nc.sync.dma_start(w2_codes[:].bitcast(I32), w2_words[0].rearrange("p n t -> p (n t)").bitcast(I32))
+        for quad in range(4):
+            nc.sync.dma_start(
+                w2_bytes[32 * quad : 32 * quad + 4, :].bitcast(I32),
+                w2_scales[0, 4 * quad : 4 * quad + 4, :].bitcast(I32),
+            )
+        nxt = [load_list("nxt%d" % d, src) for d, src in enumerate((nxt1, nxt2, nxt3))]
+        gates2 = keep.tile([P, D, U], F32, name="gates2")
+        nc.sync.dma_start(gates2[:], gate2.rearrange("d p r -> p d r"))
+
+        quantize_w1(w_raw0, 0, P, "s", "w_first")
+
+        x_codes = keep.tile([P, S], U32, name="x_codes", tag="x_codes", align_bytes=64)
+        x_bytes = keep.tile([P, S], U8, name="x_bytes", align_bytes=64)
+        h = [keep.tile([P, S], F32, name="h%d" % t) for t in range(H_TILES)]
+
+        def first_layer(t, c0, width):
+            if t == 0:
+                acc = zt_psum.tile([P, width], F32, name="h_first", tag="zt_acc%d" % (c0 // width))
+            else:
+                acc = h_psum.tile([P, width], F32, name="h_acc")
+            nc.tensor.matmul_mx(
+                out=acc[:],
+                lhsT=w1_codes[:, t * P : (t + 1) * P].bitcast(FP8X4),
+                lhsT_scale=w1_bytes[:, t * P : (t + 1) * P],
+                rhs=x_codes[:, c0 : c0 + width].bitcast(FP8X4),
+                rhs_scale=x_bytes[:, c0 : c0 + width],
+                start=True,
+                stop=True,
+            )
+            nc.scalar.activation(h[t][:, c0 : c0 + width], acc[:], GELU)
+
+        woven = []
+        for q in range(PIECES):
+            tile = keep.tile([P, PIECE * PACK], BF16, name="woven%d" % q, tag="woven%d" % q, align_bytes=64)
+            nc.scalar.copy(
+                out=tile[:].bitcast(U32).rearrange("p (c u) -> p c u", u=2),
+                in_=words[q][:].rearrange("p u c -> p c u"),
+            )
+            woven.append(tile)
+        for q in range(PIECES):
+            cols = slice(q * PIECE, (q + 1) * PIECE)
+            nc.vector.quantize_mx(out=x_codes[:, cols].bitcast(FP8X4), scales=x_bytes[:, cols], in_=woven[q][:])
+            first_layer(0, q * PIECE, PIECE)
+
+        quantize_w1(w_raw1, P, P, "v", "woven3")
+        for c0 in range(0, S, 512):
+            first_layer(1, c0, 512)
+        quantize_w1(w_raw2, 2 * P, 2 * P, "s", "woven3")
+        for t in range(2, H_TILES):
+            for c0 in range(0, S, 512):
+                first_layer(t, c0, 512)
+
+        g = [keep.tile([P, V], F32, name="g%d" % m) for m in range(M_TILES)]
+
+        zt_accs = [zt_psum.tile([P, H], F32, name="zt_acc", tag="zt_acc%d" % b) for b in range(BLOCKS)]
+        zts = [keep.tile([P, H], BF16, name="zt", tag="zt%d" % b) for b in range(BLOCKS)]
+
+        def round_z(b, i0, width):
+            nc.scalar.copy(
+                out=zts[b][:].rearrange("v (u p e) -> v u p e", u=2, e=2)[:, :, i0 // PACK : (i0 + width) // PACK, :],
+                in_=zt_accs[b][:, i0 : i0 + width].rearrange("v (p u e) -> v u p e", u=2, e=2),
+            )
+
+        def second_layer(b):
+            zt, v0 = zts[b], b * P
+            z_acc = z_psum.tile([P, 2, P], F32, name="z_acc")
+            zt_words = zt[:].bitcast(F32)
+            for u in range(2):
+                nc.tensor.transpose(z_acc[:, u, :], zt_words[:, u * P : (u + 1) * P], ident[:])
+            z_in = ring.tile([P, P * PACK], BF16, name="z_in", align_bytes=64)
+            nc.scalar.copy(
+                out=z_in[:].bitcast(F32).rearrange("p (v u) -> p v u", u=2), in_=z_acc[:].rearrange("p u v -> p v u")
+            )
+            z_codes = ring.tile([P, P], U32, name="z_codes", align_bytes=64)
+            z_bytes = ring.tile([P, P], U8, name="z_bytes", align_bytes=64)
+            nc.vector.quantize_mx(out=z_codes[:].bitcast(FP8X4), scales=z_bytes[:], in_=z_in[:])
+            g_acc = g_psum.tile([P, M_TILES, P], F32, name="g_acc")
+            for m in range(M_TILES):
+                nc.tensor.matmul_mx(
+                    out=g_acc[:, m, :],
+                    lhsT=w2_codes[:, m * P : (m + 1) * P].bitcast(FP8X4),
+                    lhsT_scale=w2_bytes[:, m * P : (m + 1) * P],
+                    rhs=z_codes[:].bitcast(FP8X4),
+                    rhs_scale=z_bytes[:],
+                    start=True,
+                    stop=True,
+                )
+            for m in range(M_TILES):
+                nc.scalar.activation(g[m][:, v0 : v0 + P], g_acc[:, m, :], RELU)
+
+        def hop_term(term, t, d, b0, blocks):
+            v0, width = b0 * P, blocks * P
+            nc.vector.tensor_tensor(
+                term[:],
+                h[t][:].indirect(pos[d][:, v0 // 16 : (v0 + width) // 16]),
+                gates[:, d, v0 : v0 + width],
+                MULT,
+            )
+            for b in range(blocks):
+                nc.tensor.matmul(
+                    zt_accs[b0 + b][:, t * P : (t + 1) * P],
+                    term[:, b * P : (b + 1) * P],
+                    ident[:],
+                    start=(d == 0),
+                    stop=(d == D - 1),
+                    is_transpose=True,
+                )
+
+        for t in range(WIDE_TILES):
+            for d in range(D):
+                if d == D - 1:
+                    term = keep.tile([P, V], F32, name="held_wide", tag=("woven3", "x_codes")[t], align_bytes=64)
+                else:
+                    term = picked.tile([P, V], F32, name="term")
+                hop_term(term, t, d, 0, BLOCKS)
+        for b in range(BLOCKS):
+            round_z(b, 0, WIDE_TILES * P)
+        for b in range(BLOCKS):
+            for t in range(WIDE_TILES, H_TILES):
+                for d in range(D):
+                    hop_term(picked.tile([P, P], F32, name="term"), t, d, b, 1)
+                round_z(b, t * P, P)
+            second_layer(b)
+
+        for m in range(M_TILES):
+            terms = []
+            for d in range(D):
+                term = keep.tile([P, U], F32, name="root_term%d_%d" % (m, d))
+                nc.vector.tensor_tensor(term[:], g[m][:].indirect(nxt[d][:]), gates2[:, d, :], MULT)
+                terms.append(term)
+            total = keep.tile([P, U], F32, name="total%d" % m)
+            if m < M_TILES - 1:
+                turned = [h_psum.tile([P, P], F32, name="h_acc") for b in range(U // P)]
+                for d in range(D):
+                    for b in range(U // P):
+                        nc.tensor.matmul(
+                            turned[b][:],
+                            terms[d][:, b * P : (b + 1) * P],
+                            ident[:],
+                            start=(d == 0),
+                            stop=(d == D - 1),
+                            is_transpose=True,
+                        )
+                sums = keep.tile([P, U // P, P], F32, name="sums")
+                back = z_psum.tile([P, U // P, P], F32, name="z_acc")
+                for b in range(U // P):
+                    nc.scalar.copy(out=sums[:, b, :], in_=turned[b][:])
+                    nc.tensor.transpose(back[:, b, :], sums[:, b, :], ident[:])
+                nc.scalar.copy(out=total[:], in_=back[:].rearrange("p b r -> p (b r)"))
+            else:
+                part = keep.tile([P, U], F32, name="part%d" % m)
+                nc.vector.tensor_tensor(part[:], terms[0][:], terms[1][:], ADD)
+                nc.vector.tensor_tensor(total[:], part[:], terms[2][:], ADD)
+            nc.sync.dma_start(out[m * P : (m + 1) * P, :], total[:])

@@ -16,6 +16,7 @@ FP8X4 = mybir.dt.float8_e4m3fn_x4
 MULT = mybir.AluOpType.mult
 ADD = mybir.AluOpType.add
 GELU = mybir.ActivationFunctionType.Gelu_apprx_tanh
+COPY = mybir.ActivationFunctionType.Copy
 RELU = mybir.ActivationFunctionType.Relu
 
 P = 128
@@ -31,6 +32,8 @@ CHUNKS = (
 )
 BLOCKS = V // P
 WIDE_TILES = 2
+SCALED_BLOCKS = 3
+FUSED_V0 = SCALED_BLOCKS * P
 
 
 def tile_picked_hop2_gelu_e_kernel(
@@ -47,10 +50,10 @@ def tile_picked_hop2_gelu_e_kernel(
     with ExitStack() as ctx:
         keep = ctx.enter_context(tc.tile_pool(name="keep", bufs=1))
         ring = ctx.enter_context(tc.tile_pool(name="ring", bufs=2))
-        picked = ctx.enter_context(tc.tile_pool(name="picked", bufs=4))
+        picked = ctx.enter_context(tc.tile_pool(name="picked", bufs=5))
         h_psum = ctx.enter_context(tc.psum_pool(name="h_psum", bufs=2))
         zt_psum = ctx.enter_context(tc.psum_pool(name="zt_psum", bufs=1))
-        z_psum = ctx.enter_context(tc.psum_pool(name="z_psum", bufs=1))
+        turn_psum = ctx.enter_context(tc.psum_pool(name="turn_psum", bufs=4))
         g_psum = ctx.enter_context(tc.psum_pool(name="g_psum", bufs=1))
 
         def load_list(name, src):
@@ -64,6 +67,8 @@ def tile_picked_hop2_gelu_e_kernel(
         nc.scalar.activation(warm[:], ident[:, 0:1], GELU)
         w2_bytes = keep.tile([P, N], U8, name="w2_bytes", align_bytes=64)
         nc.gpsimd.memset(w2_bytes[:], 0)
+        gate_rows = keep.tile([P, FUSED_V0], F32, name="gate_rows")
+        nc.gpsimd.memset(gate_rows[:], 0.0)
 
         x_rows = xT.rearrange("(p j) c -> p j c", j=PACK)
         words = [keep.tile([P, 2, PIECE], U32, name="words%d" % q) for q in range(PIECES)]
@@ -110,10 +115,11 @@ def tile_picked_hop2_gelu_e_kernel(
         w_raw0 = load_w1(0, P)
         pos = [load_list("pos%d" % d, src) for d, src in enumerate((pos1, pos2, pos3))]
         w_raw1 = load_w1(P, P)
+        nc.sync.dma_start(gate_rows[0:D, :], gate[:, 0, 0:FUSED_V0])
+        nc.sync.dma_start(gate_rows[D : 2 * D, 0:U], gate2[:, 0, :])
         w_raw2 = load_w1(2 * P, 2 * P)
-        gates = keep.tile([P, D, V], F32, name="gates")
-        for d in range(D):
-            nc.sync.dma_start(gates[:, d, :], gate[d])
+        gates = keep.tile([P, D, V - FUSED_V0], F32, name="gates")
+        nc.sync.dma_start(gates[:], gate[:, :, FUSED_V0:V].rearrange("d p v -> p d v"))
         w2_codes = keep.tile([P, N], U32, name="w2_codes", align_bytes=64)
         nc.sync.dma_start(w2_codes[:].bitcast(I32), w2_words[0].rearrange("p n t -> p (n t)").bitcast(I32))
         for quad in range(4):
@@ -132,10 +138,10 @@ def tile_picked_hop2_gelu_e_kernel(
         h = [keep.tile([P, S], F32, name="h%d" % t) for t in range(H_TILES)]
 
         def first_layer(t, c0, width):
-            if t == 0:
-                acc = zt_psum.tile([P, width], F32, name="h_first", tag="zt_acc%d" % (c0 // width))
-            else:
+            if t == 1:
                 acc = h_psum.tile([P, width], F32, name="h_acc")
+            else:
+                acc = turn_psum.tile([P, width], F32, name="turned")
             nc.tensor.matmul_mx(
                 out=acc[:],
                 lhsT=w1_codes[:, t * P : (t + 1) * P].bitcast(FP8X4),
@@ -170,8 +176,21 @@ def tile_picked_hop2_gelu_e_kernel(
 
         g = [keep.tile([P, V], F32, name="g%d" % m) for m in range(M_TILES)]
 
-        zt_accs = [zt_psum.tile([P, H], F32, name="zt_acc", tag="zt_acc%d" % b) for b in range(BLOCKS)]
-        zts = [keep.tile([P, H], BF16, name="zt", tag="zt%d" % b) for b in range(BLOCKS)]
+        gate_acc = g_psum.tile([P, SCALED_BLOCKS, P], F32, name="g_acc")
+        for b in range(SCALED_BLOCKS):
+            nc.tensor.transpose(gate_acc[:, b, :], gate_rows[:, b * P : (b + 1) * P], ident[:])
+        gate_cols = keep.tile([P, SCALED_BLOCKS, 2 * D], F32, name="gate_cols")
+        nc.scalar.copy(out=gate_cols[:], in_=gate_acc[:, :, 0 : 2 * D])
+
+        zt_accs = {
+            b: zt_psum.tile([P, H], F32, name="zt_acc", tag="zt_acc%d" % (b - SCALED_BLOCKS))
+            for b in range(SCALED_BLOCKS, BLOCKS)
+        }
+        zts = {b: keep.tile([P, H], BF16, name="zt%d" % b) for b in range(SCALED_BLOCKS, BLOCKS)}
+        scaled = [[keep.tile([P, H], F32, name="scaled%d_%d" % (b, d)) for d in range(D)] for b in range(SCALED_BLOCKS)]
+
+        def add_turned(acc, src, d):
+            nc.tensor.matmul(acc, src, ident[:], start=(d == 0), stop=(d == D - 1), is_transpose=True)
 
         def round_z(b, i0, width):
             nc.scalar.copy(
@@ -179,16 +198,35 @@ def tile_picked_hop2_gelu_e_kernel(
                 in_=zt_accs[b][:, i0 : i0 + width].rearrange("v (p u e) -> v u p e", u=2, e=2),
             )
 
-        def second_layer(b):
-            zt, v0 = zts[b], b * P
-            z_acc = z_psum.tile([P, 2, P], F32, name="z_acc")
-            zt_words = zt[:].bitcast(F32)
-            for u in range(2):
-                nc.tensor.transpose(z_acc[:, u, :], zt_words[:, u * P : (u + 1) * P], ident[:])
-            z_in = ring.tile([P, P * PACK], BF16, name="z_in", align_bytes=64)
-            nc.scalar.copy(
-                out=z_in[:].bitcast(F32).rearrange("p (v u) -> p v u", u=2), in_=z_acc[:].rearrange("p u v -> p v u")
+        def scale_turned(turned, b, d, i0):
+            width = turned.shape[1]
+            nc.scalar.activation(
+                scaled[b][d][:].rearrange("v (j p) -> v j p", j=PACK)[:, :, i0 // PACK : (i0 + width) // PACK],
+                turned.rearrange("v (p j) -> v j p", j=PACK),
+                COPY,
+                scale=gate_cols[:, b, d : d + 1],
             )
+
+        def second_layer(b):
+            v0 = b * P
+            z_in = ring.tile([P, P * PACK], BF16, name="z_in", align_bytes=64)
+            if b < SCALED_BLOCKS:
+                z_acc = h_psum.tile([P, PACK, P], F32, name="h_acc")
+                for j in range(PACK):
+                    for d in range(D):
+                        add_turned(z_acc[:, j, :], scaled[b][d][:, j * P : (j + 1) * P], d)
+                nc.scalar.copy(
+                    out=z_in[:].rearrange("p (v j) -> p v j", j=PACK), in_=z_acc[:].rearrange("p j v -> p v j")
+                )
+            else:
+                z_acc = h_psum.tile([P, 2, P], F32, name="h_acc")
+                zt_words = zts[b][:].bitcast(F32)
+                for u in range(2):
+                    nc.tensor.transpose(z_acc[:, u, :], zt_words[:, u * P : (u + 1) * P], ident[:])
+                nc.scalar.copy(
+                    out=z_in[:].bitcast(F32).rearrange("p (v u) -> p v u", u=2),
+                    in_=z_acc[:].rearrange("p u v -> p v u"),
+                )
             z_codes = ring.tile([P, P], U32, name="z_codes", align_bytes=64)
             z_bytes = ring.tile([P, P], U8, name="z_bytes", align_bytes=64)
             nc.vector.quantize_mx(out=z_codes[:].bitcast(FP8X4), scales=z_bytes[:], in_=z_in[:])
@@ -206,67 +244,73 @@ def tile_picked_hop2_gelu_e_kernel(
             for m in range(M_TILES):
                 nc.scalar.activation(g[m][:, v0 : v0 + P], g_acc[:, m, :], RELU)
 
-        def hop_term(term, t, d, b0, blocks):
+        def picked_h(t, d, v0, width):
+            return h[t][:].indirect(pos[d][:, v0 // 16 : (v0 + width) // 16])
+
+        def fused_term(t, d, b0, blocks):
             v0, width = b0 * P, blocks * P
+            term = picked.tile([P, width], F32, name="term")
             nc.vector.tensor_tensor(
-                term[:],
-                h[t][:].indirect(pos[d][:, v0 // 16 : (v0 + width) // 16]),
-                gates[:, d, v0 : v0 + width],
-                MULT,
+                term[:], picked_h(t, d, v0, width), gates[:, d, v0 - FUSED_V0 : v0 - FUSED_V0 + width], MULT
             )
             for b in range(blocks):
-                nc.tensor.matmul(
-                    zt_accs[b0 + b][:, t * P : (t + 1) * P],
-                    term[:, b * P : (b + 1) * P],
-                    ident[:],
-                    start=(d == 0),
-                    stop=(d == D - 1),
-                    is_transpose=True,
-                )
+                add_turned(zt_accs[b0 + b][:, t * P : (t + 1) * P], term[:, b * P : (b + 1) * P], d)
 
+        plain = {}
         for t in range(WIDE_TILES):
             for d in range(D):
-                if d == D - 1:
-                    term = keep.tile([P, V], F32, name="held_wide", tag=("woven3", "x_codes")[t], align_bytes=64)
-                else:
-                    term = picked.tile([P, V], F32, name="term")
-                hop_term(term, t, d, 0, BLOCKS)
-        for b in range(BLOCKS):
-            round_z(b, 0, WIDE_TILES * P)
-        for b in range(BLOCKS):
-            for t in range(WIDE_TILES, H_TILES):
+                tag = "woven3" if (t, d) == (0, D - 1) else "plain%d_%d" % (t, d)
+                plain[t, d] = keep.tile([P, FUSED_V0], F32, name="plain", tag=tag, align_bytes=64)
+                nc.vector.tensor_copy(out=plain[t, d][:], in_=picked_h(t, d, 0, FUSED_V0))
+                if t == WIDE_TILES - 1:
+                    for b in range(SCALED_BLOCKS):
+                        turned = turn_psum.tile([P, WIDE_TILES * P], F32, name="turned")
+                        for s in range(WIDE_TILES):
+                            nc.tensor.transpose(
+                                turned[:, s * P : (s + 1) * P], plain[s, d][:, b * P : (b + 1) * P], ident[:]
+                            )
+                        scale_turned(turned[:], b, d, 0)
+        for b in range(SCALED_BLOCKS):
+            for d in range(D):
+                turned = turn_psum.tile([P, (H_TILES - WIDE_TILES) * P], F32, name="turned")
+                for t in range(WIDE_TILES, H_TILES):
+                    term = picked.tile([P, P], F32, name="term")
+                    nc.vector.tensor_copy(out=term[:], in_=picked_h(t, d, b * P, P))
+                    s = t - WIDE_TILES
+                    nc.tensor.transpose(turned[:, s * P : (s + 1) * P], term[:], ident[:])
+                scale_turned(turned[:], b, d, WIDE_TILES * P)
+            second_layer(b)
+        for b in range(SCALED_BLOCKS, BLOCKS):
+            for t in range(H_TILES):
                 for d in range(D):
-                    hop_term(picked.tile([P, P], F32, name="term"), t, d, b, 1)
+                    fused_term(t, d, b, 1)
                 round_z(b, t * P, P)
             second_layer(b)
 
-        for m in range(M_TILES):
-            terms = []
-            for d in range(D):
-                term = keep.tile([P, U], F32, name="root_term%d_%d" % (m, d))
-                nc.vector.tensor_tensor(term[:], g[m][:].indirect(nxt[d][:]), gates2[:, d, :], MULT)
-                terms.append(term)
-            total = keep.tile([P, U], F32, name="total%d" % m)
-            if m < M_TILES - 1:
-                turned = [h_psum.tile([P, P], F32, name="h_acc") for b in range(U // P)]
-                for d in range(D):
-                    for b in range(U // P):
-                        nc.tensor.matmul(
-                            turned[b][:],
-                            terms[d][:, b * P : (b + 1) * P],
-                            ident[:],
-                            start=(d == 0),
-                            stop=(d == D - 1),
-                            is_transpose=True,
-                        )
-                sums = keep.tile([P, U // P, P], F32, name="sums")
-                back = z_psum.tile([P, U // P, P], F32, name="z_acc")
-                for b in range(U // P):
-                    nc.scalar.copy(out=sums[:, b, :], in_=turned[b][:])
-                    nc.tensor.transpose(back[:, b, :], sums[:, b, :], ident[:])
-                nc.scalar.copy(out=total[:], in_=back[:].rearrange("p b r -> p (b r)"))
-            else:
-                part = keep.tile([P, U], F32, name="part%d" % m)
-                nc.vector.tensor_tensor(part[:], terms[0][:], terms[1][:], ADD)
-                nc.vector.tensor_tensor(total[:], part[:], terms[2][:], ADD)
-            nc.sync.dma_start(out[m * P : (m + 1) * P, :], total[:])
+        R_BLOCKS = U // P
+        total = keep.tile([P, U], F32, name="total0")
+        backs = [h_psum.tile([P, P], F32, name="h_acc") for b in range(R_BLOCKS)]
+        for d in range(D):
+            term = keep.tile([P, U], F32, name="root_term0_%d" % d)
+            nc.vector.tensor_copy(out=term[:], in_=g[0][:].indirect(nxt[d][:]))
+            turned = turn_psum.tile([P, R_BLOCKS, P], F32, name="turned")
+            for b in range(R_BLOCKS):
+                nc.tensor.transpose(turned[:, b, :], term[:, b * P : (b + 1) * P], ident[:])
+            root_scaled = keep.tile([P, R_BLOCKS, P], F32, name="root_scaled%d" % d)
+            for b in range(R_BLOCKS):
+                nc.scalar.activation(root_scaled[:, b, :], turned[:, b, :], COPY, scale=gate_cols[:, b, D + d : D + d + 1])
+                add_turned(backs[b][:], root_scaled[:, b, :], d)
+        for b in range(R_BLOCKS):
+            nc.scalar.copy(out=total[:, b * P : (b + 1) * P], in_=backs[b][:])
+        nc.sync.dma_start(out[0:P, :], total[:])
+
+        terms = []
+        for d in range(D):
+            term = keep.tile([P, U], F32, name="root_term1_%d" % d)
+            nc.vector.tensor_tensor(term[:], g[1][:].indirect(nxt[d][:]), gates2[:, d, :], MULT)
+            terms.append(term)
+        part = keep.tile([P, U], F32, name="part")
+        nc.vector.tensor_tensor(part[:], terms[0][:], terms[1][:], ADD)
+        total = keep.tile([P, U], F32, name="total1")
+        nc.vector.tensor_tensor(total[:], part[:], terms[2][:], ADD)
+        nc.sync.dma_start(out[P : 2 * P, :], total[:])

@@ -23,17 +23,17 @@ P = 128
 PACK = 4
 LINE = 4
 PIECE = 256
-PIECES = S // PIECE
+X_RUNS = (256, 256, 256, 128, 128)
 H_TILES = H // P
 M_TILES = N // P
 CHUNKS = (
-    ((512, "v"), (512, "s"), (512, "v"), (512, "v")),
-    ((512, "s"), (512, "s"), (512, "v"), (256, "s"), (256, "v")),
+    (((1024, "v"),), ((640, "v"), (384, "s"))),
+    (((1024, "s"),), ((512, "v"),), ((256, "v"),), ((160, "v"), (96, "s"))),
 )
+V_RUNS = (2, 1, 1)
 BLOCKS = V // P
 WIDE_TILES = 2
-SCALED_BLOCKS = 3
-FUSED_V0 = SCALED_BLOCKS * P
+R_BLOCKS = U // P
 
 
 def tile_picked_hop2_gelu_e_kernel(
@@ -50,10 +50,10 @@ def tile_picked_hop2_gelu_e_kernel(
     with ExitStack() as ctx:
         keep = ctx.enter_context(tc.tile_pool(name="keep", bufs=1))
         ring = ctx.enter_context(tc.tile_pool(name="ring", bufs=2))
-        picked = ctx.enter_context(tc.tile_pool(name="picked", bufs=5))
+        picked = ctx.enter_context(tc.tile_pool(name="picked", bufs=4))
         h_psum = ctx.enter_context(tc.psum_pool(name="h_psum", bufs=2))
         zt_psum = ctx.enter_context(tc.psum_pool(name="zt_psum", bufs=1))
-        turn_psum = ctx.enter_context(tc.psum_pool(name="turn_psum", bufs=4))
+        z_psum = ctx.enter_context(tc.psum_pool(name="z_psum", bufs=1))
         g_psum = ctx.enter_context(tc.psum_pool(name="g_psum", bufs=1))
 
         def load_list(name, src):
@@ -63,34 +63,43 @@ def tile_picked_hop2_gelu_e_kernel(
 
         ident = keep.tile([P, P], F32, name="ident")
         make_identity(nc, ident[:])
-        warm = keep.tile([P, 1], F32, name="warm")
-        nc.scalar.activation(warm[:], ident[:, 0:1], GELU)
+        warm = keep.tile([P, 2], F32, name="warm")
+        nc.vector.memset(warm[:, 0:1], 0.0)
+        nc.scalar.activation(warm[:, 1:2], warm[:, 0:1], GELU)
         w2_bytes = keep.tile([P, N], U8, name="w2_bytes", align_bytes=64)
         nc.gpsimd.memset(w2_bytes[:], 0)
-        gate_rows = keep.tile([P, FUSED_V0], F32, name="gate_rows")
-        nc.gpsimd.memset(gate_rows[:], 0.0)
+        gate2_rows = keep.tile([P, U], F32, name="gate2_rows")
+        nc.gpsimd.memset(gate2_rows[:], 0.0)
 
         x_rows = xT.rearrange("(p j) c -> p j c", j=PACK)
-        words = [keep.tile([P, 2, PIECE], U32, name="words%d" % q) for q in range(PIECES)]
+        words = keep.tile([P, 2, S], U32, name="words")
         offs_t = None
         for u in range(2):
             pairs = keep.tile([P, T], U32, name="pairs%d" % u)
             pairs_bf = pairs[:].bitcast(BF16)
             c0 = 0
-            for n, (width, engine) in enumerate(CHUNKS[u]):
+            for n, shares in enumerate(CHUNKS[u]):
+                width = sum(share for share, engine in shares)
                 raw = keep.tile([P, 2, width], F32, name="raw%d_%d" % (u, n))
                 nc.sync.dma_start(raw[:], x_rows[:, 2 * u : 2 * u + 2, c0 : c0 + width])
-                copy(
-                    engine,
-                    pairs_bf[:, 2 * c0 : 2 * (c0 + width)].rearrange("p (c i e) -> p c e i", i=LINE, e=2),
-                    raw[:].rearrange("p e (c i) -> p c e i", i=LINE),
-                )
+                s0 = 0
+                for share, engine in shares:
+                    copy(
+                        engine,
+                        pairs_bf[:, 2 * (c0 + s0) : 2 * (c0 + s0 + share)].rearrange(
+                            "p (c i e) -> p c e i", i=LINE, e=2
+                        ),
+                        raw[:, :, s0 : s0 + share].rearrange("p e (c i) -> p c e i", i=LINE),
+                    )
+                    s0 = s0 + share
                 c0 = c0 + width
             if u == 0:
                 offs_t = load_list("offs_t", offs)
-            for q in range(PIECES):
-                cols = slice(q * PIECE // 16, (q + 1) * PIECE // 16)
-                nc.vector.tensor_copy(out=words[q][:, u, :], in_=pairs[:].indirect(offs_t[:, cols]))
+            run = S if u == 0 else PIECE
+            for e0 in range(0, S, run):
+                nc.vector.tensor_copy(
+                    out=words[:, u, e0 : e0 + run], in_=pairs[:].indirect(offs_t[:, e0 // 16 : (e0 + run) // 16])
+                )
 
         w_rows = w1.rearrange("(p j) c -> p j c", j=PACK)
         w1_codes = keep.tile([P, H], U32, name="w1_codes", align_bytes=64)
@@ -115,11 +124,10 @@ def tile_picked_hop2_gelu_e_kernel(
         w_raw0 = load_w1(0, P)
         pos = [load_list("pos%d" % d, src) for d, src in enumerate((pos1, pos2, pos3))]
         w_raw1 = load_w1(P, P)
-        nc.sync.dma_start(gate_rows[0:D, :], gate[:, 0, 0:FUSED_V0])
-        nc.sync.dma_start(gate_rows[D : 2 * D, 0:U], gate2[:, 0, :])
         w_raw2 = load_w1(2 * P, 2 * P)
-        gates = keep.tile([P, D, V - FUSED_V0], F32, name="gates")
-        nc.sync.dma_start(gates[:], gate[:, :, FUSED_V0:V].rearrange("d p v -> p d v"))
+        gates = keep.tile([P, D, V], F32, name="gates")
+        for d in range(D):
+            nc.sync.dma_start(gates[:, d, :], gate[d])
         w2_codes = keep.tile([P, N], U32, name="w2_codes", align_bytes=64)
         nc.sync.dma_start(w2_codes[:].bitcast(I32), w2_words[0].rearrange("p n t -> p (n t)").bitcast(I32))
         for quad in range(4):
@@ -128,6 +136,7 @@ def tile_picked_hop2_gelu_e_kernel(
                 w2_scales[0, 4 * quad : 4 * quad + 4, :].bitcast(I32),
             )
         nxt = [load_list("nxt%d" % d, src) for d, src in enumerate((nxt1, nxt2, nxt3))]
+        nc.sync.dma_start(gate2_rows[0:D, :], gate2[:, 0, :])
         gates2 = keep.tile([P, D, U], F32, name="gates2")
         nc.sync.dma_start(gates2[:], gate2.rearrange("d p r -> p d r"))
 
@@ -138,10 +147,12 @@ def tile_picked_hop2_gelu_e_kernel(
         h = [keep.tile([P, S], F32, name="h%d" % t) for t in range(H_TILES)]
 
         def first_layer(t, c0, width):
-            if t == 1:
-                acc = h_psum.tile([P, width], F32, name="h_acc")
+            if t == 0 and c0 + width == S:
+                acc = g_psum.tile([P, width], F32, name="g_acc")
+            elif t == 0:
+                acc = zt_psum.tile([P, width], F32, name="h_first", tag="zt_acc%d" % (c0 // PIECE))
             else:
-                acc = turn_psum.tile([P, width], F32, name="turned")
+                acc = h_psum.tile([P, width], F32, name="h_acc")
             nc.tensor.matmul_mx(
                 out=acc[:],
                 lhsT=w1_codes[:, t * P : (t + 1) * P].bitcast(FP8X4),
@@ -153,44 +164,33 @@ def tile_picked_hop2_gelu_e_kernel(
             )
             nc.scalar.activation(h[t][:, c0 : c0 + width], acc[:], GELU)
 
+        starts = [sum(X_RUNS[:q]) for q in range(len(X_RUNS))]
         woven = []
-        for q in range(PIECES):
-            tile = keep.tile([P, PIECE * PACK], BF16, name="woven%d" % q, tag="woven%d" % q, align_bytes=64)
+        for e0, run in zip(starts, X_RUNS):
+            tag = "woven_last" if e0 + run == S else "woven%d" % e0
+            tile = keep.tile([P, run * PACK], BF16, name="woven", tag=tag, align_bytes=64)
             nc.scalar.copy(
                 out=tile[:].bitcast(U32).rearrange("p (c u) -> p c u", u=2),
-                in_=words[q][:].rearrange("p u c -> p c u"),
+                in_=words[:, :, e0 : e0 + run].rearrange("p u c -> p c u"),
             )
             woven.append(tile)
-        for q in range(PIECES):
-            cols = slice(q * PIECE, (q + 1) * PIECE)
-            nc.vector.quantize_mx(out=x_codes[:, cols].bitcast(FP8X4), scales=x_bytes[:, cols], in_=woven[q][:])
-            first_layer(0, q * PIECE, PIECE)
+        for e0, run, tile in zip(starts, X_RUNS, woven):
+            cols = slice(e0, e0 + run)
+            nc.vector.quantize_mx(out=x_codes[:, cols].bitcast(FP8X4), scales=x_bytes[:, cols], in_=tile[:])
+            first_layer(0, e0, run)
 
-        quantize_w1(w_raw1, P, P, "v", "woven3")
+        quantize_w1(w_raw1, P, P, "v", "woven_last")
         for c0 in range(0, S, 512):
             first_layer(1, c0, 512)
-        quantize_w1(w_raw2, 2 * P, 2 * P, "s", "woven3")
+        quantize_w1(w_raw2, 2 * P, 2 * P, "s", "woven_last")
         for t in range(2, H_TILES):
             for c0 in range(0, S, 512):
                 first_layer(t, c0, 512)
 
         g = [keep.tile([P, V], F32, name="g%d" % m) for m in range(M_TILES)]
 
-        gate_acc = g_psum.tile([P, SCALED_BLOCKS, P], F32, name="g_acc")
-        for b in range(SCALED_BLOCKS):
-            nc.tensor.transpose(gate_acc[:, b, :], gate_rows[:, b * P : (b + 1) * P], ident[:])
-        gate_cols = keep.tile([P, SCALED_BLOCKS, 2 * D], F32, name="gate_cols")
-        nc.scalar.copy(out=gate_cols[:], in_=gate_acc[:, :, 0 : 2 * D])
-
-        zt_accs = {
-            b: zt_psum.tile([P, H], F32, name="zt_acc", tag="zt_acc%d" % (b - SCALED_BLOCKS))
-            for b in range(SCALED_BLOCKS, BLOCKS)
-        }
-        zts = {b: keep.tile([P, H], BF16, name="zt%d" % b) for b in range(SCALED_BLOCKS, BLOCKS)}
-        scaled = [[keep.tile([P, H], F32, name="scaled%d_%d" % (b, d)) for d in range(D)] for b in range(SCALED_BLOCKS)]
-
-        def add_turned(acc, src, d):
-            nc.tensor.matmul(acc, src, ident[:], start=(d == 0), stop=(d == D - 1), is_transpose=True)
+        zt_accs = [zt_psum.tile([P, H], F32, name="zt_acc", tag="zt_acc%d" % b) for b in range(BLOCKS)]
+        zts = [keep.tile([P, H], BF16, name="zt", tag="zt%d" % b) for b in range(BLOCKS)]
 
         def round_z(b, i0, width):
             nc.scalar.copy(
@@ -198,42 +198,24 @@ def tile_picked_hop2_gelu_e_kernel(
                 in_=zt_accs[b][:, i0 : i0 + width].rearrange("v (p u e) -> v u p e", u=2, e=2),
             )
 
-        def scale_turned(turned, b, d, i0):
-            width = turned.shape[1]
-            nc.scalar.activation(
-                scaled[b][d][:].rearrange("v (j p) -> v j p", j=PACK)[:, :, i0 // PACK : (i0 + width) // PACK],
-                turned.rearrange("v (p j) -> v j p", j=PACK),
-                COPY,
-                scale=gate_cols[:, b, d : d + 1],
-            )
-
-        def second_layer(b):
-            v0 = b * P
-            z_in = ring.tile([P, P * PACK], BF16, name="z_in", align_bytes=64)
-            if b < SCALED_BLOCKS:
-                z_acc = h_psum.tile([P, PACK, P], F32, name="h_acc")
-                for j in range(PACK):
-                    for d in range(D):
-                        add_turned(z_acc[:, j, :], scaled[b][d][:, j * P : (j + 1) * P], d)
-                nc.scalar.copy(
-                    out=z_in[:].rearrange("p (v j) -> p v j", j=PACK), in_=z_acc[:].rearrange("p j v -> p v j")
-                )
-            else:
-                z_acc = h_psum.tile([P, 2, P], F32, name="h_acc")
-                zt_words = zts[b][:].bitcast(F32)
+        def second_layer(b0, blocks):
+            v0, width = b0 * P, blocks * P
+            z_acc = z_psum.tile([P, 2, width], F32, name="z_acc")
+            for b in range(blocks):
+                zt_words = zts[b0 + b][:].bitcast(F32)
                 for u in range(2):
-                    nc.tensor.transpose(z_acc[:, u, :], zt_words[:, u * P : (u + 1) * P], ident[:])
-                nc.scalar.copy(
-                    out=z_in[:].bitcast(F32).rearrange("p (v u) -> p v u", u=2),
-                    in_=z_acc[:].rearrange("p u v -> p v u"),
-                )
-            z_codes = ring.tile([P, P], U32, name="z_codes", align_bytes=64)
-            z_bytes = ring.tile([P, P], U8, name="z_bytes", align_bytes=64)
+                    nc.tensor.transpose(z_acc[:, u, b * P : (b + 1) * P], zt_words[:, u * P : (u + 1) * P], ident[:])
+            z_in = ring.tile([P, width * PACK], BF16, name="z_in", align_bytes=64)
+            nc.scalar.copy(
+                out=z_in[:].bitcast(F32).rearrange("p (v u) -> p v u", u=2), in_=z_acc[:].rearrange("p u v -> p v u")
+            )
+            z_codes = ring.tile([P, width], U32, name="z_codes", align_bytes=64)
+            z_bytes = ring.tile([P, width], U8, name="z_bytes", align_bytes=64)
             nc.vector.quantize_mx(out=z_codes[:].bitcast(FP8X4), scales=z_bytes[:], in_=z_in[:])
-            g_acc = g_psum.tile([P, M_TILES, P], F32, name="g_acc")
+            g_accs = [g_psum.tile([P, width], F32, name="g_acc"), h_psum.tile([P, width], F32, name="h_acc")]
             for m in range(M_TILES):
                 nc.tensor.matmul_mx(
-                    out=g_acc[:, m, :],
+                    out=g_accs[m][:],
                     lhsT=w2_codes[:, m * P : (m + 1) * P].bitcast(FP8X4),
                     lhsT_scale=w2_bytes[:, m * P : (m + 1) * P],
                     rhs=z_codes[:].bitcast(FP8X4),
@@ -242,64 +224,65 @@ def tile_picked_hop2_gelu_e_kernel(
                     stop=True,
                 )
             for m in range(M_TILES):
-                nc.scalar.activation(g[m][:, v0 : v0 + P], g_acc[:, m, :], RELU)
+                nc.scalar.activation(g[m][:, v0 : v0 + width], g_accs[m][:], RELU)
 
-        def picked_h(t, d, v0, width):
-            return h[t][:].indirect(pos[d][:, v0 // 16 : (v0 + width) // 16])
-
-        def fused_term(t, d, b0, blocks):
+        def hop_term(term, t, d, b0, blocks):
             v0, width = b0 * P, blocks * P
-            term = picked.tile([P, width], F32, name="term")
             nc.vector.tensor_tensor(
-                term[:], picked_h(t, d, v0, width), gates[:, d, v0 - FUSED_V0 : v0 - FUSED_V0 + width], MULT
+                term[:],
+                h[t][:].indirect(pos[d][:, v0 // 16 : (v0 + width) // 16]),
+                gates[:, d, v0 : v0 + width],
+                MULT,
             )
             for b in range(blocks):
-                add_turned(zt_accs[b0 + b][:, t * P : (t + 1) * P], term[:, b * P : (b + 1) * P], d)
+                nc.tensor.matmul(
+                    zt_accs[b0 + b][:, t * P : (t + 1) * P],
+                    term[:, b * P : (b + 1) * P],
+                    ident[:],
+                    start=(d == 0),
+                    stop=(d == D - 1),
+                    is_transpose=True,
+                )
 
-        plain = {}
         for t in range(WIDE_TILES):
             for d in range(D):
-                tag = "woven3" if (t, d) == (0, D - 1) else "plain%d_%d" % (t, d)
-                plain[t, d] = keep.tile([P, FUSED_V0], F32, name="plain", tag=tag, align_bytes=64)
-                nc.vector.tensor_copy(out=plain[t, d][:], in_=picked_h(t, d, 0, FUSED_V0))
-                if t == WIDE_TILES - 1:
-                    for b in range(SCALED_BLOCKS):
-                        turned = turn_psum.tile([P, WIDE_TILES * P], F32, name="turned")
-                        for s in range(WIDE_TILES):
-                            nc.tensor.transpose(
-                                turned[:, s * P : (s + 1) * P], plain[s, d][:, b * P : (b + 1) * P], ident[:]
-                            )
-                        scale_turned(turned[:], b, d, 0)
-        for b in range(SCALED_BLOCKS):
-            for d in range(D):
-                turned = turn_psum.tile([P, (H_TILES - WIDE_TILES) * P], F32, name="turned")
-                for t in range(WIDE_TILES, H_TILES):
-                    term = picked.tile([P, P], F32, name="term")
-                    nc.vector.tensor_copy(out=term[:], in_=picked_h(t, d, b * P, P))
-                    s = t - WIDE_TILES
-                    nc.tensor.transpose(turned[:, s * P : (s + 1) * P], term[:], ident[:])
-                scale_turned(turned[:], b, d, WIDE_TILES * P)
-            second_layer(b)
-        for b in range(SCALED_BLOCKS, BLOCKS):
-            for t in range(H_TILES):
-                for d in range(D):
-                    fused_term(t, d, b, 1)
-                round_z(b, t * P, P)
-            second_layer(b)
+                if d == D - 1:
+                    term = keep.tile([P, V], F32, name="held_wide", tag=("woven_last", "x_codes")[t], align_bytes=64)
+                else:
+                    term = picked.tile([P, V], F32, name="term")
+                hop_term(term, t, d, 0, BLOCKS)
+        for b in range(BLOCKS):
+            round_z(b, 0, WIDE_TILES * P)
+        gate2_acc = g_psum.tile([P, R_BLOCKS, P], F32, name="g_acc")
+        for b in range(R_BLOCKS):
+            nc.tensor.transpose(gate2_acc[:, b, :], gate2_rows[:, b * P : (b + 1) * P], ident[:])
+        gate2_cols = keep.tile([P, R_BLOCKS, D], F32, name="gate2_cols")
+        nc.scalar.copy(out=gate2_cols[:], in_=gate2_acc[:, :, 0:D])
 
-        R_BLOCKS = U // P
+        b0 = 0
+        for blocks in V_RUNS:
+            for t in range(WIDE_TILES, H_TILES):
+                for d in range(D):
+                    hop_term(picked.tile([P, blocks * P], F32, name="term"), t, d, b0, blocks)
+                for b in range(b0, b0 + blocks):
+                    round_z(b, t * P, P)
+            second_layer(b0, blocks)
+            b0 = b0 + blocks
+
         total = keep.tile([P, U], F32, name="total0")
         backs = [h_psum.tile([P, P], F32, name="h_acc") for b in range(R_BLOCKS)]
         for d in range(D):
             term = keep.tile([P, U], F32, name="root_term0_%d" % d)
             nc.vector.tensor_copy(out=term[:], in_=g[0][:].indirect(nxt[d][:]))
-            turned = turn_psum.tile([P, R_BLOCKS, P], F32, name="turned")
+            turned = zt_psum.tile([P, R_BLOCKS, P], F32, name="turned", tag="zt_acc%d" % d)
             for b in range(R_BLOCKS):
                 nc.tensor.transpose(turned[:, b, :], term[:, b * P : (b + 1) * P], ident[:])
             root_scaled = keep.tile([P, R_BLOCKS, P], F32, name="root_scaled%d" % d)
             for b in range(R_BLOCKS):
-                nc.scalar.activation(root_scaled[:, b, :], turned[:, b, :], COPY, scale=gate_cols[:, b, D + d : D + d + 1])
-                add_turned(backs[b][:], root_scaled[:, b, :], d)
+                nc.scalar.activation(root_scaled[:, b, :], turned[:, b, :], COPY, scale=gate2_cols[:, b, d : d + 1])
+                nc.tensor.matmul(
+                    backs[b][:], root_scaled[:, b, :], ident[:], start=(d == 0), stop=(d == D - 1), is_transpose=True
+                )
         for b in range(R_BLOCKS):
             nc.scalar.copy(out=total[:, b * P : (b + 1) * P], in_=backs[b][:])
         nc.sync.dma_start(out[0:P, :], total[:])

@@ -16,7 +16,6 @@ FP8X4 = mybir.dt.float8_e4m3fn_x4
 MULT = mybir.AluOpType.mult
 ADD = mybir.AluOpType.add
 GELU = mybir.ActivationFunctionType.Gelu_apprx_tanh
-COPY = mybir.ActivationFunctionType.Copy
 RELU = mybir.ActivationFunctionType.Relu
 
 P = 128
@@ -27,13 +26,13 @@ X_RUNS = (256, 256, 256, 128, 128)
 H_TILES = H // P
 M_TILES = N // P
 CHUNKS = (
-    (((1024, "v"),), ((640, "v"), (384, "s"))),
-    (((1024, "s"),), ((512, "v"),), ((256, "v"),), ((160, "v"), (96, "s"))),
+    (((640, "v"), (384, "s")), ((640, "v"), (384, "s"))),
+    (((768, "s"), (256, "v")), ((512, "v"),), ((256, "v"),), ((160, "v"), (96, "s"))),
 )
-V_RUNS = (2, 1, 1)
 BLOCKS = V // P
-WIDE_TILES = 2
+TURNED = 2
 R_BLOCKS = U // P
+HALF = H // 2
 
 
 def tile_picked_hop2_gelu_e_kernel(
@@ -49,12 +48,10 @@ def tile_picked_hop2_gelu_e_kernel(
 
     with ExitStack() as ctx:
         keep = ctx.enter_context(tc.tile_pool(name="keep", bufs=1))
-        ring = ctx.enter_context(tc.tile_pool(name="ring", bufs=2))
         picked = ctx.enter_context(tc.tile_pool(name="picked", bufs=4))
         h_psum = ctx.enter_context(tc.psum_pool(name="h_psum", bufs=2))
         zt_psum = ctx.enter_context(tc.psum_pool(name="zt_psum", bufs=1))
         z_psum = ctx.enter_context(tc.psum_pool(name="z_psum", bufs=1))
-        g_psum = ctx.enter_context(tc.psum_pool(name="g_psum", bufs=1))
 
         def load_list(name, src):
             tile = keep.tile(list(src.shape), U16, name=name)
@@ -68,8 +65,6 @@ def tile_picked_hop2_gelu_e_kernel(
         nc.scalar.activation(warm[:, 1:2], warm[:, 0:1], GELU)
         w2_bytes = keep.tile([P, N], U8, name="w2_bytes", align_bytes=64)
         nc.gpsimd.memset(w2_bytes[:], 0)
-        gate2_rows = keep.tile([P, U], F32, name="gate2_rows")
-        nc.gpsimd.memset(gate2_rows[:], 0.0)
 
         x_rows = xT.rearrange("(p j) c -> p j c", j=PACK)
         words = keep.tile([P, 2, S], U32, name="words")
@@ -105,26 +100,24 @@ def tile_picked_hop2_gelu_e_kernel(
         w1_codes = keep.tile([P, H], U32, name="w1_codes", align_bytes=64)
         w1_bytes = keep.tile([P, H], U8, name="w1_bytes", align_bytes=64)
 
-        def load_w1(c0, width):
-            raw = keep.tile([P, PACK, width], F32, name="w_raw%d" % c0)
-            nc.sync.dma_start(raw[:], w_rows[:, :, c0 : c0 + width])
-            return raw
+        def load_w1(half):
+            raw = keep.tile([P, PACK, HALF], F32, name="w_raw%d" % half)
+            nc.sync.dma_start(raw[:], w_rows[:, :, half * HALF : (half + 1) * HALF])
+            return raw[:].rearrange("p j (m f) -> p m j f", f=PACK)
 
-        def quantize_w1(raw, c0, width, engine, tag):
-            grouped = keep.tile([P, width * PACK], BF16, name="w_grouped%d" % c0, tag=tag, align_bytes=64)
-            copy(
-                engine,
-                grouped[:].rearrange("p (c i j) -> p c j i", i=LINE, j=PACK),
-                raw[:].rearrange("p j (c i) -> p c j i", i=LINE),
-            )
+        def quantize_w1(grouped, c0, width):
             nc.vector.quantize_mx(
                 out=w1_codes[:, c0 : c0 + width].bitcast(FP8X4), scales=w1_bytes[:, c0 : c0 + width], in_=grouped[:]
             )
 
-        w_raw0 = load_w1(0, P)
+        def low_tile(t, engine, tag):
+            grouped = keep.tile([P, P * PACK], BF16, name="w_low%d" % t, tag=tag, align_bytes=64)
+            copy(engine, grouped[:].rearrange("p (m e j) -> p m j e", e=2, j=PACK), w_raw[t][:, :, :, 0:2])
+            quantize_w1(grouped, t * P, P)
+
+        w_raw = [load_w1(0)]
         pos = [load_list("pos%d" % d, src) for d, src in enumerate((pos1, pos2, pos3))]
-        w_raw1 = load_w1(P, P)
-        w_raw2 = load_w1(2 * P, 2 * P)
+        w_raw.append(load_w1(1))
         gates = keep.tile([P, D, V], F32, name="gates")
         for d in range(D):
             nc.sync.dma_start(gates[:, d, :], gate[d])
@@ -136,11 +129,10 @@ def tile_picked_hop2_gelu_e_kernel(
                 w2_scales[0, 4 * quad : 4 * quad + 4, :].bitcast(I32),
             )
         nxt = [load_list("nxt%d" % d, src) for d, src in enumerate((nxt1, nxt2, nxt3))]
-        nc.sync.dma_start(gate2_rows[0:D, :], gate2[:, 0, :])
         gates2 = keep.tile([P, D, U], F32, name="gates2")
         nc.sync.dma_start(gates2[:], gate2.rearrange("d p r -> p d r"))
 
-        quantize_w1(w_raw0, 0, P, "s", "w_first")
+        low_tile(0, "v", "w_first")
 
         x_codes = keep.tile([P, S], U32, name="x_codes", tag="x_codes", align_bytes=64)
         x_bytes = keep.tile([P, S], U8, name="x_bytes", align_bytes=64)
@@ -148,9 +140,11 @@ def tile_picked_hop2_gelu_e_kernel(
 
         def first_layer(t, c0, width):
             if t == 0 and c0 + width == S:
-                acc = g_psum.tile([P, width], F32, name="g_acc")
+                acc = z_psum.tile([P, width], F32, name="h_last", tag="back0")
             elif t == 0:
                 acc = zt_psum.tile([P, width], F32, name="h_first", tag="zt_acc%d" % (c0 // PIECE))
+            elif t == 2:
+                acc = z_psum.tile([P, width], F32, name="h_third", tag="back%d" % (c0 // 512))
             else:
                 acc = h_psum.tile([P, width], F32, name="h_acc")
             nc.tensor.matmul_mx(
@@ -179,40 +173,54 @@ def tile_picked_hop2_gelu_e_kernel(
             nc.vector.quantize_mx(out=x_codes[:, cols].bitcast(FP8X4), scales=x_bytes[:, cols], in_=tile[:])
             first_layer(0, e0, run)
 
-        quantize_w1(w_raw1, P, P, "v", "woven_last")
-        for c0 in range(0, S, 512):
-            first_layer(1, c0, 512)
-        quantize_w1(w_raw2, 2 * P, 2 * P, "s", "woven_last")
-        for t in range(2, H_TILES):
+        low_tile(1, "v", "woven_last")
+        w_high = keep.tile([P, 2 * P * PACK], BF16, name="w_high", tag="woven_last", align_bytes=64)
+        for half in range(2):
+            nc.scalar.copy(
+                out=w_high[:].rearrange("p (e m j) -> p m j e", e=2, j=PACK)[:, half * 64 : (half + 1) * 64, :, :],
+                in_=w_raw[half][:, :, :, 2:4],
+            )
+        quantize_w1(w_high, 2 * P, 2 * P)
+        for t in range(1, H_TILES):
             for c0 in range(0, S, 512):
                 first_layer(t, c0, 512)
 
         g = [keep.tile([P, V], F32, name="g%d" % m) for m in range(M_TILES)]
 
-        zt_accs = [zt_psum.tile([P, H], F32, name="zt_acc", tag="zt_acc%d" % b) for b in range(BLOCKS)]
-        zts = [keep.tile([P, H], BF16, name="zt", tag="zt%d" % b) for b in range(BLOCKS)]
-
-        def round_z(b, i0, width):
-            nc.scalar.copy(
-                out=zts[b][:].rearrange("v (u p e) -> v u p e", u=2, e=2)[:, :, i0 // PACK : (i0 + width) // PACK, :],
-                in_=zt_accs[b][:, i0 : i0 + width].rearrange("v (p u e) -> v u p e", u=2, e=2),
+        def gather_term(term, t, d, v0, width):
+            nc.vector.tensor_tensor(
+                term, h[t][:].indirect(pos[d][:, v0 // 16 : (v0 + width) // 16]), gates[:, d, v0 : v0 + width], MULT
             )
 
-        def second_layer(b0, blocks):
-            v0, width = b0 * P, blocks * P
-            z_acc = z_psum.tile([P, 2, width], F32, name="z_acc")
-            for b in range(blocks):
-                zt_words = zts[b0 + b][:].bitcast(F32)
-                for u in range(2):
-                    nc.tensor.transpose(z_acc[:, u, b * P : (b + 1) * P], zt_words[:, u * P : (u + 1) * P], ident[:])
-            z_in = ring.tile([P, width * PACK], BF16, name="z_in", align_bytes=64)
-            nc.scalar.copy(
-                out=z_in[:].bitcast(F32).rearrange("p (v u) -> p v u", u=2), in_=z_acc[:].rearrange("p u v -> p v u")
-            )
-            z_codes = ring.tile([P, width], U32, name="z_codes", align_bytes=64)
-            z_bytes = ring.tile([P, width], U8, name="z_bytes", align_bytes=64)
+        def turned_sums(u, blocks):
+            accs = [zt_psum.tile([P, 2, P], F32, name="zt_acc", tag="zt_acc%d" % b) for b in range(blocks)]
+            for e in range(2):
+                for d in range(D):
+                    if u == 1:
+                        term = keep.tile([P, blocks * P], F32, name="high_term", tag="high%d_%d" % (e, d))
+                    else:
+                        term = picked.tile([P, blocks * P], F32, name="term")
+                    gather_term(term[:], 2 * u + e, d, 0, blocks * P)
+                    for b in range(blocks):
+                        nc.tensor.matmul(
+                            accs[b][:, e, :],
+                            term[:, b * P : (b + 1) * P],
+                            ident[:],
+                            start=(d == 0),
+                            stop=(d == D - 1),
+                            is_transpose=True,
+                        )
+            return accs
+
+        def rounded(acc_view, name):
+            zt = keep.tile([P, P, 2], BF16, name="zt", tag=name)
+            nc.scalar.copy(out=zt[:], in_=acc_view)
+            return zt[:].rearrange("v w e -> v (w e)").bitcast(F32)
+
+        def second_layer(z_in, v0, width, g_accs):
+            z_codes = keep.tile([P, width], U32, name="z_codes%d" % v0, align_bytes=64)
+            z_bytes = keep.tile([P, width], U8, name="z_bytes%d" % v0, align_bytes=64)
             nc.vector.quantize_mx(out=z_codes[:].bitcast(FP8X4), scales=z_bytes[:], in_=z_in[:])
-            g_accs = [g_psum.tile([P, width], F32, name="g_acc"), h_psum.tile([P, width], F32, name="h_acc")]
             for m in range(M_TILES):
                 nc.tensor.matmul_mx(
                     out=g_accs[m][:],
@@ -226,73 +234,78 @@ def tile_picked_hop2_gelu_e_kernel(
             for m in range(M_TILES):
                 nc.scalar.activation(g[m][:, v0 : v0 + width], g_accs[m][:], RELU)
 
-        def hop_term(term, t, d, b0, blocks):
-            v0, width = b0 * P, blocks * P
-            nc.vector.tensor_tensor(
-                term[:],
-                h[t][:].indirect(pos[d][:, v0 // 16 : (v0 + width) // 16]),
-                gates[:, d, v0 : v0 + width],
-                MULT,
+        wide = TURNED * P
+        back_turned = z_psum.tile([P, 2, wide], F32, name="back_turned", tag="back0")
+        accs = turned_sums(0, BLOCKS)
+        low = [rounded(accs[b][:].rearrange("v t (m e) -> v (t m) e", e=2), "zt_low%d" % b) for b in range(BLOCKS)]
+        for b in range(TURNED):
+            nc.tensor.transpose(back_turned[:, 0, b * P : (b + 1) * P], low[b], ident[:])
+
+        accs = turned_sums(1, TURNED)
+        for b in range(TURNED):
+            high = rounded(accs[b][:].rearrange("v e w -> v w e"), "zt_high%d" % b)
+            nc.tensor.transpose(back_turned[:, 1, b * P : (b + 1) * P], high, ident[:])
+        z_first = keep.tile([P, wide * PACK], BF16, name="z_first", tag="z_first", align_bytes=64)
+        nc.scalar.copy(
+            out=z_first[:].bitcast(F32).rearrange("p (v u) -> p v u", u=2),
+            in_=back_turned[:].rearrange("p u v -> p v u"),
+        )
+
+        back_added = z_psum.tile([P, V - wide], F32, name="back_added", tag="back0")
+        z_late = []
+        for b in range(TURNED, BLOCKS):
+            nc.tensor.transpose(back_added[:, (b - TURNED) * P : (b - TURNED + 1) * P], low[b], ident[:])
+        for b in range(TURNED, BLOCKS):
+            z_in = keep.tile([P, P * PACK], BF16, name="z_late%d" % b, align_bytes=64)
+            nc.scalar.copy(
+                out=z_in[:].bitcast(F32)[:, 0 : 2 * P : 2], in_=back_added[:, (b - TURNED) * P : (b - TURNED + 1) * P]
             )
-            for b in range(blocks):
-                nc.tensor.matmul(
-                    zt_accs[b0 + b][:, t * P : (t + 1) * P],
-                    term[:, b * P : (b + 1) * P],
-                    ident[:],
-                    start=(d == 0),
-                    stop=(d == D - 1),
-                    is_transpose=True,
-                )
+            z_late.append(z_in)
+        early = [keep.tile([P, 2, V - wide], F32, name="early", tag="high0_%d" % d) for d in range(D - 1)]
+        for e in range(2):
+            for d in range(D - 1):
+                gather_term(early[d][:, e, :], 2 + e, d, wide, V - wide)
+        second_layer(z_first, 0, wide, [h_psum.tile([P, wide], F32, name="h_acc") for m in range(M_TILES)])
+        part = keep.tile([P, 2, V - wide], F32, name="part")
+        for b in range(TURNED, BLOCKS):
+            last = keep.tile([P, 2, P], F32, name="last", tag="zt_low%d" % b if b == BLOCKS - 1 else "zt_high1")
+            for e in range(2):
+                gather_term(last[:, e, :], 2 + e, D - 1, b * P, P)
+            if b == TURNED:
+                nc.vector.tensor_tensor(part[:], early[0][:], early[1][:], ADD)
+            z_in = z_late[b - TURNED]
+            nc.vector.tensor_tensor(
+                z_in[:].rearrange("p (c i j) -> p c j i", i=LINE, j=PACK)[:, :, 2:4, :],
+                part[:, :, (b - TURNED) * P : (b - TURNED + 1) * P].rearrange("p e (c i) -> p c e i", i=LINE),
+                last[:].rearrange("p e (c i) -> p c e i", i=LINE),
+                ADD,
+            )
+            banks = ["zt_acc%d" % (M_TILES * (b - TURNED) + m) for m in range(M_TILES)]
+            second_layer(z_in, b * P, P, [zt_psum.tile([P, P], F32, name="g_acc", tag=bank) for bank in banks])
 
-        for t in range(WIDE_TILES):
-            for d in range(D):
-                if d == D - 1:
-                    term = keep.tile([P, V], F32, name="held_wide", tag=("woven_last", "x_codes")[t], align_bytes=64)
-                else:
-                    term = picked.tile([P, V], F32, name="term")
-                hop_term(term, t, d, 0, BLOCKS)
-        for b in range(BLOCKS):
-            round_z(b, 0, WIDE_TILES * P)
-        gate2_acc = g_psum.tile([P, R_BLOCKS, P], F32, name="g_acc")
-        for b in range(R_BLOCKS):
-            nc.tensor.transpose(gate2_acc[:, b, :], gate2_rows[:, b * P : (b + 1) * P], ident[:])
-        gate2_cols = keep.tile([P, R_BLOCKS, D], F32, name="gate2_cols")
-        nc.scalar.copy(out=gate2_cols[:], in_=gate2_acc[:, :, 0:D])
+        def root_term(m, d):
+            term = keep.tile([P, U], F32, name="root_term%d_%d" % (m, d))
+            nc.vector.tensor_tensor(term[:], g[m][:].indirect(nxt[d][:]), gates2[:, d, :], MULT)
+            return term
 
-        b0 = 0
-        for blocks in V_RUNS:
-            for t in range(WIDE_TILES, H_TILES):
-                for d in range(D):
-                    hop_term(picked.tile([P, blocks * P], F32, name="term"), t, d, b0, blocks)
-                for b in range(b0, b0 + blocks):
-                    round_z(b, t * P, P)
-            second_layer(b0, blocks)
-            b0 = b0 + blocks
-
-        total = keep.tile([P, U], F32, name="total0")
-        backs = [h_psum.tile([P, P], F32, name="h_acc") for b in range(R_BLOCKS)]
+        turned = [zt_psum.tile([P, P], F32, name="turned", tag="zt_acc%d" % b) for b in range(R_BLOCKS)]
         for d in range(D):
-            term = keep.tile([P, U], F32, name="root_term0_%d" % d)
-            nc.vector.tensor_copy(out=term[:], in_=g[0][:].indirect(nxt[d][:]))
-            turned = zt_psum.tile([P, R_BLOCKS, P], F32, name="turned", tag="zt_acc%d" % d)
+            term = root_term(0, d)
             for b in range(R_BLOCKS):
-                nc.tensor.transpose(turned[:, b, :], term[:, b * P : (b + 1) * P], ident[:])
-            root_scaled = keep.tile([P, R_BLOCKS, P], F32, name="root_scaled%d" % d)
-            for b in range(R_BLOCKS):
-                nc.scalar.activation(root_scaled[:, b, :], turned[:, b, :], COPY, scale=gate2_cols[:, b, d : d + 1])
                 nc.tensor.matmul(
-                    backs[b][:], root_scaled[:, b, :], ident[:], start=(d == 0), stop=(d == D - 1), is_transpose=True
+                    turned[b][:], term[:, b * P : (b + 1) * P], ident[:], start=(d == 0), stop=(d == D - 1), is_transpose=True
                 )
+        total = keep.tile([P, U], F32, name="total0")
         for b in range(R_BLOCKS):
-            nc.scalar.copy(out=total[:, b * P : (b + 1) * P], in_=backs[b][:])
+            summed = keep.tile([P, P], F32, name="summed%d" % b)
+            nc.scalar.copy(out=summed[:], in_=turned[b][:])
+            back = zt_psum.tile([P, P], F32, name="back", tag="zt_acc%d" % (R_BLOCKS + b))
+            nc.tensor.transpose(back[:], summed[:], ident[:])
+            nc.scalar.copy(out=total[:, b * P : (b + 1) * P], in_=back[:])
         nc.sync.dma_start(out[0:P, :], total[:])
 
-        terms = []
-        for d in range(D):
-            term = keep.tile([P, U], F32, name="root_term1_%d" % d)
-            nc.vector.tensor_tensor(term[:], g[1][:].indirect(nxt[d][:]), gates2[:, d, :], MULT)
-            terms.append(term)
-        part = keep.tile([P, U], F32, name="part")
+        terms = [root_term(1, d) for d in range(D)]
+        part = keep.tile([P, U], F32, name="root_part")
         nc.vector.tensor_tensor(part[:], terms[0][:], terms[1][:], ADD)
         total = keep.tile([P, U], F32, name="total1")
         nc.vector.tensor_tensor(total[:], part[:], terms[2][:], ADD)

@@ -22,7 +22,7 @@ P = 128
 PACK = 4
 LINE = 4
 PIECE = 256
-X_RUNS = (256, 256, 256, 128, 128)
+X_RUNS = (256, 256, 256, 256)
 H_TILES = H // P
 M_TILES = N // P
 CHUNKS = (
@@ -139,9 +139,7 @@ def tile_picked_hop2_gelu_e_kernel(
         h = [keep.tile([P, S], F32, name="h%d" % t) for t in range(H_TILES)]
 
         def first_layer(t, c0, width):
-            if t == 0 and c0 + width == S:
-                acc = z_psum.tile([P, width], F32, name="h_last", tag="back0")
-            elif t == 0:
+            if t == 0:
                 acc = zt_psum.tile([P, width], F32, name="h_first", tag="zt_acc%d" % (c0 // PIECE))
             elif t == 2:
                 acc = z_psum.tile([P, width], F32, name="h_third", tag="back%d" % (c0 // 512))
@@ -192,25 +190,10 @@ def tile_picked_hop2_gelu_e_kernel(
                 term, h[t][:].indirect(pos[d][:, v0 // 16 : (v0 + width) // 16]), gates[:, d, v0 : v0 + width], MULT
             )
 
-        def turned_sums(u, blocks):
-            accs = [zt_psum.tile([P, 2, P], F32, name="zt_acc", tag="zt_acc%d" % b) for b in range(blocks)]
-            for e in range(2):
-                for d in range(D):
-                    if u == 1:
-                        term = keep.tile([P, blocks * P], F32, name="high_term", tag="high%d_%d" % (e, d))
-                    else:
-                        term = picked.tile([P, blocks * P], F32, name="term")
-                    gather_term(term[:], 2 * u + e, d, 0, blocks * P)
-                    for b in range(blocks):
-                        nc.tensor.matmul(
-                            accs[b][:, e, :],
-                            term[:, b * P : (b + 1) * P],
-                            ident[:],
-                            start=(d == 0),
-                            stop=(d == D - 1),
-                            is_transpose=True,
-                        )
-            return accs
+        def turn(acc, term, b, d, last):
+            nc.tensor.matmul(
+                acc, term[:, b * P : (b + 1) * P], ident[:], start=(d == 0), stop=(d == last), is_transpose=True
+            )
 
         def rounded(acc_view, name):
             zt = keep.tile([P, P, 2], BF16, name="zt", tag=name)
@@ -235,53 +218,71 @@ def tile_picked_hop2_gelu_e_kernel(
                 nc.scalar.activation(g[m][:, v0 : v0 + width], g_accs[m][:], RELU)
 
         wide = TURNED * P
-        back_turned = z_psum.tile([P, 2, wide], F32, name="back_turned", tag="back0")
-        accs = turned_sums(0, BLOCKS)
+        late = range(TURNED, BLOCKS)
+
+        def late_cols(b):
+            return slice((b - TURNED) * P, (b - TURNED + 1) * P)
+
+        accs = [zt_psum.tile([P, 2, P], F32, name="zt_acc", tag="zt_acc%d" % b) for b in range(BLOCKS)]
+        for e in range(2):
+            for d in range(D):
+                term = picked.tile([P, V], F32, name="term")
+                gather_term(term[:], e, d, 0, V)
+                for b in range(BLOCKS):
+                    turn(accs[b][:, e, :], term, b, d, D - 1)
         low = [rounded(accs[b][:].rearrange("v t (m e) -> v (t m) e", e=2), "zt_low%d" % b) for b in range(BLOCKS)]
+        back_turned = z_psum.tile([P, 2, wide], F32, name="back_turned", tag="back0")
         for b in range(TURNED):
             nc.tensor.transpose(back_turned[:, 0, b * P : (b + 1) * P], low[b], ident[:])
+        back_added = h_psum.tile([P, V - wide], F32, name="h_acc")
+        for b in late:
+            nc.tensor.transpose(back_added[:, late_cols(b)], low[b], ident[:])
+        z_late = {}
+        for b in late:
+            z_late[b] = keep.tile([P, P * PACK], BF16, name="z_late%d" % b, align_bytes=64)
+            nc.scalar.copy(out=z_late[b][:].bitcast(F32)[:, 0 : 2 * P : 2], in_=back_added[:, late_cols(b)])
 
-        accs = turned_sums(1, TURNED)
+        accs = [zt_psum.tile([P, 2, P], F32, name="zt_acc", tag="zt_acc%d" % b) for b in range(BLOCKS)]
+        part = z_psum.tile([P, 2, V - wide], F32, name="part", tag="back1")
+        for e in range(2):
+            for d in range(D - 1):
+                term = picked.tile([P, V], F32, name="term")
+                gather_term(term[:], 2 + e, d, 0, V)
+                for b in range(BLOCKS):
+                    turn(accs[b][:, e, :], term, b, d, D - 1 if b < TURNED else D - 2)
+            for b in late:
+                two = keep.tile([P, P], F32, name="two_terms%d_%d" % (e, b))
+                nc.scalar.copy(out=two[:], in_=accs[b][:, e, :])
+                nc.tensor.transpose(part[:, e, late_cols(b)], two[:], ident[:])
+            term = keep.tile([P, wide], F32, name="third", tag="third%d" % e)
+            gather_term(term[:], 2 + e, D - 1, 0, wide)
+            for b in range(TURNED):
+                turn(accs[b][:, e, :], term, b, D - 1, D - 1)
         for b in range(TURNED):
             high = rounded(accs[b][:].rearrange("v e w -> v w e"), "zt_high%d" % b)
             nc.tensor.transpose(back_turned[:, 1, b * P : (b + 1) * P], high, ident[:])
-        z_first = keep.tile([P, wide * PACK], BF16, name="z_first", tag="z_first", align_bytes=64)
+        z_first = keep.tile([P, wide * PACK], BF16, name="z_first", align_bytes=64)
         nc.scalar.copy(
             out=z_first[:].bitcast(F32).rearrange("p (v u) -> p v u", u=2),
             in_=back_turned[:].rearrange("p u v -> p v u"),
         )
 
-        back_added = z_psum.tile([P, V - wide], F32, name="back_added", tag="back0")
-        z_late = []
-        for b in range(TURNED, BLOCKS):
-            nc.tensor.transpose(back_added[:, (b - TURNED) * P : (b - TURNED + 1) * P], low[b], ident[:])
-        for b in range(TURNED, BLOCKS):
-            z_in = keep.tile([P, P * PACK], BF16, name="z_late%d" % b, align_bytes=64)
-            nc.scalar.copy(
-                out=z_in[:].bitcast(F32)[:, 0 : 2 * P : 2], in_=back_added[:, (b - TURNED) * P : (b - TURNED + 1) * P]
-            )
-            z_late.append(z_in)
-        early = [keep.tile([P, 2, V - wide], F32, name="early", tag="high0_%d" % d) for d in range(D - 1)]
-        for e in range(2):
-            for d in range(D - 1):
-                gather_term(early[d][:, e, :], 2 + e, d, wide, V - wide)
-        second_layer(z_first, 0, wide, [h_psum.tile([P, wide], F32, name="h_acc") for m in range(M_TILES)])
-        part = keep.tile([P, 2, V - wide], F32, name="part")
-        for b in range(TURNED, BLOCKS):
-            last = keep.tile([P, 2, P], F32, name="last", tag="zt_low%d" % b if b == BLOCKS - 1 else "zt_high1")
+        last = {}
+        for b in late:
+            last[b] = keep.tile([P, 2, P], F32, name="last", tag="third%d" % (b - TURNED))
             for e in range(2):
-                gather_term(last[:, e, :], 2 + e, D - 1, b * P, P)
-            if b == TURNED:
-                nc.vector.tensor_tensor(part[:], early[0][:], early[1][:], ADD)
-            z_in = z_late[b - TURNED]
+                gather_term(last[b][:, e, :], 2 + e, D - 1, b * P, P)
+        second_layer(z_first, 0, wide, [h_psum.tile([P, wide], F32, name="h_acc") for m in range(M_TILES)])
+        for b in late:
             nc.vector.tensor_tensor(
-                z_in[:].rearrange("p (c i j) -> p c j i", i=LINE, j=PACK)[:, :, 2:4, :],
-                part[:, :, (b - TURNED) * P : (b - TURNED + 1) * P].rearrange("p e (c i) -> p c e i", i=LINE),
-                last[:].rearrange("p e (c i) -> p c e i", i=LINE),
+                z_late[b][:].rearrange("p (c i j) -> p c j i", i=LINE, j=PACK)[:, :, 2:4, :],
+                part[:, :, late_cols(b)].rearrange("p e (c i) -> p c e i", i=LINE),
+                last[b][:].rearrange("p e (c i) -> p c e i", i=LINE),
                 ADD,
             )
+        for b in late:
             banks = ["zt_acc%d" % (M_TILES * (b - TURNED) + m) for m in range(M_TILES)]
-            second_layer(z_in, b * P, P, [zt_psum.tile([P, P], F32, name="g_acc", tag=bank) for bank in banks])
+            second_layer(z_late[b], b * P, P, [zt_psum.tile([P, P], F32, name="g_acc", tag=bank) for bank in banks])
 
         def root_term(m, d):
             term = keep.tile([P, U], F32, name="root_term%d_%d" % (m, d))
@@ -302,11 +303,23 @@ def tile_picked_hop2_gelu_e_kernel(
             back = zt_psum.tile([P, P], F32, name="back", tag="zt_acc%d" % (R_BLOCKS + b))
             nc.tensor.transpose(back[:], summed[:], ident[:])
             nc.scalar.copy(out=total[:, b * P : (b + 1) * P], in_=back[:])
-        nc.sync.dma_start(out[0:P, :], total[:])
+        nc.scalar.dma_start(out[0:P, :], total[:])
 
-        terms = [root_term(1, d) for d in range(D)]
+        terms = [root_term(1, d) for d in range(D - 1)]
         part = keep.tile([P, U], F32, name="root_part")
-        nc.vector.tensor_tensor(part[:], terms[0][:], terms[1][:], ADD)
-        total = keep.tile([P, U], F32, name="total1")
-        nc.vector.tensor_tensor(total[:], part[:], terms[2][:], ADD)
-        nc.sync.dma_start(out[P : 2 * P, :], total[:])
+        thirds = []
+        for b in range(R_BLOCKS):
+            third = keep.tile([P, P], F32, name="root_third%d" % b)
+            nc.vector.tensor_tensor(
+                third[:],
+                g[1][:].indirect(nxt[D - 1][:, b * P // 16 : (b + 1) * P // 16]),
+                gates2[:, D - 1, b * P : (b + 1) * P],
+                MULT,
+            )
+            thirds.append(third)
+            if b == 0:
+                nc.vector.tensor_tensor(part[:], terms[0][:], terms[1][:], ADD)
+        for b in range(R_BLOCKS):
+            total = keep.tile([P, P], F32, name="total1_%d" % b)
+            nc.vector.tensor_tensor(total[:], part[:, b * P : (b + 1) * P], thirds[b][:], ADD)
+            nc.sync.dma_start(out[P : 2 * P, b * P : (b + 1) * P], total[:])

@@ -27,12 +27,13 @@ H_TILES = H // P
 M_TILES = N // P
 CHUNKS = (
     (((640, "v"), (384, "s")), ((640, "v"), (384, "s"))),
-    (((768, "s"), (256, "v")), ((512, "v"),), ((256, "v"),), ((160, "v"), (96, "s"))),
+    (((768, "s"), (256, "v")), ((640, "v"), (128, "s")), ((160, "v"), (96, "s"))),
 )
 BLOCKS = V // P
 TURNED = 2
 R_BLOCKS = U // P
 HALF = H // 2
+H_BANKS = (0, 4, 6, 4)
 
 
 def tile_picked_hop2_gelu_e_kernel(
@@ -48,10 +49,11 @@ def tile_picked_hop2_gelu_e_kernel(
 
     with ExitStack() as ctx:
         keep = ctx.enter_context(tc.tile_pool(name="keep", bufs=1))
-        picked = ctx.enter_context(tc.tile_pool(name="picked", bufs=4))
-        h_psum = ctx.enter_context(tc.psum_pool(name="h_psum", bufs=2))
-        zt_psum = ctx.enter_context(tc.psum_pool(name="zt_psum", bufs=1))
-        z_psum = ctx.enter_context(tc.psum_pool(name="z_psum", bufs=1))
+        picked = ctx.enter_context(tc.tile_pool(name="picked", bufs=6))
+        psum = ctx.enter_context(tc.psum_pool(name="psum", bufs=1))
+
+        def bank(n, shape):
+            return psum.tile(shape, F32, name="bank", tag="bank%d" % n)
 
         def load_list(name, src):
             tile = keep.tile(list(src.shape), U16, name=name)
@@ -139,12 +141,7 @@ def tile_picked_hop2_gelu_e_kernel(
         h = [keep.tile([P, S], F32, name="h%d" % t) for t in range(H_TILES)]
 
         def first_layer(t, c0, width):
-            if t == 0:
-                acc = zt_psum.tile([P, width], F32, name="h_first", tag="zt_acc%d" % (c0 // PIECE))
-            elif t == 2:
-                acc = z_psum.tile([P, width], F32, name="h_third", tag="back%d" % (c0 // 512))
-            else:
-                acc = h_psum.tile([P, width], F32, name="h_acc")
+            acc = bank(c0 // PIECE if t == 0 else H_BANKS[t] + c0 // 512, [P, width])
             nc.tensor.matmul_mx(
                 out=acc[:],
                 lhsT=w1_codes[:, t * P : (t + 1) * P].bitcast(FP8X4),
@@ -200,22 +197,22 @@ def tile_picked_hop2_gelu_e_kernel(
             nc.scalar.copy(out=zt[:], in_=acc_view)
             return zt[:].rearrange("v w e -> v (w e)").bitcast(F32)
 
-        def second_layer(z_in, v0, width, g_accs):
+        def quantize_z(z_in, v0, width):
             z_codes = keep.tile([P, width], U32, name="z_codes%d" % v0, align_bytes=64)
             z_bytes = keep.tile([P, width], U8, name="z_bytes%d" % v0, align_bytes=64)
             nc.vector.quantize_mx(out=z_codes[:].bitcast(FP8X4), scales=z_bytes[:], in_=z_in[:])
-            for m in range(M_TILES):
-                nc.tensor.matmul_mx(
-                    out=g_accs[m][:],
-                    lhsT=w2_codes[:, m * P : (m + 1) * P].bitcast(FP8X4),
-                    lhsT_scale=w2_bytes[:, m * P : (m + 1) * P],
-                    rhs=z_codes[:].bitcast(FP8X4),
-                    rhs_scale=z_bytes[:],
-                    start=True,
-                    stop=True,
-                )
-            for m in range(M_TILES):
-                nc.scalar.activation(g[m][:, v0 : v0 + width], g_accs[m][:], RELU)
+            return z_codes, z_bytes
+
+        def second_layer(acc, m, z_codes, z_bytes):
+            nc.tensor.matmul_mx(
+                out=acc,
+                lhsT=w2_codes[:, m * P : (m + 1) * P].bitcast(FP8X4),
+                lhsT_scale=w2_bytes[:, m * P : (m + 1) * P],
+                rhs=z_codes[:].bitcast(FP8X4),
+                rhs_scale=z_bytes[:],
+                start=True,
+                stop=True,
+            )
 
         wide = TURNED * P
         late = range(TURNED, BLOCKS)
@@ -223,7 +220,7 @@ def tile_picked_hop2_gelu_e_kernel(
         def late_cols(b):
             return slice((b - TURNED) * P, (b - TURNED + 1) * P)
 
-        accs = [zt_psum.tile([P, 2, P], F32, name="zt_acc", tag="zt_acc%d" % b) for b in range(BLOCKS)]
+        accs = [bank(b, [P, 2, P]) for b in range(BLOCKS)]
         for e in range(2):
             for d in range(D):
                 term = picked.tile([P, V], F32, name="term")
@@ -231,10 +228,10 @@ def tile_picked_hop2_gelu_e_kernel(
                 for b in range(BLOCKS):
                     turn(accs[b][:, e, :], term, b, d, D - 1)
         low = [rounded(accs[b][:].rearrange("v t (m e) -> v (t m) e", e=2), "zt_low%d" % b) for b in range(BLOCKS)]
-        back_turned = z_psum.tile([P, 2, wide], F32, name="back_turned", tag="back0")
+        back_turned = [bank(3 * b, [P, 2, P]) for b in range(TURNED)]
         for b in range(TURNED):
-            nc.tensor.transpose(back_turned[:, 0, b * P : (b + 1) * P], low[b], ident[:])
-        back_added = h_psum.tile([P, V - wide], F32, name="h_acc")
+            nc.tensor.transpose(back_turned[b][:, 0, :], low[b], ident[:])
+        back_added = bank(1, [P, V - wide])
         for b in late:
             nc.tensor.transpose(back_added[:, late_cols(b)], low[b], ident[:])
         z_late = {}
@@ -242,11 +239,12 @@ def tile_picked_hop2_gelu_e_kernel(
             z_late[b] = keep.tile([P, P * PACK], BF16, name="z_late%d" % b, align_bytes=64)
             nc.scalar.copy(out=z_late[b][:].bitcast(F32)[:, 0 : 2 * P : 2], in_=back_added[:, late_cols(b)])
 
-        accs = [zt_psum.tile([P, 2, P], F32, name="zt_acc", tag="zt_acc%d" % b) for b in range(BLOCKS)]
-        part = z_psum.tile([P, 2, V - wide], F32, name="part", tag="back1")
+        accs = [bank((6, 7, 4, 5)[b], [P, 2, P]) for b in range(BLOCKS)]
+        part = bank(2, [P, 2, V - wide])
+        high = [keep.tile([P, 2 * P], BF16, name="zt_high%d" % b) for b in range(TURNED)]
         for e in range(2):
             for d in range(D - 1):
-                term = picked.tile([P, V], F32, name="term")
+                term = keep.tile([P, V], F32, name="high_term", tag="high%d_%d" % (e, d))
                 gather_term(term[:], 2 + e, d, 0, V)
                 for b in range(BLOCKS):
                     turn(accs[b][:, e, :], term, b, d, D - 1 if b < TURNED else D - 2)
@@ -258,38 +256,45 @@ def tile_picked_hop2_gelu_e_kernel(
             gather_term(term[:], 2 + e, D - 1, 0, wide)
             for b in range(TURNED):
                 turn(accs[b][:, e, :], term, b, D - 1, D - 1)
+            for b in range(TURNED):
+                nc.scalar.copy(out=high[b][:, e : 2 * P : 2], in_=accs[b][:, e, :])
         for b in range(TURNED):
-            high = rounded(accs[b][:].rearrange("v e w -> v w e"), "zt_high%d" % b)
-            nc.tensor.transpose(back_turned[:, 1, b * P : (b + 1) * P], high, ident[:])
+            nc.tensor.transpose(back_turned[b][:, 1, :], high[b][:].bitcast(F32), ident[:])
         z_first = keep.tile([P, wide * PACK], BF16, name="z_first", align_bytes=64)
-        nc.scalar.copy(
-            out=z_first[:].bitcast(F32).rearrange("p (v u) -> p v u", u=2),
-            in_=back_turned[:].rearrange("p u v -> p v u"),
-        )
+        for b in range(TURNED):
+            nc.scalar.copy(
+                out=z_first[:].bitcast(F32).rearrange("p (v u) -> p v u", u=2)[:, b * P : (b + 1) * P, :],
+                in_=back_turned[b][:].rearrange("p u v -> p v u"),
+            )
 
-        last = {}
+        last = keep.tile([P, 2, V - wide], F32, name="last", tag="high1_0")
+        gather_term(last[:, 0, :], 2, D - 1, wide, V - wide)
         for b in late:
-            last[b] = keep.tile([P, 2, P], F32, name="last", tag="third%d" % (b - TURNED))
-            for e in range(2):
-                gather_term(last[b][:, e, :], 2 + e, D - 1, b * P, P)
-        second_layer(z_first, 0, wide, [h_psum.tile([P, wide], F32, name="h_acc") for m in range(M_TILES)])
+            gather_term(last[:, 1, late_cols(b)], 3, D - 1, b * P, P)
+        first_mx = quantize_z(z_first, 0, wide)
         for b in late:
             nc.vector.tensor_tensor(
                 z_late[b][:].rearrange("p (c i j) -> p c j i", i=LINE, j=PACK)[:, :, 2:4, :],
                 part[:, :, late_cols(b)].rearrange("p e (c i) -> p c e i", i=LINE),
-                last[b][:].rearrange("p e (c i) -> p c e i", i=LINE),
+                last[:, :, late_cols(b)].rearrange("p e (c i) -> p c e i", i=LINE),
                 ADD,
             )
-        for b in late:
-            banks = ["zt_acc%d" % (M_TILES * (b - TURNED) + m) for m in range(M_TILES)]
-            second_layer(z_late[b], b * P, P, [zt_psum.tile([P, P], F32, name="g_acc", tag=bank) for bank in banks])
+        late_mx = {b: quantize_z(z_late[b], b * P, P) for b in late}
+        for m in range(M_TILES):
+            acc = bank(1, [P, wide])
+            second_layer(acc[:], m, *first_mx)
+            nc.scalar.activation(g[m][:, 0:wide], acc[:], RELU)
+            acc = bank(7 - m, [P, V - wide])
+            for b in late:
+                second_layer(acc[:, late_cols(b)], m, *late_mx[b])
+            nc.scalar.activation(g[m][:, wide:V], acc[:], RELU)
 
         def root_term(m, d):
             term = keep.tile([P, U], F32, name="root_term%d_%d" % (m, d))
             nc.vector.tensor_tensor(term[:], g[m][:].indirect(nxt[d][:]), gates2[:, d, :], MULT)
             return term
 
-        turned = [zt_psum.tile([P, P], F32, name="turned", tag="zt_acc%d" % b) for b in range(R_BLOCKS)]
+        turned = [bank(2 * b, [P, P]) for b in range(R_BLOCKS)]
         for d in range(D):
             term = root_term(0, d)
             for b in range(R_BLOCKS):
@@ -300,7 +305,7 @@ def tile_picked_hop2_gelu_e_kernel(
         for b in range(R_BLOCKS):
             summed = keep.tile([P, P], F32, name="summed%d" % b)
             nc.scalar.copy(out=summed[:], in_=turned[b][:])
-            back = zt_psum.tile([P, P], F32, name="back", tag="zt_acc%d" % (R_BLOCKS + b))
+            back = bank(3 + b, [P, P])
             nc.tensor.transpose(back[:], summed[:], ident[:])
             nc.scalar.copy(out=total[:, b * P : (b + 1) * P], in_=back[:])
         nc.scalar.dma_start(out[0:P, :], total[:])

@@ -134,7 +134,7 @@ def tile_picked_hop2_gelu_e_kernel(
         gates2 = keep.tile([P, D, U], F32, name="gates2")
         nc.sync.dma_start(gates2[:], gate2.rearrange("d p r -> p d r"))
 
-        low_tile(0, "v", "w_first")
+        low_tile(0, "s", "w_first")
 
         x_codes = keep.tile([P, S], U32, name="x_codes", tag="x_codes", align_bytes=64)
         x_bytes = keep.tile([P, S], U8, name="x_bytes", align_bytes=64)
@@ -284,10 +284,10 @@ def tile_picked_hop2_gelu_e_kernel(
             acc = bank(1, [P, wide])
             second_layer(acc[:], m, *first_mx)
             nc.scalar.activation(g[m][:, 0:wide], acc[:], RELU)
-            acc = bank(7 - m, [P, V - wide])
             for b in late:
-                second_layer(acc[:, late_cols(b)], m, *late_mx[b])
-            nc.scalar.activation(g[m][:, wide:V], acc[:], RELU)
+                acc = bank(((7, 5), (6, 4))[m][b - TURNED], [P, P])
+                second_layer(acc[:], m, *late_mx[b])
+                nc.scalar.activation(g[m][:, b * P : (b + 1) * P], acc[:], RELU)
 
         def root_term(m, d):
             term = keep.tile([P, U], F32, name="root_term%d_%d" % (m, d))

@@ -26,7 +26,7 @@ X_RUNS = (256, 256, 256, 256)
 H_TILES = H // P
 M_TILES = N // P
 CHUNKS = (
-    (((640, "v"), (384, "s")), ((640, "v"), (384, "s"))),
+    (((1024, "v"), (512, "s")), ((336, "v"), (176, "s"))),
     (((768, "s"), (256, "v")), ((640, "v"), (128, "s")), ((160, "v"), (96, "s"))),
 )
 BLOCKS = V // P

@@ -26,8 +26,8 @@ X_RUNS = (256, 256, 256, 256)
 H_TILES = H // P
 M_TILES = N // P
 CHUNKS = (
-    (((1024, "v"), (512, "s")), ((336, "v"), (176, "s"))),
-    (((768, "s"), (256, "v")), ((640, "v"), (128, "s")), ((160, "v"), (96, "s"))),
+    (((832, "v"), (448, "s")), ((512, "v"), (256, "s"))),
+    (((448, "v"), (320, "s")), ((432, "v"), (208, "s")), ((256, "v"), (128, "s")), ((160, "v"), (96, "s"))),
 )
 BLOCKS = V // P
 TURNED = 2
@@ -68,30 +68,34 @@ def tile_picked_hop2_gelu_e_kernel(
         w2_bytes = keep.tile([P, N], U8, name="w2_bytes", align_bytes=64)
         nc.gpsimd.memset(w2_bytes[:], 0)
 
-        x_rows = xT.rearrange("(p j) c -> p j c", j=PACK)
+        x_rows = xT.rearrange("(p j) c -> p (j c)", j=PACK)
         words = keep.tile([P, 2, S], U32, name="words")
         offs_t = None
         for u in range(2):
             pairs = keep.tile([P, T], U32, name="pairs%d" % u)
             pairs_bf = pairs[:].bitcast(BF16)
+            raw = keep.tile([P, 2 * T], F32, name="raw%d" % u)
+            planes = raw[:].rearrange("p (e c) -> p e c", e=2)
             c0 = 0
             for n, shares in enumerate(CHUNKS[u]):
                 width = sum(share for share, engine in shares)
-                raw = keep.tile([P, 2, width], F32, name="raw%d_%d" % (u, n))
-                nc.sync.dma_start(raw[:], x_rows[:, 2 * u : 2 * u + 2, c0 : c0 + width])
-                s0 = 0
+                first = 0 if n == 0 else T + c0
+                nc.sync.dma_start(
+                    raw[:, first : T + c0 + width], x_rows[:, 2 * u * T + first : (2 * u + 1) * T + c0 + width]
+                )
+                if u == 0 and n == 0:
+                    offs_t = load_list("offs_t", offs)
+                s0 = c0
                 for share, engine in shares:
                     copy(
                         engine,
-                        pairs_bf[:, 2 * (c0 + s0) : 2 * (c0 + s0 + share)].rearrange(
+                        pairs_bf[:, 2 * s0 : 2 * (s0 + share)].rearrange(
                             "p (c i e) -> p c e i", i=LINE, e=2
                         ),
-                        raw[:, :, s0 : s0 + share].rearrange("p e (c i) -> p c e i", i=LINE),
+                        planes[:, :, s0 : s0 + share].rearrange("p e (c i) -> p c e i", i=LINE),
                     )
                     s0 = s0 + share
                 c0 = c0 + width
-            if u == 0:
-                offs_t = load_list("offs_t", offs)
             run = S if u == 0 else PIECE
             for e0 in range(0, S, run):
                 nc.vector.tensor_copy(

@@ -22,7 +22,8 @@ P = 128
 PACK = 4
 LINE = 4
 PIECE = 256
-X_RUNS = (256, 256, 256, 256)
+X_RUNS = (256, 256, 256, 128, 128)
+X_BANKS = (0, 1, 2, 3, 6)
 H_TILES = H // P
 M_TILES = N // P
 CHUNKS = (
@@ -138,14 +139,21 @@ def tile_picked_hop2_gelu_e_kernel(
         gates2 = keep.tile([P, D, U], F32, name="gates2")
         nc.sync.dma_start(gates2[:], gate2.rearrange("d p r -> p d r"))
 
-        low_tile(0, "s", "w_first")
+        w_first = keep.tile([P, P * PACK], BF16, name="w_first", align_bytes=64)
+        nc.gpsimd.tensor_copy(
+            out=w_first[:].rearrange("p (m e j) -> p m e j", e=2, j=PACK),
+            in_=w_raw[0][:, :, :, 0:2].rearrange("p m j e -> p m e j"),
+        )
+        quantize_w1(w_first, 0, P)
 
         x_codes = keep.tile([P, S], U32, name="x_codes", tag="x_codes", align_bytes=64)
         x_bytes = keep.tile([P, S], U8, name="x_bytes", align_bytes=64)
         h = [keep.tile([P, S], F32, name="h%d" % t) for t in range(H_TILES)]
 
+        starts = [sum(X_RUNS[:q]) for q in range(len(X_RUNS))]
+
         def first_layer(t, c0, width):
-            acc = bank(c0 // PIECE if t == 0 else H_BANKS[t] + c0 // 512, [P, width])
+            acc = bank(X_BANKS[starts.index(c0)] if t == 0 else H_BANKS[t] + c0 // 512, [P, width])
             nc.tensor.matmul_mx(
                 out=acc[:],
                 lhsT=w1_codes[:, t * P : (t + 1) * P].bitcast(FP8X4),
@@ -157,19 +165,23 @@ def tile_picked_hop2_gelu_e_kernel(
             )
             nc.scalar.activation(h[t][:, c0 : c0 + width], acc[:], GELU)
 
-        starts = [sum(X_RUNS[:q]) for q in range(len(X_RUNS))]
         woven = []
-        for e0, run in zip(starts, X_RUNS):
-            tag = "woven_last" if e0 + run == S else "woven%d" % e0
-            tile = keep.tile([P, run * PACK], BF16, name="woven", tag=tag, align_bytes=64)
+        for e0 in range(0, S, PIECE):
+            tag = "woven_last" if e0 + PIECE == S else "woven%d" % e0
+            tile = keep.tile([P, PIECE * PACK], BF16, name="woven", tag=tag, align_bytes=64)
             nc.scalar.copy(
                 out=tile[:].bitcast(U32).rearrange("p (c u) -> p c u", u=2),
-                in_=words[:, :, e0 : e0 + run].rearrange("p u c -> p c u"),
+                in_=words[:, :, e0 : e0 + PIECE].rearrange("p u c -> p c u"),
             )
             woven.append(tile)
-        for e0, run, tile in zip(starts, X_RUNS, woven):
+        for e0, run in zip(starts, X_RUNS):
             cols = slice(e0, e0 + run)
-            nc.vector.quantize_mx(out=x_codes[:, cols].bitcast(FP8X4), scales=x_bytes[:, cols], in_=tile[:])
+            at = e0 % PIECE * PACK
+            nc.vector.quantize_mx(
+                out=x_codes[:, cols].bitcast(FP8X4),
+                scales=x_bytes[:, cols],
+                in_=woven[e0 // PIECE][:, at : at + run * PACK],
+            )
             first_layer(0, e0, run)
 
         low_tile(1, "v", "woven_last")
@@ -201,22 +213,24 @@ def tile_picked_hop2_gelu_e_kernel(
             nc.scalar.copy(out=zt[:], in_=acc_view)
             return zt[:].rearrange("v w e -> v (w e)").bitcast(F32)
 
-        def quantize_z(z_in, v0, width):
-            z_codes = keep.tile([P, width], U32, name="z_codes%d" % v0, align_bytes=64)
-            z_bytes = keep.tile([P, width], U8, name="z_bytes%d" % v0, align_bytes=64)
-            nc.vector.quantize_mx(out=z_codes[:].bitcast(FP8X4), scales=z_bytes[:], in_=z_in[:])
-            return z_codes, z_bytes
+        z_codes = keep.tile([P, V], U32, name="z_codes", align_bytes=64)
+        z_bytes = keep.tile([P, V], U8, name="z_bytes", align_bytes=64)
 
-        def second_layer(acc, m, z_codes, z_bytes):
+        def quantize_z(z_in, b):
+            cols = slice(b * P, (b + 1) * P)
+            nc.vector.quantize_mx(out=z_codes[:, cols].bitcast(FP8X4), scales=z_bytes[:, cols], in_=z_in[:])
+
+        def second_layer(acc, m, cols):
             nc.tensor.matmul_mx(
-                out=acc,
+                out=acc[:],
                 lhsT=w2_codes[:, m * P : (m + 1) * P].bitcast(FP8X4),
                 lhsT_scale=w2_bytes[:, m * P : (m + 1) * P],
-                rhs=z_codes[:].bitcast(FP8X4),
-                rhs_scale=z_bytes[:],
+                rhs=z_codes[:, cols].bitcast(FP8X4),
+                rhs_scale=z_bytes[:, cols],
                 start=True,
                 stop=True,
             )
+            nc.scalar.activation(g[m][:, cols], acc[:], RELU)
 
         wide = TURNED * P
         late = range(TURNED, BLOCKS)
@@ -264,10 +278,10 @@ def tile_picked_hop2_gelu_e_kernel(
                 nc.scalar.copy(out=high[b][:, e : 2 * P : 2], in_=accs[b][:, e, :])
         for b in range(TURNED):
             nc.tensor.transpose(back_turned[b][:, 1, :], high[b][:].bitcast(F32), ident[:])
-        z_first = keep.tile([P, wide * PACK], BF16, name="z_first", align_bytes=64)
         for b in range(TURNED):
+            z_late[b] = keep.tile([P, P * PACK], BF16, name="z_first%d" % b, align_bytes=64)
             nc.scalar.copy(
-                out=z_first[:].bitcast(F32).rearrange("p (v u) -> p v u", u=2)[:, b * P : (b + 1) * P, :],
+                out=z_late[b][:].bitcast(F32).rearrange("p (v u) -> p v u", u=2),
                 in_=back_turned[b][:].rearrange("p u v -> p v u"),
             )
 
@@ -275,7 +289,6 @@ def tile_picked_hop2_gelu_e_kernel(
         gather_term(last[:, 0, :], 2, D - 1, wide, V - wide)
         for b in late:
             gather_term(last[:, 1, late_cols(b)], 3, D - 1, b * P, P)
-        first_mx = quantize_z(z_first, 0, wide)
         for b in late:
             nc.vector.tensor_tensor(
                 z_late[b][:].rearrange("p (c i j) -> p c j i", i=LINE, j=PACK)[:, :, 2:4, :],
@@ -283,15 +296,10 @@ def tile_picked_hop2_gelu_e_kernel(
                 last[:, :, late_cols(b)].rearrange("p e (c i) -> p c e i", i=LINE),
                 ADD,
             )
-        late_mx = {b: quantize_z(z_late[b], b * P, P) for b in late}
-        for m in range(M_TILES):
-            acc = bank(1, [P, wide])
-            second_layer(acc[:], m, *first_mx)
-            nc.scalar.activation(g[m][:, 0:wide], acc[:], RELU)
-            for b in late:
-                acc = bank(((7, 5), (6, 4))[m][b - TURNED], [P, P])
-                second_layer(acc[:], m, *late_mx[b])
-                nc.scalar.activation(g[m][:, b * P : (b + 1) * P], acc[:], RELU)
+        for b in list(late) + list(range(TURNED)):
+            quantize_z(z_late[b], b)
+            second_layer(bank((1, 6, 4, 5)[b], [P, P]), 0, slice(b * P, (b + 1) * P))
+        second_layer(bank(7, [P, V]), 1, slice(0, V))
 
         def root_term(m, d):
             term = keep.tile([P, U], F32, name="root_term%d_%d" % (m, d))

@@ -16,6 +16,7 @@ FP8X4 = mybir.dt.float8_e4m3fn_x4
 MULT = mybir.AluOpType.mult
 ADD = mybir.AluOpType.add
 GELU = mybir.ActivationFunctionType.Gelu_apprx_tanh
+COPY = mybir.ActivationFunctionType.Copy
 RELU = mybir.ActivationFunctionType.Relu
 
 P = 128
@@ -26,10 +27,6 @@ X_RUNS = (256, 256, 256, 128, 128)
 X_BANKS = (0, 1, 2, 3, 6)
 H_TILES = H // P
 M_TILES = N // P
-CHUNKS = (
-    (((832, "v"), (448, "s")), ((512, "v"), (256, "s"))),
-    (((448, "v"), (320, "s")), ((432, "v"), (208, "s")), ((256, "v"), (128, "s")), ((160, "v"), (96, "s"))),
-)
 BLOCKS = V // P
 TURNED = 2
 R_BLOCKS = U // P
@@ -69,38 +66,40 @@ def tile_picked_hop2_gelu_e_kernel(
         w2_bytes = keep.tile([P, N], U8, name="w2_bytes", align_bytes=64)
         nc.gpsimd.memset(w2_bytes[:], 0)
 
-        x_rows = xT.rearrange("(p j) c -> p (j c)", j=PACK)
-        words = keep.tile([P, 2, S], U32, name="words")
-        offs_t = None
-        for u in range(2):
-            pairs = keep.tile([P, T], U32, name="pairs%d" % u)
-            pairs_bf = pairs[:].bitcast(BF16)
-            raw = keep.tile([P, 2 * T], F32, name="raw%d" % u)
-            planes = raw[:].rearrange("p (e c) -> p e c", e=2)
-            c0 = 0
-            for n, shares in enumerate(CHUNKS[u]):
-                width = sum(share for share, engine in shares)
-                first = 0 if n == 0 else T + c0
-                nc.sync.dma_start(
-                    raw[:, first : T + c0 + width], x_rows[:, 2 * u * T + first : (2 * u + 1) * T + c0 + width]
-                )
-                if u == 0 and n == 0:
-                    offs_t = load_list("offs_t", offs)
-                s0 = c0
-                for share, engine in shares:
-                    copy(
-                        engine,
-                        pairs_bf[:, 2 * s0 : 2 * (s0 + share)].rearrange(
-                            "p (c i e) -> p c e i", i=LINE, e=2
-                        ),
-                        planes[:, :, s0 : s0 + share].rearrange("p e (c i) -> p c e i", i=LINE),
-                    )
-                    s0 = s0 + share
-                c0 = c0 + width
-            run = S if u == 0 else PIECE
+        x_rows = xT.rearrange("(p j) c -> p j c", j=PACK)
+        offs_t = load_list("offs_t", offs)
+        planes = []
+        for j in range(PACK):
+            plane = keep.tile([P, T], F32, name="plane%d" % j)
+            nc.sync.dma_start(plane[:], x_rows[:, j, :])
+            planes.append(plane)
+        word_row = keep.tile([P, 2 * S], U32, name="word_row")
+        words = word_row[:].rearrange("p (u c) -> p u c", u=2)
+        halves = word_row[:].bitcast(BF16)
+        low_planes = keep.tile([P, 2 * S], BF16, name="low_planes")
+        rest = S - PIECE
+        nc.vector.tensor_copy(out=low_planes[:, 0:S], in_=planes[0][:].indirect(offs_t[:]))
+        nc.vector.tensor_copy(out=low_planes[:, S : S + rest], in_=planes[1][:].indirect(offs_t[:, 0 : rest // 16]))
+        rounded_plane = keep.tile([P, T], BF16, name="rounded_plane")
+        nc.gpsimd.tensor_copy(out=rounded_plane[:], in_=planes[1][:])
+
+        def pair_low(e0, run):
+            nc.scalar.copy(
+                out=halves[:, 2 * e0 : 2 * (e0 + run)].rearrange("p (c i e) -> p c e i", i=LINE, e=2),
+                in_=low_planes[:].rearrange("p (e c) -> p e c", e=2)[:, :, e0 : e0 + run].rearrange(
+                    "p e (c i) -> p c e i", i=LINE
+                ),
+            )
+
+        pair_low(0, rest)
+        nc.scalar.activation(low_planes[:, S + rest : 2 * S], rounded_plane[:].indirect(offs_t[:, rest // 16 :]), COPY)
+        pair_low(rest, PIECE)
+        for e in range(2):
+            run = S if e == 0 else PIECE
             for e0 in range(0, S, run):
                 nc.vector.tensor_copy(
-                    out=words[:, u, e0 : e0 + run], in_=pairs[:].indirect(offs_t[:, e0 // 16 : (e0 + run) // 16])
+                    out=halves[:, 2 * (S + e0) + e : 2 * (S + e0 + run) : 2],
+                    in_=planes[2 + e][:].indirect(offs_t[:, e0 // 16 : (e0 + run) // 16]),
                 )
 
         w_rows = w1.rearrange("(p j) c -> p j c", j=PACK)

@@ -39,12 +39,6 @@ def tile_picked_hop2_gelu_e_kernel(
 ):
     nc = tc.nc
 
-    def copy(engine, dst, src):
-        if engine == "v":
-            nc.vector.tensor_copy(out=dst, in_=src)
-        else:
-            nc.scalar.copy(out=dst, in_=src)
-
     with ExitStack() as ctx:
         keep = ctx.enter_context(tc.tile_pool(name="keep", bufs=1))
         picked = ctx.enter_context(tc.tile_pool(name="picked", bufs=6))
@@ -73,7 +67,7 @@ def tile_picked_hop2_gelu_e_kernel(
             plane = keep.tile([P, T], F32, name="plane%d" % j)
             nc.sync.dma_start(plane[:], x_rows[:, j, :])
             planes.append(plane)
-        word_row = keep.tile([P, 2 * S], U32, name="word_row")
+        word_row = keep.tile([P, 2 * S], U32, name="word_row", tag="word_row", align_bytes=64)
         words = word_row[:].rearrange("p (u c) -> p u c", u=2)
         halves = word_row[:].bitcast(BF16)
         low_planes = keep.tile([P, 2 * S], BF16, name="low_planes")
@@ -106,24 +100,21 @@ def tile_picked_hop2_gelu_e_kernel(
         w1_codes = keep.tile([P, H], U32, name="w1_codes", align_bytes=64)
         w1_bytes = keep.tile([P, H], U8, name="w1_bytes", align_bytes=64)
 
+        w_raw = keep.tile([P, PACK, H], F32, name="w_raw")
+        w_cols = w_raw[:].rearrange("p j (m f) -> p m j f", f=PACK)
+
         def load_w1(half):
-            raw = keep.tile([P, PACK, HALF], F32, name="w_raw%d" % half)
-            nc.sync.dma_start(raw[:], w_rows[:, :, half * HALF : (half + 1) * HALF])
-            return raw[:].rearrange("p j (m f) -> p m j f", f=PACK)
+            cols = slice(half * HALF, (half + 1) * HALF)
+            nc.sync.dma_start(w_raw[:, :, cols], w_rows[:, :, cols])
 
         def quantize_w1(grouped, c0, width):
             nc.vector.quantize_mx(
-                out=w1_codes[:, c0 : c0 + width].bitcast(FP8X4), scales=w1_bytes[:, c0 : c0 + width], in_=grouped[:]
+                out=w1_codes[:, c0 : c0 + width].bitcast(FP8X4), scales=w1_bytes[:, c0 : c0 + width], in_=grouped
             )
 
-        def low_tile(t, engine, tag):
-            grouped = keep.tile([P, P * PACK], BF16, name="w_low%d" % t, tag=tag, align_bytes=64)
-            copy(engine, grouped[:].rearrange("p (m e j) -> p m j e", e=2, j=PACK), w_raw[t][:, :, :, 0:2])
-            quantize_w1(grouped, t * P, P)
-
-        w_raw = [load_w1(0)]
+        load_w1(0)
         pos = [load_list("pos%d" % d, src) for d, src in enumerate((pos1, pos2, pos3))]
-        w_raw.append(load_w1(1))
+        load_w1(1)
         gates = keep.tile([P, D, V], F32, name="gates")
         for d in range(D):
             nc.sync.dma_start(gates[:, d, :], gate[d])
@@ -141,9 +132,9 @@ def tile_picked_hop2_gelu_e_kernel(
         w_first = keep.tile([P, P * PACK], BF16, name="w_first", align_bytes=64)
         nc.gpsimd.tensor_copy(
             out=w_first[:].rearrange("p (m e j) -> p m e j", e=2, j=PACK),
-            in_=w_raw[0][:, :, :, 0:2].rearrange("p m j e -> p m e j"),
+            in_=w_cols[:, 0:64, :, 0:2].rearrange("p m j e -> p m e j"),
         )
-        quantize_w1(w_first, 0, P)
+        quantize_w1(w_first[:], 0, P)
 
         x_codes = keep.tile([P, S], U32, name="x_codes", tag="x_codes", align_bytes=64)
         x_bytes = keep.tile([P, S], U8, name="x_bytes", align_bytes=64)
@@ -183,14 +174,14 @@ def tile_picked_hop2_gelu_e_kernel(
             )
             first_layer(0, e0, run)
 
-        low_tile(1, "v", "woven_last")
         w_high = keep.tile([P, 2 * P * PACK], BF16, name="w_high", tag="woven_last", align_bytes=64)
-        for half in range(2):
-            nc.scalar.copy(
-                out=w_high[:].rearrange("p (e m j) -> p m j e", e=2, j=PACK)[:, half * 64 : (half + 1) * 64, :, :],
-                in_=w_raw[half][:, :, :, 2:4],
-            )
-        quantize_w1(w_high, 2 * P, 2 * P)
+        nc.vector.tensor_copy(out=w_high[:].rearrange("p (e m j) -> p m j e", e=2, j=PACK), in_=w_cols[:, :, :, 2:4])
+        w_second = keep.tile([P, P * PACK], BF16, name="w_second", tag="word_row", align_bytes=64)
+        nc.vector.tensor_copy(
+            out=w_second[:].rearrange("p (m e j) -> p m j e", e=2, j=PACK), in_=w_cols[:, 64:P, :, 0:2]
+        )
+        quantize_w1(w_high[:], 2 * P, 2 * P)
+        quantize_w1(w_second[:], P, P)
         for t in range(1, H_TILES):
             for c0 in range(0, S, 512):
                 first_layer(t, c0, 512)
@@ -238,10 +229,14 @@ def tile_picked_hop2_gelu_e_kernel(
             return slice((b - TURNED) * P, (b - TURNED + 1) * P)
 
         accs = [bank(b, [P, 2, P]) for b in range(BLOCKS)]
+        first_terms = keep.tile([P, D * V], F32, name="first_terms", tag="woven_last", align_bytes=64)
         for e in range(2):
             for d in range(D):
-                term = picked.tile([P, V], F32, name="term")
-                gather_term(term[:], e, d, 0, V)
+                if e == 0:
+                    term = first_terms[:, d * V : (d + 1) * V]
+                else:
+                    term = picked.tile([P, V], F32, name="term")[:]
+                gather_term(term, e, d, 0, V)
                 for b in range(BLOCKS):
                     turn(accs[b][:, e, :], term, b, d, D - 1)
         low = [rounded(accs[b][:].rearrange("v t (m e) -> v (t m) e", e=2), "zt_low%d" % b) for b in range(BLOCKS)]

@@ -23,8 +23,8 @@ P = 128
 PACK = 4
 LINE = 4
 PIECE = 256
-X_RUNS = (256, 256, 256, 128, 128)
-X_BANKS = (0, 1, 2, 3, 6)
+X_RUNS = (256, 256, 256, 256)
+X_BANKS = (0, 1, 2, 3)
 H_TILES = H // P
 M_TILES = N // P
 BLOCKS = V // P
@@ -67,7 +67,7 @@ def tile_picked_hop2_gelu_e_kernel(
             plane = keep.tile([P, T], F32, name="plane%d" % j)
             nc.sync.dma_start(plane[:], x_rows[:, j, :])
             planes.append(plane)
-        word_row = keep.tile([P, 2 * S], U32, name="word_row", tag="word_row", align_bytes=64)
+        word_row = keep.tile([P, 2 * S], U32, name="word_row")
         words = word_row[:].rearrange("p (u c) -> p u c", u=2)
         halves = word_row[:].bitcast(BF16)
         low_planes = keep.tile([P, 2 * S], BF16, name="low_planes")
@@ -164,6 +164,9 @@ def tile_picked_hop2_gelu_e_kernel(
                 in_=words[:, :, e0 : e0 + PIECE].rearrange("p u c -> p c u"),
             )
             woven.append(tile)
+        w_high = keep.tile([P, 2 * P * PACK], BF16, name="w_high", tag="w_high", align_bytes=64)
+        high_view = w_high[:].rearrange("p (e m j) -> p m j e", e=2, j=PACK)
+        nc.scalar.copy(out=high_view[:, 0:64, :, :], in_=w_cols[:, 0:64, :, 2:4])
         for e0, run in zip(starts, X_RUNS):
             cols = slice(e0, e0 + run)
             at = e0 % PIECE * PACK
@@ -174,9 +177,8 @@ def tile_picked_hop2_gelu_e_kernel(
             )
             first_layer(0, e0, run)
 
-        w_high = keep.tile([P, 2 * P * PACK], BF16, name="w_high", tag="woven_last", align_bytes=64)
-        nc.vector.tensor_copy(out=w_high[:].rearrange("p (e m j) -> p m j e", e=2, j=PACK), in_=w_cols[:, :, :, 2:4])
-        w_second = keep.tile([P, P * PACK], BF16, name="w_second", tag="word_row", align_bytes=64)
+        nc.vector.tensor_copy(out=high_view[:, 64:P, :, :], in_=w_cols[:, 64:P, :, 2:4])
+        w_second = keep.tile([P, P * PACK], BF16, name="w_second", tag="woven_last", align_bytes=64)
         nc.vector.tensor_copy(
             out=w_second[:].rearrange("p (m e j) -> p m j e", e=2, j=PACK), in_=w_cols[:, 64:P, :, 0:2]
         )
@@ -229,7 +231,7 @@ def tile_picked_hop2_gelu_e_kernel(
             return slice((b - TURNED) * P, (b - TURNED + 1) * P)
 
         accs = [bank(b, [P, 2, P]) for b in range(BLOCKS)]
-        first_terms = keep.tile([P, D * V], F32, name="first_terms", tag="woven_last", align_bytes=64)
+        first_terms = keep.tile([P, D * V], F32, name="first_terms", tag="w_high", align_bytes=64)
         for e in range(2):
             for d in range(D):
                 if e == 0:

@@ -21,17 +21,27 @@ RELU = mybir.ActivationFunctionType.Relu
 
 P = 128
 PACK = 4
+PER_COLUMN = 16
 LINE = 4
 PIECE = 256
-X_RUNS = (256, 256, 256, 256)
-X_BANKS = (0, 1, 2, 3)
+BANK = 512
 H_TILES = H // P
 M_TILES = N // P
 BLOCKS = V // P
-TURNED = 2
+EARLY = 2
 R_BLOCKS = U // P
 HALF = H // 2
-H_BANKS = (0, 4, 6, 4)
+GROUPS = HALF // PACK
+TERM_BUFFERS = 6
+H_BANKS = {1: 4, 2: 6, 3: 4}
+HIGH_BANKS = (6, 7, 4, 5)
+EARLY_BACK_BANKS = (0, 3)
+LATE_BACK_BANK = 1
+LATE_PART_BANK = 2
+G_BANKS = (1, 6, 4, 5)
+G_LAST_BANK = 7
+ROOT_BANKS = (0, 2)
+ROOT_BACK_BANKS = (3, 4)
 
 
 def tile_picked_hop2_gelu_e_kernel(
@@ -41,7 +51,7 @@ def tile_picked_hop2_gelu_e_kernel(
 
     with ExitStack() as ctx:
         keep = ctx.enter_context(tc.tile_pool(name="keep", bufs=1))
-        picked = ctx.enter_context(tc.tile_pool(name="picked", bufs=6))
+        picked = ctx.enter_context(tc.tile_pool(name="picked", bufs=TERM_BUFFERS))
         psum = ctx.enter_context(tc.psum_pool(name="psum", bufs=1))
 
         def bank(n, shape):
@@ -52,6 +62,12 @@ def tile_picked_hop2_gelu_e_kernel(
             nc.sync.dma_start(tile[:], src)
             return tile
 
+        def entries(list_tile, first, count):
+            return list_tile[:, first // PER_COLUMN : (first + count) // PER_COLUMN]
+
+        def block(b):
+            return slice(b * P, (b + 1) * P)
+
         ident = keep.tile([P, P], F32, name="ident")
         make_identity(nc, ident[:])
         warm = keep.tile([P, 2], F32, name="warm")
@@ -61,40 +77,48 @@ def tile_picked_hop2_gelu_e_kernel(
         nc.gpsimd.memset(w2_bytes[:], 0)
 
         x_rows = xT.rearrange("(p j) c -> p j c", j=PACK)
-        offs_t = load_list("offs_t", offs)
-        planes = []
-        for j in range(PACK):
+
+        def load_plane(j):
             plane = keep.tile([P, T], F32, name="plane%d" % j)
             nc.sync.dma_start(plane[:], x_rows[:, j, :])
-            planes.append(plane)
+            return plane
+
+        planes = [load_plane(0)]
+        offs_t = load_list("offs_t", offs)
+        planes.extend([load_plane(j) for j in range(1, PACK)])
+
         word_row = keep.tile([P, 2 * S], U32, name="word_row")
         words = word_row[:].rearrange("p (u c) -> p u c", u=2)
         halves = word_row[:].bitcast(BF16)
         low_planes = keep.tile([P, 2 * S], BF16, name="low_planes")
         rest = S - PIECE
         nc.vector.tensor_copy(out=low_planes[:, 0:S], in_=planes[0][:].indirect(offs_t[:]))
-        nc.vector.tensor_copy(out=low_planes[:, S : S + rest], in_=planes[1][:].indirect(offs_t[:, 0 : rest // 16]))
+        nc.vector.tensor_copy(out=low_planes[:, S : S + rest], in_=planes[1][:].indirect(entries(offs_t, 0, rest)))
         rounded_plane = keep.tile([P, T], BF16, name="rounded_plane")
         nc.gpsimd.tensor_copy(out=rounded_plane[:], in_=planes[1][:])
 
-        def pair_low(e0, run):
+        def pair_low(e0, count):
             nc.scalar.copy(
-                out=halves[:, 2 * e0 : 2 * (e0 + run)].rearrange("p (c i e) -> p c e i", i=LINE, e=2),
-                in_=low_planes[:].rearrange("p (e c) -> p e c", e=2)[:, :, e0 : e0 + run].rearrange(
+                out=halves[:, 2 * e0 : 2 * (e0 + count)].rearrange("p (c i e) -> p c e i", i=LINE, e=2),
+                in_=low_planes[:].rearrange("p (e c) -> p e c", e=2)[:, :, e0 : e0 + count].rearrange(
                     "p e (c i) -> p c e i", i=LINE
                 ),
             )
 
+        def gather_high(e, e0, count):
+            nc.vector.tensor_copy(
+                out=halves[:, 2 * (S + e0) + e : 2 * (S + e0 + count) : 2],
+                in_=planes[2 + e][:].indirect(entries(offs_t, e0, count)),
+            )
+
         pair_low(0, rest)
-        nc.scalar.activation(low_planes[:, S + rest : 2 * S], rounded_plane[:].indirect(offs_t[:, rest // 16 :]), COPY)
+        nc.scalar.activation(
+            low_planes[:, S + rest : 2 * S], rounded_plane[:].indirect(entries(offs_t, rest, PIECE)), COPY
+        )
         pair_low(rest, PIECE)
-        for e in range(2):
-            run = S if e == 0 else PIECE
-            for e0 in range(0, S, run):
-                nc.vector.tensor_copy(
-                    out=halves[:, 2 * (S + e0) + e : 2 * (S + e0 + run) : 2],
-                    in_=planes[2 + e][:].indirect(offs_t[:, e0 // 16 : (e0 + run) // 16]),
-                )
+        gather_high(0, 0, S)
+        for e0 in range(0, S, PIECE):
+            gather_high(1, e0, PIECE)
 
         w_rows = w1.rearrange("(p j) c -> p j c", j=PACK)
         w1_codes = keep.tile([P, H], U32, name="w1_codes", align_bytes=64)
@@ -132,22 +156,20 @@ def tile_picked_hop2_gelu_e_kernel(
         w_first = keep.tile([P, P * PACK], BF16, name="w_first", align_bytes=64)
         nc.gpsimd.tensor_copy(
             out=w_first[:].rearrange("p (m e j) -> p m e j", e=2, j=PACK),
-            in_=w_cols[:, 0:64, :, 0:2].rearrange("p m j e -> p m e j"),
+            in_=w_cols[:, 0:GROUPS, :, 0:2].rearrange("p m j e -> p m e j"),
         )
         quantize_w1(w_first[:], 0, P)
 
-        x_codes = keep.tile([P, S], U32, name="x_codes", tag="x_codes", align_bytes=64)
+        x_codes = keep.tile([P, S], U32, name="x_codes", align_bytes=64)
         x_bytes = keep.tile([P, S], U8, name="x_bytes", align_bytes=64)
         h = [keep.tile([P, S], F32, name="h%d" % t) for t in range(H_TILES)]
 
-        starts = [sum(X_RUNS[:q]) for q in range(len(X_RUNS))]
-
-        def first_layer(t, c0, width):
-            acc = bank(X_BANKS[starts.index(c0)] if t == 0 else H_BANKS[t] + c0 // 512, [P, width])
+        def first_layer(t, c0, width, n):
+            acc = bank(n, [P, width])
             nc.tensor.matmul_mx(
                 out=acc[:],
-                lhsT=w1_codes[:, t * P : (t + 1) * P].bitcast(FP8X4),
-                lhsT_scale=w1_bytes[:, t * P : (t + 1) * P],
+                lhsT=w1_codes[:, block(t)].bitcast(FP8X4),
+                lhsT_scale=w1_bytes[:, block(t)],
                 rhs=x_codes[:, c0 : c0 + width].bitcast(FP8X4),
                 rhs_scale=x_bytes[:, c0 : c0 + width],
                 start=True,
@@ -157,8 +179,7 @@ def tile_picked_hop2_gelu_e_kernel(
 
         woven = []
         for e0 in range(0, S, PIECE):
-            tag = "woven_last" if e0 + PIECE == S else "woven%d" % e0
-            tile = keep.tile([P, PIECE * PACK], BF16, name="woven", tag=tag, align_bytes=64)
+            tile = keep.tile([P, PIECE * PACK], BF16, name="woven", tag="woven%d" % e0, align_bytes=64)
             nc.scalar.copy(
                 out=tile[:].bitcast(U32).rearrange("p (c u) -> p c u", u=2),
                 in_=words[:, :, e0 : e0 + PIECE].rearrange("p u c -> p c u"),
@@ -166,57 +187,44 @@ def tile_picked_hop2_gelu_e_kernel(
             woven.append(tile)
         w_high = keep.tile([P, 2 * P * PACK], BF16, name="w_high", tag="w_high", align_bytes=64)
         high_view = w_high[:].rearrange("p (e m j) -> p m j e", e=2, j=PACK)
-        nc.scalar.copy(out=high_view[:, 0:64, :, :], in_=w_cols[:, 0:64, :, 2:4])
-        for e0, run in zip(starts, X_RUNS):
-            cols = slice(e0, e0 + run)
-            at = e0 % PIECE * PACK
-            nc.vector.quantize_mx(
-                out=x_codes[:, cols].bitcast(FP8X4),
-                scales=x_bytes[:, cols],
-                in_=woven[e0 // PIECE][:, at : at + run * PACK],
-            )
-            first_layer(0, e0, run)
+        nc.scalar.copy(out=high_view[:, 0:GROUPS, :, :], in_=w_cols[:, 0:GROUPS, :, 2:4])
+        for n, e0 in enumerate(range(0, S, PIECE)):
+            cols = slice(e0, e0 + PIECE)
+            nc.vector.quantize_mx(out=x_codes[:, cols].bitcast(FP8X4), scales=x_bytes[:, cols], in_=woven[n][:])
+            first_layer(0, e0, PIECE, n)
 
-        nc.vector.tensor_copy(out=high_view[:, 64:P, :, :], in_=w_cols[:, 64:P, :, 2:4])
-        w_second = keep.tile([P, P * PACK], BF16, name="w_second", tag="woven_last", align_bytes=64)
+        nc.vector.tensor_copy(out=high_view[:, GROUPS:P, :, :], in_=w_cols[:, GROUPS:P, :, 2:4])
+        w_second = keep.tile([P, P * PACK], BF16, name="w_second", tag="woven%d" % (S - PIECE), align_bytes=64)
         nc.vector.tensor_copy(
-            out=w_second[:].rearrange("p (m e j) -> p m j e", e=2, j=PACK), in_=w_cols[:, 64:P, :, 0:2]
+            out=w_second[:].rearrange("p (m e j) -> p m j e", e=2, j=PACK), in_=w_cols[:, GROUPS:P, :, 0:2]
         )
         quantize_w1(w_high[:], 2 * P, 2 * P)
         quantize_w1(w_second[:], P, P)
         for t in range(1, H_TILES):
-            for c0 in range(0, S, 512):
-                first_layer(t, c0, 512)
+            for half in range(S // BANK):
+                first_layer(t, half * BANK, BANK, H_BANKS[t] + half)
 
         g = [keep.tile([P, V], F32, name="g%d" % m) for m in range(M_TILES)]
 
         def gather_term(term, t, d, v0, width):
             nc.vector.tensor_tensor(
-                term, h[t][:].indirect(pos[d][:, v0 // 16 : (v0 + width) // 16]), gates[:, d, v0 : v0 + width], MULT
+                term, h[t][:].indirect(entries(pos[d], v0, width)), gates[:, d, v0 : v0 + width], MULT
             )
 
         def turn(acc, term, b, d, last):
-            nc.tensor.matmul(
-                acc, term[:, b * P : (b + 1) * P], ident[:], start=(d == 0), stop=(d == last), is_transpose=True
-            )
-
-        def rounded(acc_view, name):
-            zt = keep.tile([P, P, 2], BF16, name="zt", tag=name)
-            nc.scalar.copy(out=zt[:], in_=acc_view)
-            return zt[:].rearrange("v w e -> v (w e)").bitcast(F32)
+            nc.tensor.matmul(acc, term[:, block(b)], ident[:], start=(d == 0), stop=(d == last), is_transpose=True)
 
         z_codes = keep.tile([P, V], U32, name="z_codes", align_bytes=64)
         z_bytes = keep.tile([P, V], U8, name="z_bytes", align_bytes=64)
 
-        def quantize_z(z_in, b):
-            cols = slice(b * P, (b + 1) * P)
-            nc.vector.quantize_mx(out=z_codes[:, cols].bitcast(FP8X4), scales=z_bytes[:, cols], in_=z_in[:])
+        def quantize_z(values, b):
+            nc.vector.quantize_mx(out=z_codes[:, block(b)].bitcast(FP8X4), scales=z_bytes[:, block(b)], in_=values[:])
 
         def second_layer(acc, m, cols):
             nc.tensor.matmul_mx(
                 out=acc[:],
-                lhsT=w2_codes[:, m * P : (m + 1) * P].bitcast(FP8X4),
-                lhsT_scale=w2_bytes[:, m * P : (m + 1) * P],
+                lhsT=w2_codes[:, block(m)].bitcast(FP8X4),
+                lhsT_scale=w2_bytes[:, block(m)],
                 rhs=z_codes[:, cols].bitcast(FP8X4),
                 rhs_scale=z_bytes[:, cols],
                 start=True,
@@ -224,115 +232,112 @@ def tile_picked_hop2_gelu_e_kernel(
             )
             nc.scalar.activation(g[m][:, cols], acc[:], RELU)
 
-        wide = TURNED * P
-        late = range(TURNED, BLOCKS)
+        early = range(EARLY)
+        late = range(EARLY, BLOCKS)
+        early_width = EARLY * P
+        late_width = V - early_width
 
         def late_cols(b):
-            return slice((b - TURNED) * P, (b - TURNED + 1) * P)
+            return block(b - EARLY)
 
-        accs = [bank(b, [P, 2, P]) for b in range(BLOCKS)]
+        low_sums = [bank(b, [P, 2, P]) for b in range(BLOCKS)]
         first_terms = keep.tile([P, D * V], F32, name="first_terms", tag="w_high", align_bytes=64)
-        for e in range(2):
+        for t in range(2):
             for d in range(D):
-                if e == 0:
+                if t == 0:
                     term = first_terms[:, d * V : (d + 1) * V]
                 else:
                     term = picked.tile([P, V], F32, name="term")[:]
-                gather_term(term, e, d, 0, V)
+                gather_term(term, t, d, 0, V)
                 for b in range(BLOCKS):
-                    turn(accs[b][:, e, :], term, b, d, D - 1)
-        low = [rounded(accs[b][:].rearrange("v t (m e) -> v (t m) e", e=2), "zt_low%d" % b) for b in range(BLOCKS)]
-        back_turned = [bank(3 * b, [P, 2, P]) for b in range(TURNED)]
-        for b in range(TURNED):
-            nc.tensor.transpose(back_turned[b][:, 0, :], low[b], ident[:])
-        back_added = bank(1, [P, V - wide])
+                    turn(low_sums[b][:, t, :], term, b, d, D - 1)
+        low_words = []
+        for b in range(BLOCKS):
+            pairs = keep.tile([P, P, 2], BF16, name="low_pairs%d" % b)
+            nc.scalar.copy(out=pairs[:], in_=low_sums[b][:].rearrange("v t (m e) -> v (t m) e", e=2))
+            low_words.append(pairs[:].rearrange("v w e -> v (w e)").bitcast(F32))
+        early_back = [bank(EARLY_BACK_BANKS[b], [P, 2, P]) for b in early]
+        for b in early:
+            nc.tensor.transpose(early_back[b][:, 0, :], low_words[b], ident[:])
+        late_back = bank(LATE_BACK_BANK, [P, late_width])
         for b in late:
-            nc.tensor.transpose(back_added[:, late_cols(b)], low[b], ident[:])
-        z_late = {}
+            nc.tensor.transpose(late_back[:, late_cols(b)], low_words[b], ident[:])
+        z_in = {}
         for b in late:
-            z_late[b] = keep.tile([P, P * PACK], BF16, name="z_late%d" % b, align_bytes=64)
-            nc.scalar.copy(out=z_late[b][:].bitcast(F32)[:, 0 : 2 * P : 2], in_=back_added[:, late_cols(b)])
+            z_in[b] = keep.tile([P, P * PACK], BF16, name="z_in%d" % b, align_bytes=64)
+            nc.scalar.copy(out=z_in[b][:].bitcast(F32)[:, 0 : 2 * P : 2], in_=late_back[:, late_cols(b)])
 
-        accs = [bank((6, 7, 4, 5)[b], [P, 2, P]) for b in range(BLOCKS)]
-        part = bank(2, [P, 2, V - wide])
-        high = [keep.tile([P, 2 * P], BF16, name="zt_high%d" % b) for b in range(TURNED)]
+        high_sums = [bank(HIGH_BANKS[b], [P, 2, P]) for b in range(BLOCKS)]
+        late_part = bank(LATE_PART_BANK, [P, 2, late_width])
+        high_pairs = [keep.tile([P, 2 * P], BF16, name="high_pairs%d" % b) for b in early]
         for e in range(2):
             for d in range(D - 1):
                 term = keep.tile([P, V], F32, name="high_term", tag="high%d_%d" % (e, d))
                 gather_term(term[:], 2 + e, d, 0, V)
                 for b in range(BLOCKS):
-                    turn(accs[b][:, e, :], term, b, d, D - 1 if b < TURNED else D - 2)
+                    turn(high_sums[b][:, e, :], term, b, d, D - 1 if b < EARLY else D - 2)
             for b in late:
                 two = keep.tile([P, P], F32, name="two_terms%d_%d" % (e, b))
-                nc.scalar.copy(out=two[:], in_=accs[b][:, e, :])
-                nc.tensor.transpose(part[:, e, late_cols(b)], two[:], ident[:])
-            term = keep.tile([P, wide], F32, name="third", tag="third%d" % e)
-            gather_term(term[:], 2 + e, D - 1, 0, wide)
-            for b in range(TURNED):
-                turn(accs[b][:, e, :], term, b, D - 1, D - 1)
-            for b in range(TURNED):
-                nc.scalar.copy(out=high[b][:, e : 2 * P : 2], in_=accs[b][:, e, :])
-        for b in range(TURNED):
-            nc.tensor.transpose(back_turned[b][:, 1, :], high[b][:].bitcast(F32), ident[:])
-        for b in range(TURNED):
-            z_late[b] = keep.tile([P, P * PACK], BF16, name="z_first%d" % b, align_bytes=64)
+                nc.scalar.copy(out=two[:], in_=high_sums[b][:, e, :])
+                nc.tensor.transpose(late_part[:, e, late_cols(b)], two[:], ident[:])
+            term = keep.tile([P, early_width], F32, name="early_third%d" % e)
+            gather_term(term[:], 2 + e, D - 1, 0, early_width)
+            for b in early:
+                turn(high_sums[b][:, e, :], term, b, D - 1, D - 1)
+            for b in early:
+                nc.scalar.copy(out=high_pairs[b][:, e : 2 * P : 2], in_=high_sums[b][:, e, :])
+        for b in early:
+            nc.tensor.transpose(early_back[b][:, 1, :], high_pairs[b][:].bitcast(F32), ident[:])
+        for b in early:
+            z_in[b] = keep.tile([P, P * PACK], BF16, name="z_in%d" % b, align_bytes=64)
             nc.scalar.copy(
-                out=z_late[b][:].bitcast(F32).rearrange("p (v u) -> p v u", u=2),
-                in_=back_turned[b][:].rearrange("p u v -> p v u"),
+                out=z_in[b][:].bitcast(F32).rearrange("p (v u) -> p v u", u=2),
+                in_=early_back[b][:].rearrange("p u v -> p v u"),
             )
 
-        last = keep.tile([P, 2, V - wide], F32, name="last", tag="high1_0")
-        gather_term(last[:, 0, :], 2, D - 1, wide, V - wide)
+        late_third = keep.tile([P, 2, late_width], F32, name="late_third", tag="high1_0")
+        gather_term(late_third[:, 0, :], 2, D - 1, early_width, late_width)
         for b in late:
-            gather_term(last[:, 1, late_cols(b)], 3, D - 1, b * P, P)
+            gather_term(late_third[:, 1, late_cols(b)], 3, D - 1, b * P, P)
         for b in late:
             nc.vector.tensor_tensor(
-                z_late[b][:].rearrange("p (c i j) -> p c j i", i=LINE, j=PACK)[:, :, 2:4, :],
-                part[:, :, late_cols(b)].rearrange("p e (c i) -> p c e i", i=LINE),
-                last[:, :, late_cols(b)].rearrange("p e (c i) -> p c e i", i=LINE),
+                z_in[b][:].rearrange("p (c i j) -> p c j i", i=LINE, j=PACK)[:, :, 2:4, :],
+                late_part[:, :, late_cols(b)].rearrange("p e (c i) -> p c e i", i=LINE),
+                late_third[:, :, late_cols(b)].rearrange("p e (c i) -> p c e i", i=LINE),
                 ADD,
             )
-        for b in list(late) + list(range(TURNED)):
-            quantize_z(z_late[b], b)
-            second_layer(bank((1, 6, 4, 5)[b], [P, P]), 0, slice(b * P, (b + 1) * P))
-        second_layer(bank(7, [P, V]), 1, slice(0, V))
+        for b in list(late) + list(early):
+            quantize_z(z_in[b], b)
+            second_layer(bank(G_BANKS[b], [P, P]), 0, block(b))
+        second_layer(bank(G_LAST_BANK, [P, V]), 1, slice(0, V))
 
-        def root_term(m, d):
-            term = keep.tile([P, U], F32, name="root_term%d_%d" % (m, d))
-            nc.vector.tensor_tensor(term[:], g[m][:].indirect(nxt[d][:]), gates2[:, d, :], MULT)
+        def root_term(m, d, r0, width):
+            term = keep.tile([P, width], F32, name="root_term%d_%d_%d" % (m, d, r0))
+            nc.vector.tensor_tensor(
+                term[:], g[m][:].indirect(entries(nxt[d], r0, width)), gates2[:, d, r0 : r0 + width], MULT
+            )
             return term
 
-        turned = [bank(2 * b, [P, P]) for b in range(R_BLOCKS)]
+        root_sums = [bank(ROOT_BANKS[b], [P, P]) for b in range(R_BLOCKS)]
         for d in range(D):
-            term = root_term(0, d)
+            term = root_term(0, d, 0, U)
             for b in range(R_BLOCKS):
-                nc.tensor.matmul(
-                    turned[b][:], term[:, b * P : (b + 1) * P], ident[:], start=(d == 0), stop=(d == D - 1), is_transpose=True
-                )
-        total = keep.tile([P, U], F32, name="total0")
+                turn(root_sums[b][:], term, b, d, D - 1)
+        first_rows = keep.tile([P, U], F32, name="first_rows")
         for b in range(R_BLOCKS):
             summed = keep.tile([P, P], F32, name="summed%d" % b)
-            nc.scalar.copy(out=summed[:], in_=turned[b][:])
-            back = bank(3 + b, [P, P])
+            nc.scalar.copy(out=summed[:], in_=root_sums[b][:])
+            back = bank(ROOT_BACK_BANKS[b], [P, P])
             nc.tensor.transpose(back[:], summed[:], ident[:])
-            nc.scalar.copy(out=total[:, b * P : (b + 1) * P], in_=back[:])
-        nc.scalar.dma_start(out[0:P, :], total[:])
+            nc.scalar.copy(out=first_rows[:, block(b)], in_=back[:])
+        nc.scalar.dma_start(out[0:P, :], first_rows[:])
 
-        terms = [root_term(1, d) for d in range(D - 1)]
-        part = keep.tile([P, U], F32, name="root_part")
-        thirds = []
+        terms = [root_term(1, d, 0, U) for d in range(D - 1)]
+        root_part = keep.tile([P, U], F32, name="root_part")
+        thirds = [root_term(1, D - 1, 0, P)]
+        nc.vector.tensor_tensor(root_part[:], terms[0][:], terms[1][:], ADD)
+        thirds.append(root_term(1, D - 1, P, P))
         for b in range(R_BLOCKS):
-            third = keep.tile([P, P], F32, name="root_third%d" % b)
-            nc.vector.tensor_tensor(
-                third[:],
-                g[1][:].indirect(nxt[D - 1][:, b * P // 16 : (b + 1) * P // 16]),
-                gates2[:, D - 1, b * P : (b + 1) * P],
-                MULT,
-            )
-            thirds.append(third)
-            if b == 0:
-                nc.vector.tensor_tensor(part[:], terms[0][:], terms[1][:], ADD)
-        for b in range(R_BLOCKS):
-            total = keep.tile([P, P], F32, name="total1_%d" % b)
-            nc.vector.tensor_tensor(total[:], part[:, b * P : (b + 1) * P], thirds[b][:], ADD)
-            nc.sync.dma_start(out[P : 2 * P, b * P : (b + 1) * P], total[:])
+            last_rows = keep.tile([P, P], F32, name="last_rows%d" % b)
+            nc.vector.tensor_tensor(last_rows[:], root_part[:, block(b)], thirds[b][:], ADD)
+            nc.sync.dma_start(out[P : 2 * P, block(b)], last_rows[:])

@@ -83,42 +83,36 @@ def tile_picked_hop2_gelu_e_kernel(
             nc.sync.dma_start(plane[:], x_rows[:, j, :])
             return plane
 
-        planes = [load_plane(0)]
+        planes = {2: load_plane(2)}
         offs_t = load_list("offs_t", offs)
-        planes.extend([load_plane(j) for j in range(1, PACK)])
+        for j in (0, 1, 3):
+            planes[j] = load_plane(j)
 
         word_row = keep.tile([P, 2 * S], U32, name="word_row")
         words = word_row[:].rearrange("p (u c) -> p u c", u=2)
         halves = word_row[:].bitcast(BF16)
-        low_planes = keep.tile([P, 2 * S], BF16, name="low_planes")
         rest = S - PIECE
-        nc.vector.tensor_copy(out=low_planes[:, 0:S], in_=planes[0][:].indirect(offs_t[:]))
-        nc.vector.tensor_copy(out=low_planes[:, S : S + rest], in_=planes[1][:].indirect(entries(offs_t, 0, rest)))
-        rounded_plane = keep.tile([P, T], BF16, name="rounded_plane")
-        nc.gpsimd.tensor_copy(out=rounded_plane[:], in_=planes[1][:])
 
-        def pair_low(e0, count):
-            nc.scalar.copy(
-                out=halves[:, 2 * e0 : 2 * (e0 + count)].rearrange("p (c i e) -> p c e i", i=LINE, e=2),
-                in_=low_planes[:].rearrange("p (e c) -> p e c", e=2)[:, :, e0 : e0 + count].rearrange(
-                    "p e (c i) -> p c e i", i=LINE
-                ),
+        def half_words(j, e0, count):
+            first = 2 * (j // 2 * S + e0)
+            return halves[:, first + j % 2 : first + 2 * count : 2]
+
+        def gather_half(j, e0, count):
+            nc.vector.tensor_copy(out=half_words(j, e0, count), in_=planes[j][:].indirect(entries(offs_t, e0, count)))
+
+        gather_half(2, 0, S)
+        gather_half(0, 0, rest)
+        gather_half(1, 0, rest)
+        rounded = [keep.tile([P, T], BF16, name="rounded%d" % j) for j in range(2)]
+        nc.gpsimd.tensor_copy(out=rounded[0][:], in_=planes[0][:])
+        nc.gpsimd.tensor_copy(out=rounded[1][:, 0 : T // 2], in_=planes[1][:, 0 : T // 2])
+        nc.scalar.copy(out=rounded[1][:, T // 2 : T], in_=planes[1][:, T // 2 : T])
+        for j in range(2):
+            nc.scalar.activation(
+                half_words(j, rest, PIECE), rounded[j][:].indirect(entries(offs_t, rest, PIECE)), COPY
             )
-
-        def gather_high(e, e0, count):
-            nc.vector.tensor_copy(
-                out=halves[:, 2 * (S + e0) + e : 2 * (S + e0 + count) : 2],
-                in_=planes[2 + e][:].indirect(entries(offs_t, e0, count)),
-            )
-
-        pair_low(0, rest)
-        nc.scalar.activation(
-            low_planes[:, S + rest : 2 * S], rounded_plane[:].indirect(entries(offs_t, rest, PIECE)), COPY
-        )
-        pair_low(rest, PIECE)
-        gather_high(0, 0, S)
         for e0 in range(0, S, PIECE):
-            gather_high(1, e0, PIECE)
+            gather_half(3, e0, PIECE)
 
         w_rows = w1.rearrange("(p j) c -> p j c", j=PACK)
         w1_codes = keep.tile([P, H], U32, name="w1_codes", align_bytes=64)

@@ -32,6 +32,7 @@ EARLY = 2
 R_BLOCKS = U // P
 HALF = H // 2
 GROUPS = HALF // PACK
+POOL_GROUPS = 40
 TERM_BUFFERS = 6
 H_BANKS = {1: 4, 2: 6, 3: 4}
 HIGH_BANKS = (6, 7, 4, 5)
@@ -149,10 +150,9 @@ def tile_picked_hop2_gelu_e_kernel(
 
         w_first = keep.tile([P, P * PACK], BF16, name="w_first", align_bytes=64)
         nc.gpsimd.tensor_copy(
-            out=w_first[:].rearrange("p (m e j) -> p m e j", e=2, j=PACK),
-            in_=w_cols[:, 0:GROUPS, :, 0:2].rearrange("p m j e -> p m e j"),
+            out=w_first[:].rearrange("p (m e j) -> p m e j", e=2, j=PACK)[:, 0:POOL_GROUPS, :, :],
+            in_=w_cols[:, 0:POOL_GROUPS, :, 0:2].rearrange("p m j e -> p m e j"),
         )
-        quantize_w1(w_first[:], 0, P)
 
         x_codes = keep.tile([P, S], U32, name="x_codes", align_bytes=64)
         x_bytes = keep.tile([P, S], U8, name="x_bytes", align_bytes=64)
@@ -179,6 +179,12 @@ def tile_picked_hop2_gelu_e_kernel(
                 in_=words[:, :, e0 : e0 + PIECE].rearrange("p u c -> p c u"),
             )
             woven.append(tile)
+            if e0 == PIECE:
+                nc.scalar.copy(
+                    out=w_first[:].rearrange("p (m e j) -> p m j e", e=2, j=PACK)[:, POOL_GROUPS:GROUPS, :, :],
+                    in_=w_cols[:, POOL_GROUPS:GROUPS, :, 0:2],
+                )
+        quantize_w1(w_first[:], 0, P)
         w_high = keep.tile([P, 2 * P * PACK], BF16, name="w_high", tag="w_high", align_bytes=64)
         high_view = w_high[:].rearrange("p (e m j) -> p m j e", e=2, j=PACK)
         nc.scalar.copy(out=high_view[:, 0:GROUPS, :, :], in_=w_cols[:, 0:GROUPS, :, 2:4])

@@ -28,21 +28,20 @@ BANK = 512
 H_TILES = H // P
 M_TILES = N // P
 BLOCKS = V // P
-EARLY = 2
+OWN = 2
 R_BLOCKS = U // P
 HALF = H // 2
 GROUPS = HALF // PACK
-POOL_GROUPS = 40
-TERM_BUFFERS = 6
+TERM_BUFFERS = 4
 H_BANKS = {1: 4, 2: 6, 3: 4}
-HIGH_BANKS = (6, 7, 4, 5)
-EARLY_BACK_BANKS = (0, 3)
-LATE_BACK_BANK = 1
-LATE_PART_BANK = 2
-G_BANKS = (1, 6, 4, 5)
-G_LAST_BANK = 7
-ROOT_BANKS = (0, 2)
-ROOT_BACK_BANKS = (3, 4)
+TURN_BANKS = (2, 6)
+SHARED_BACK_BANK = 4
+OWN_BACK_BANK = 2
+G_BANKS = (0, 1, 6, 7)
+G_LAST_BANK = 2
+MERGE = (False, False)
+ROOT_BANKS = (4, 5)
+ROOT_BACK_BANKS = (3, 6)
 
 
 def tile_picked_hop2_gelu_e_kernel(
@@ -119,8 +118,9 @@ def tile_picked_hop2_gelu_e_kernel(
         w1_codes = keep.tile([P, H], U32, name="w1_codes", align_bytes=64)
         w1_bytes = keep.tile([P, H], U8, name="w1_bytes", align_bytes=64)
 
-        w_raw = keep.tile([P, PACK, H], F32, name="w_raw")
-        w_cols = w_raw[:].rearrange("p j (m f) -> p m j f", f=PACK)
+        w_wide = keep.tile([P, PACK, 2 * H], F32, name="w_wide", align_bytes=64)
+        w_raw = w_wide[:, :, 0:H]
+        w_cols = w_raw.rearrange("p j (m f) -> p m j f", f=PACK)
 
         def load_w1(half):
             cols = slice(half * HALF, (half + 1) * HALF)
@@ -132,11 +132,17 @@ def tile_picked_hop2_gelu_e_kernel(
             )
 
         load_w1(0)
-        pos = [load_list("pos%d" % d, src) for d, src in enumerate((pos1, pos2, pos3))]
         load_w1(1)
-        gates = keep.tile([P, D, V], F32, name="gates")
-        for d in range(D):
-            nc.sync.dma_start(gates[:, d, :], gate[d])
+        pos = [load_list("pos%d" % d, src) for d, src in enumerate((pos1, pos2, pos3))]
+        own_width = OWN * P
+        own_gates = keep.tile([P, D - 1, own_width], F32, name="own_gates")
+        nc.sync.dma_start(own_gates[:], gate[0 : D - 1, :, 0:own_width].rearrange("d p v -> p d v"))
+        last_gates = keep.tile([P, V], F32, name="last_gates")
+        nc.sync.dma_start(last_gates[:], gate[D - 1])
+        gate_cols = [keep.tile([P, BLOCKS - OWN], F32, name="gate_cols%d" % d) for d in range(D - 1)]
+        with nc.allow_non_contiguous_dma(reason="one gate a partition"):
+            for d in range(D - 1):
+                nc.sync.dma_start(gate_cols[d][:], gate[d, 0, own_width:V].rearrange("(b p) -> p b", p=P))
         w2_codes = keep.tile([P, N], U32, name="w2_codes", align_bytes=64)
         nc.sync.dma_start(w2_codes[:].bitcast(I32), w2_words[0].rearrange("p n t -> p (n t)").bitcast(I32))
         for quad in range(4):
@@ -149,16 +155,14 @@ def tile_picked_hop2_gelu_e_kernel(
         nc.sync.dma_start(gates2[:], gate2.rearrange("d p r -> p d r"))
 
         w_first = keep.tile([P, P * PACK], BF16, name="w_first", align_bytes=64)
-        nc.gpsimd.tensor_copy(
-            out=w_first[:].rearrange("p (m e j) -> p m e j", e=2, j=PACK)[:, 0:POOL_GROUPS, :, :],
-            in_=w_cols[:, 0:POOL_GROUPS, :, 0:2].rearrange("p m j e -> p m e j"),
-        )
+        first_view = w_first[:].rearrange("p (m j) -> p m j", j=PACK)
+        nc.gpsimd.tensor_copy(out=first_view[:, 0:GROUPS, :], in_=w_cols[:, 0:GROUPS, :, 0])
 
         x_codes = keep.tile([P, S], U32, name="x_codes", align_bytes=64)
         x_bytes = keep.tile([P, S], U8, name="x_bytes", align_bytes=64)
         h = [keep.tile([P, S], F32, name="h%d" % t) for t in range(H_TILES)]
 
-        def first_layer(t, c0, width, n):
+        def product(t, c0, width, n):
             acc = bank(n, [P, width])
             nc.tensor.matmul_mx(
                 out=acc[:],
@@ -169,56 +173,43 @@ def tile_picked_hop2_gelu_e_kernel(
                 start=True,
                 stop=True,
             )
-            nc.scalar.activation(h[t][:, c0 : c0 + width], acc[:], GELU)
+            return acc
+
+        def gelu(t, c0, acc):
+            nc.scalar.activation(h[t][:, c0 : c0 + acc.shape[1]], acc[:], GELU)
 
         woven = []
         for e0 in range(0, S, PIECE):
-            tile = keep.tile([P, PIECE * PACK], BF16, name="woven", tag="woven%d" % e0, align_bytes=64)
+            if e0 == S - PIECE:
+                nc.scalar.copy(out=first_view[:, GROUPS:P, :], in_=w_cols[:, GROUPS:P, :, 0])
+                tile = w_wide[:, 0, H : 2 * H].bitcast(BF16)
+            else:
+                tile = keep.tile([P, PIECE * PACK], BF16, name="woven", tag="woven%d" % e0, align_bytes=64)[:]
             nc.scalar.copy(
-                out=tile[:].bitcast(U32).rearrange("p (c u) -> p c u", u=2),
+                out=tile.bitcast(U32).rearrange("p (c u) -> p c u", u=2),
                 in_=words[:, :, e0 : e0 + PIECE].rearrange("p u c -> p c u"),
             )
             woven.append(tile)
-            if e0 == PIECE:
-                nc.scalar.copy(
-                    out=w_first[:].rearrange("p (m e j) -> p m j e", e=2, j=PACK)[:, POOL_GROUPS:GROUPS, :, :],
-                    in_=w_cols[:, POOL_GROUPS:GROUPS, :, 0:2],
-                )
-        quantize_w1(w_first[:], 0, P)
-        w_high = keep.tile([P, 2 * P * PACK], BF16, name="w_high", tag="w_high", align_bytes=64)
-        high_view = w_high[:].rearrange("p (e m j) -> p m j e", e=2, j=PACK)
-        nc.scalar.copy(out=high_view[:, 0:GROUPS, :, :], in_=w_cols[:, 0:GROUPS, :, 2:4])
+        w_rest = keep.tile([P, (H_TILES - 1) * P * PACK], BF16, name="w_rest", tag="w_rest", align_bytes=64)
+        rest_view = w_rest[:].rearrange("p (t m j) -> p m j t", t=H_TILES - 1, j=PACK)
         for n, e0 in enumerate(range(0, S, PIECE)):
             cols = slice(e0, e0 + PIECE)
-            nc.vector.quantize_mx(out=x_codes[:, cols].bitcast(FP8X4), scales=x_bytes[:, cols], in_=woven[n][:])
-            first_layer(0, e0, PIECE, n)
+            nc.vector.quantize_mx(out=x_codes[:, cols].bitcast(FP8X4), scales=x_bytes[:, cols], in_=woven[n])
+            if n == 0:
+                quantize_w1(w_first[:], 0, P)
+            gelu(0, e0, product(0, e0, PIECE, n))
 
-        nc.vector.tensor_copy(out=high_view[:, GROUPS:P, :, :], in_=w_cols[:, GROUPS:P, :, 2:4])
-        w_second = keep.tile([P, P * PACK], BF16, name="w_second", tag="woven%d" % (S - PIECE), align_bytes=64)
-        nc.vector.tensor_copy(
-            out=w_second[:].rearrange("p (m e j) -> p m j e", e=2, j=PACK), in_=w_cols[:, GROUPS:P, :, 0:2]
-        )
-        quantize_w1(w_high[:], 2 * P, 2 * P)
-        quantize_w1(w_second[:], P, P)
-        for t in range(1, H_TILES):
-            for half in range(S // BANK):
-                first_layer(t, half * BANK, BANK, H_BANKS[t] + half)
+        nc.vector.tensor_copy(out=rest_view, in_=w_cols[:, :, :, 1:PACK])
+        quantize_w1(w_rest[:, 0 : P * PACK], P, P)
+        quantize_w1(w_rest[:, P * PACK : 3 * P * PACK], 2 * P, 2 * P)
 
         g = [keep.tile([P, V], F32, name="g%d" % m) for m in range(M_TILES)]
-
-        def gather_term(term, t, d, v0, width):
-            nc.vector.tensor_tensor(
-                term, h[t][:].indirect(entries(pos[d], v0, width)), gates[:, d, v0 : v0 + width], MULT
-            )
 
         def turn(acc, term, b, d, last):
             nc.tensor.matmul(acc, term[:, block(b)], ident[:], start=(d == 0), stop=(d == last), is_transpose=True)
 
         z_codes = keep.tile([P, V], U32, name="z_codes", align_bytes=64)
         z_bytes = keep.tile([P, V], U8, name="z_bytes", align_bytes=64)
-
-        def quantize_z(values, b):
-            nc.vector.quantize_mx(out=z_codes[:, block(b)].bitcast(FP8X4), scales=z_bytes[:, block(b)], in_=values[:])
 
         def second_layer(acc, m, cols):
             nc.tensor.matmul_mx(
@@ -232,82 +223,107 @@ def tile_picked_hop2_gelu_e_kernel(
             )
             nc.scalar.activation(g[m][:, cols], acc[:], RELU)
 
-        early = range(EARLY)
-        late = range(EARLY, BLOCKS)
-        early_width = EARLY * P
-        late_width = V - early_width
+        own = range(OWN)
+        shared = range(BLOCKS - OWN)
+        shared_width = V - own_width
+        held = keep.tile([P, H_TILES * V + (D - 1) * own_width], F32, name="held", tag="w_rest", align_bytes=64)
+        third = held[:, 0 : H_TILES * V].rearrange("p (t v) -> p t v", t=H_TILES)
+        own_sums = [bank(b, [P, H_TILES, P]) for b in own]
+        turned = {}
 
-        def late_cols(b):
-            return block(b - EARLY)
+        def products(t):
+            return [product(t, c0, BANK, H_BANKS[t] + c0 // BANK) for c0 in range(0, S, BANK)]
 
-        low_sums = [bank(b, [P, 2, P]) for b in range(BLOCKS)]
-        first_terms = keep.tile([P, D * V], F32, name="first_terms", tag="w_high", align_bytes=64)
-        for t in range(2):
-            for d in range(D):
-                if t == 0:
-                    term = first_terms[:, d * V : (d + 1) * V]
-                else:
-                    term = picked.tile([P, V], F32, name="term")[:]
-                gather_term(term, t, d, 0, V)
-                for b in range(BLOCKS):
-                    turn(low_sums[b][:, t, :], term, b, d, D - 1)
-        low_words = []
-        for b in range(BLOCKS):
-            pairs = keep.tile([P, P, 2], BF16, name="low_pairs%d" % b)
-            nc.scalar.copy(out=pairs[:], in_=low_sums[b][:].rearrange("v t (m e) -> v (t m) e", e=2))
-            low_words.append(pairs[:].rearrange("v w e -> v (w e)").bitcast(F32))
-        early_back = [bank(EARLY_BACK_BANKS[b], [P, 2, P]) for b in early]
-        for b in early:
-            nc.tensor.transpose(early_back[b][:, 0, :], low_words[b], ident[:])
-        late_back = bank(LATE_BACK_BANK, [P, late_width])
-        for b in late:
-            nc.tensor.transpose(late_back[:, late_cols(b)], low_words[b], ident[:])
-        z_in = {}
-        for b in late:
-            z_in[b] = keep.tile([P, P * PACK], BF16, name="z_in%d" % b, align_bytes=64)
-            nc.scalar.copy(out=z_in[b][:].bitcast(F32)[:, 0 : 2 * P : 2], in_=late_back[:, late_cols(b)])
+        def gelus(t, accs):
+            for half, acc in enumerate(accs):
+                gelu(t, half * BANK, acc)
 
-        high_sums = [bank(HIGH_BANKS[b], [P, 2, P]) for b in range(BLOCKS)]
-        late_part = bank(LATE_PART_BANK, [P, 2, late_width])
-        high_pairs = [keep.tile([P, 2 * P], BF16, name="high_pairs%d" % b) for b in early]
-        for e in range(2):
+        def vector_terms(t):
             for d in range(D - 1):
-                term = keep.tile([P, V], F32, name="high_term", tag="high%d_%d" % (e, d))
-                gather_term(term[:], 2 + e, d, 0, V)
-                for b in range(BLOCKS):
-                    turn(high_sums[b][:, e, :], term, b, d, D - 1 if b < EARLY else D - 2)
-            for b in late:
-                two = keep.tile([P, P], F32, name="two_terms%d_%d" % (e, b))
-                nc.scalar.copy(out=two[:], in_=high_sums[b][:, e, :])
-                nc.tensor.transpose(late_part[:, e, late_cols(b)], two[:], ident[:])
-            term = keep.tile([P, early_width], F32, name="early_third%d" % e)
-            gather_term(term[:], 2 + e, D - 1, 0, early_width)
-            for b in early:
-                turn(high_sums[b][:, e, :], term, b, D - 1, D - 1)
-            for b in early:
-                nc.scalar.copy(out=high_pairs[b][:, e : 2 * P : 2], in_=high_sums[b][:, e, :])
-        for b in early:
-            nc.tensor.transpose(early_back[b][:, 1, :], high_pairs[b][:].bitcast(F32), ident[:])
-        for b in early:
-            z_in[b] = keep.tile([P, P * PACK], BF16, name="z_in%d" % b, align_bytes=64)
+                if t == 0:
+                    term = held[:, H_TILES * V + d * own_width : H_TILES * V + (d + 1) * own_width]
+                else:
+                    term = picked.tile([P, own_width], F32, name="term")[:]
+                nc.vector.tensor_tensor(term, h[t][:].indirect(entries(pos[d], 0, own_width)), own_gates[:, d, :], MULT)
+                for b in own:
+                    turn(own_sums[b][:, t, :], term, b, d, D - 1)
+            cuts = (0, own_width, V) if t == H_TILES - 1 else (0, V)
+            for v0, v1 in zip(cuts, cuts[1:]):
+                nc.vector.tensor_tensor(
+                    third[:, t, v0:v1], h[t][:].indirect(entries(pos[D - 1], v0, v1 - v0)), last_gates[:, v0:v1], MULT
+                )
+                if v0 == 0:
+                    for b in own:
+                        turn(own_sums[b][:, t, :], third[:, t, :], b, D - 1, D - 1)
+
+        def scalar_terms(t):
+            if t % 2 == 0:
+                for b in shared:
+                    turned[t // 2, b] = bank(TURN_BANKS[t // 2] + b, [P, D - 1, 2, P])
+            for d in range(D - 1):
+                raw = keep.tile([P, shared_width], F32, name="raw%d_%d" % (t, d))
+                nc.scalar.activation(raw[:], h[t][:].indirect(entries(pos[d], own_width, shared_width)), COPY)
+                for b in shared:
+                    nc.tensor.transpose(turned[t // 2, b][:, d, t % 2, :], raw[:, block(b)], ident[:])
+
+        second, next_tile = products(1), products(2)
+        scalar_terms(0)
+        gelus(1, second)
+        gelus(2, next_tile)
+        last = products(3)
+        vector_terms(0)
+        scalar_terms(1)
+        gelus(3, last)
+        vector_terms(1)
+        scalar_terms(2)
+        vector_terms(2)
+        scalar_terms(3)
+        vector_terms(3)
+
+        shared_back = [bank(SHARED_BACK_BANK + b, [P, H_TILES, P]) for b in shared]
+        for pair in range(2):
+            for b in shared:
+                first = keep.tile([P, 2, P], F32, name="first%d_%d" % (pair, b))
+                nc.scalar.activation(first[:], turned[pair, b][:, 0, :, :], COPY, scale=gate_cols[0][:, b : b + 1])
+                if MERGE[pair]:
+                    both = keep.tile([P, 2, P], F32, name="both%d_%d" % (pair, b))
+                    nc.vector.scalar_tensor_tensor(
+                        both[:], turned[pair, b][:, 1, :, :], gate_cols[1][:, b : b + 1], first[:], MULT, ADD
+                    )
+                    for e in range(2):
+                        nc.tensor.transpose(shared_back[b][:, 2 * pair + e, :], both[:, e, :], ident[:])
+                else:
+                    second = keep.tile([P, 2, P], F32, name="second%d_%d" % (pair, b))
+                    nc.scalar.activation(second[:], turned[pair, b][:, 1, :, :], COPY, scale=gate_cols[1][:, b : b + 1])
+                    for e in range(2):
+                        for d, gated in enumerate((first, second)):
+                            turn(shared_back[b][:, 2 * pair + e, :], gated[:, e, :], 0, d, 1)
+
+        z_in = [keep.tile([P, P * PACK], BF16, name="z_in%d" % b, align_bytes=64) for b in range(BLOCKS)]
+        own_back = []
+        for b in own:
+            pairs = keep.tile([P, 2, P, 2], BF16, name="pairs%d" % b)
+            nc.scalar.copy(out=pairs[:], in_=own_sums[b][:].rearrange("v (u e) p -> v u p e", e=2))
+            own_back.append(bank(OWN_BACK_BANK + b, [P, 2, P]))
+            for u in range(2):
+                nc.tensor.transpose(
+                    own_back[b][:, u, :], pairs[:, u, :, :].rearrange("v p e -> v (p e)").bitcast(F32), ident[:]
+                )
+        for b in own:
             nc.scalar.copy(
                 out=z_in[b][:].bitcast(F32).rearrange("p (v u) -> p v u", u=2),
-                in_=early_back[b][:].rearrange("p u v -> p v u"),
+                in_=own_back[b][:].rearrange("p u v -> p v u"),
             )
 
-        late_third = keep.tile([P, 2, late_width], F32, name="late_third", tag="high1_0")
-        gather_term(late_third[:, 0, :], 2, D - 1, early_width, late_width)
-        for b in late:
-            gather_term(late_third[:, 1, late_cols(b)], 3, D - 1, b * P, P)
-        for b in late:
+        for b in shared:
             nc.vector.tensor_tensor(
-                z_in[b][:].rearrange("p (c i j) -> p c j i", i=LINE, j=PACK)[:, :, 2:4, :],
-                late_part[:, :, late_cols(b)].rearrange("p e (c i) -> p c e i", i=LINE),
-                late_third[:, :, late_cols(b)].rearrange("p e (c i) -> p c e i", i=LINE),
+                z_in[OWN + b][:].rearrange("p (c i j) -> p c j i", i=LINE, j=PACK),
+                shared_back[b][:].rearrange("p j (c i) -> p c j i", i=LINE),
+                third[:, :, block(OWN + b)].rearrange("p j (c i) -> p c j i", i=LINE),
                 ADD,
             )
-        for b in list(late) + list(early):
-            quantize_z(z_in[b], b)
+        for b in list(range(OWN, BLOCKS)) + list(own):
+            nc.vector.quantize_mx(out=z_codes[:, block(b)].bitcast(FP8X4), scales=z_bytes[:, block(b)], in_=z_in[b][:])
             second_layer(bank(G_BANKS[b], [P, P]), 0, block(b))
         second_layer(bank(G_LAST_BANK, [P, V]), 1, slice(0, V))
 

@@ -30,8 +30,6 @@ M_TILES = N // P
 BLOCKS = V // P
 OWN = 2
 R_BLOCKS = U // P
-HALF = H // 2
-GROUPS = HALF // PACK
 TERM_BUFFERS = 4
 H_BANKS = {1: 4, 2: 6, 3: 4}
 TURN_BANKS = (2, 6)
@@ -123,8 +121,8 @@ def tile_picked_hop2_gelu_e_kernel(
         w_cols = w_raw.rearrange("p j (m f) -> p m j f", f=PACK)
 
         def load_w1(half):
-            cols = slice(half * HALF, (half + 1) * HALF)
-            nc.sync.dma_start(w_raw[:, :, cols], w_rows[:, :, cols])
+            rows = slice(2 * half, 2 * half + 2)
+            nc.sync.dma_start(w_raw[:, rows, :], w_rows[:, rows, :])
 
         def quantize_w1(grouped, c0, width):
             nc.vector.quantize_mx(
@@ -156,7 +154,7 @@ def tile_picked_hop2_gelu_e_kernel(
 
         w_first = keep.tile([P, P * PACK], BF16, name="w_first", align_bytes=64)
         first_view = w_first[:].rearrange("p (m j) -> p m j", j=PACK)
-        nc.gpsimd.tensor_copy(out=first_view[:, 0:GROUPS, :], in_=w_cols[:, 0:GROUPS, :, 0])
+        nc.gpsimd.tensor_copy(out=first_view[:, :, 0:2], in_=w_cols[:, :, 0:2, 0])
 
         x_codes = keep.tile([P, S], U32, name="x_codes", align_bytes=64)
         x_bytes = keep.tile([P, S], U8, name="x_bytes", align_bytes=64)
@@ -181,8 +179,8 @@ def tile_picked_hop2_gelu_e_kernel(
         woven = []
         for e0 in range(0, S, PIECE):
             if e0 == S - PIECE:
-                nc.scalar.copy(out=first_view[:, GROUPS:P, :], in_=w_cols[:, GROUPS:P, :, 0])
-                tile = w_wide[:, 0, H : 2 * H].bitcast(BF16)
+                nc.scalar.copy(out=first_view[:, :, 2:PACK], in_=w_cols[:, :, 2:PACK, 0])
+                tile = w_wide[:, 2, H : 2 * H].bitcast(BF16)
             else:
                 tile = keep.tile([P, PIECE * PACK], BF16, name="woven", tag="woven%d" % e0, align_bytes=64)[:]
             nc.scalar.copy(
@@ -334,6 +332,9 @@ def tile_picked_hop2_gelu_e_kernel(
             )
             return term
 
+        plain = keep.tile([P, D, U], F32, name="plain")
+        for d in range(D):
+            nc.scalar.activation(plain[:, d, :], g[1][:].indirect(nxt[d][:]), COPY)
         root_sums = [bank(ROOT_BANKS[b], [P, P]) for b in range(R_BLOCKS)]
         for d in range(D):
             term = root_term(0, d, 0, U)
@@ -348,12 +349,13 @@ def tile_picked_hop2_gelu_e_kernel(
             nc.scalar.copy(out=first_rows[:, block(b)], in_=back[:])
         nc.scalar.dma_start(out[0:P, :], first_rows[:])
 
-        terms = [root_term(1, d, 0, U) for d in range(D - 1)]
+        terms = keep.tile([P, D, U], F32, name="terms")
+        nc.vector.tensor_tensor(terms[:, 0:2, :], plain[:, 0:2, :], gates2[:, 0:2, :], MULT)
+        nc.vector.tensor_tensor(terms[:, 2, :], plain[:, 2, :], gates2[:, 2, :], MULT)
         root_part = keep.tile([P, U], F32, name="root_part")
-        thirds = [root_term(1, D - 1, 0, P)]
-        nc.vector.tensor_tensor(root_part[:], terms[0][:], terms[1][:], ADD)
-        thirds.append(root_term(1, D - 1, P, P))
+        for b in range(R_BLOCKS):
+            nc.vector.tensor_tensor(root_part[:, block(b)], terms[:, 0, block(b)], terms[:, 1, block(b)], ADD)
         for b in range(R_BLOCKS):
             last_rows = keep.tile([P, P], F32, name="last_rows%d" % b)
-            nc.vector.tensor_tensor(last_rows[:], root_part[:, block(b)], thirds[b][:], ADD)
+            nc.vector.tensor_tensor(last_rows[:], root_part[:, block(b)], terms[:, 2, block(b)], ADD)
             nc.sync.dma_start(out[P : 2 * P, block(b)], last_rows[:])

@@ -36,10 +36,10 @@ TURN_BANKS = (2, 6)
 SHARED_BACK_BANK = 4
 OWN_BACK_BANK = 2
 G_BANKS = (0, 1, 6, 7)
-G_LAST_BANK = 2
+G_SECOND_BANKS = (4, 5)
 MERGE = (False, False)
-ROOT_BANKS = (4, 5)
-ROOT_BACK_BANKS = (3, 6)
+ROOT_BANKS = (2, 3)
+ROOT_BACK_BANKS = (6, 7)
 
 
 def tile_picked_hop2_gelu_e_kernel(
@@ -188,8 +188,6 @@ def tile_picked_hop2_gelu_e_kernel(
                 in_=words[:, :, e0 : e0 + PIECE].rearrange("p u c -> p c u"),
             )
             woven.append(tile)
-        w_rest = keep.tile([P, (H_TILES - 1) * P * PACK], BF16, name="w_rest", tag="w_rest", align_bytes=64)
-        rest_view = w_rest[:].rearrange("p (t m j) -> p m j t", t=H_TILES - 1, j=PACK)
         for n, e0 in enumerate(range(0, S, PIECE)):
             cols = slice(e0, e0 + PIECE)
             nc.vector.quantize_mx(out=x_codes[:, cols].bitcast(FP8X4), scales=x_bytes[:, cols], in_=woven[n])
@@ -197,9 +195,14 @@ def tile_picked_hop2_gelu_e_kernel(
                 quantize_w1(w_first[:], 0, P)
             gelu(0, e0, product(0, e0, PIECE, n))
 
-        nc.vector.tensor_copy(out=rest_view, in_=w_cols[:, :, :, 1:PACK])
-        quantize_w1(w_rest[:, 0 : P * PACK], P, P)
-        quantize_w1(w_rest[:, P * PACK : 3 * P * PACK], 2 * P, 2 * P)
+        w_second = keep.tile([P, P * PACK], BF16, name="w_second", align_bytes=64)
+        nc.vector.tensor_copy(out=w_second[:].rearrange("p (m j) -> p m j", j=PACK), in_=w_cols[:, :, :, 1])
+        w_high = keep.tile([P, 2 * P * PACK], BF16, name="w_high", tag="w_high", align_bytes=64)
+        nc.vector.tensor_copy(
+            out=w_high[:].rearrange("p (e m j) -> p m j e", e=2, j=PACK), in_=w_cols[:, :, :, 2:PACK]
+        )
+        quantize_w1(w_second[:], P, P)
+        quantize_w1(w_high[:], 2 * P, 2 * P)
 
         g = [keep.tile([P, V], F32, name="g%d" % m) for m in range(M_TILES)]
 
@@ -211,7 +214,7 @@ def tile_picked_hop2_gelu_e_kernel(
 
         def second_layer(acc, m, cols):
             nc.tensor.matmul_mx(
-                out=acc[:],
+                out=acc,
                 lhsT=w2_codes[:, block(m)].bitcast(FP8X4),
                 lhsT_scale=w2_bytes[:, block(m)],
                 rhs=z_codes[:, cols].bitcast(FP8X4),
@@ -219,12 +222,11 @@ def tile_picked_hop2_gelu_e_kernel(
                 start=True,
                 stop=True,
             )
-            nc.scalar.activation(g[m][:, cols], acc[:], RELU)
 
         own = range(OWN)
         shared = range(BLOCKS - OWN)
         shared_width = V - own_width
-        held = keep.tile([P, H_TILES * V + (D - 1) * own_width], F32, name="held", tag="w_rest", align_bytes=64)
+        held = keep.tile([P, H_TILES * V + (D - 1) * own_width], F32, name="held", tag="w_second", align_bytes=64)
         third = held[:, 0 : H_TILES * V].rearrange("p (t v) -> p t v", t=H_TILES)
         own_sums = [bank(b, [P, H_TILES, P]) for b in own]
         turned = {}
@@ -298,16 +300,17 @@ def tile_picked_hop2_gelu_e_kernel(
                             turn(shared_back[b][:, 2 * pair + e, :], gated[:, e, :], 0, d, 1)
 
         z_in = [keep.tile([P, P * PACK], BF16, name="z_in%d" % b, align_bytes=64) for b in range(BLOCKS)]
-        own_back = []
-        for b in own:
+        own_back = {}
+        for b in reversed(own):
             pairs = keep.tile([P, 2, P, 2], BF16, name="pairs%d" % b)
-            nc.scalar.copy(out=pairs[:], in_=own_sums[b][:].rearrange("v (u e) p -> v u p e", e=2))
-            own_back.append(bank(OWN_BACK_BANK + b, [P, 2, P]))
+            rounding = nc.vector.tensor_copy if b == OWN - 1 else nc.scalar.copy
+            rounding(out=pairs[:], in_=own_sums[b][:].rearrange("v (u e) p -> v u p e", e=2))
+            own_back[b] = bank(OWN_BACK_BANK + b, [P, 2, P])
             for u in range(2):
                 nc.tensor.transpose(
                     own_back[b][:, u, :], pairs[:, u, :, :].rearrange("v p e -> v (p e)").bitcast(F32), ident[:]
                 )
-        for b in own:
+        for b in reversed(own):
             nc.scalar.copy(
                 out=z_in[b][:].bitcast(F32).rearrange("p (v u) -> p v u", u=2),
                 in_=own_back[b][:].rearrange("p u v -> p v u"),
@@ -320,10 +323,20 @@ def tile_picked_hop2_gelu_e_kernel(
                 third[:, :, block(OWN + b)].rearrange("p j (c i) -> p c j i", i=LINE),
                 ADD,
             )
-        for b in list(range(OWN, BLOCKS)) + list(own):
+        early_g = bank(G_SECOND_BANKS[0], [P, V])
+        for b in (2, 3, 1, 0):
             nc.vector.quantize_mx(out=z_codes[:, block(b)].bitcast(FP8X4), scales=z_bytes[:, block(b)], in_=z_in[b][:])
-            second_layer(bank(G_BANKS[b], [P, P]), 0, block(b))
-        second_layer(bank(G_LAST_BANK, [P, V]), 1, slice(0, V))
+            acc = bank(G_BANKS[b], [P, P])
+            second_layer(acc[:], 0, block(b))
+            nc.scalar.activation(g[0][:, block(b)], acc[:], RELU)
+            if b == 3:
+                second_layer(early_g[:, own_width:V], 1, slice(own_width, V))
+            if b == 1:
+                second_layer(early_g[:, block(b)], 1, block(b))
+        last_g = bank(G_SECOND_BANKS[1], [P, P])
+        second_layer(last_g[:], 1, block(0))
+        nc.scalar.activation(g[1][:, block(0)], last_g[:], RELU)
+        nc.vector.tensor_scalar_max(g[1][:, P:V], early_g[:, P:V], 0.0)
 
         def root_term(m, d, r0, width):
             term = keep.tile([P, width], F32, name="root_term%d_%d_%d" % (m, d, r0))
@@ -332,30 +345,41 @@ def tile_picked_hop2_gelu_e_kernel(
             )
             return term
 
-        plain = keep.tile([P, D, U], F32, name="plain")
-        for d in range(D):
-            nc.scalar.activation(plain[:, d, :], g[1][:].indirect(nxt[d][:]), COPY)
+        def plain_term(dst, m, d):
+            nc.scalar.activation(dst, g[m][:].indirect(nxt[d][:]), COPY)
+
+        plain_first = keep.tile([P, U], F32, name="plain_first")
+        plain_term(plain_first[:], 0, D - 1)
+        plain = keep.tile([P, D - 1, U], F32, name="plain")
+        for d in range(D - 1):
+            plain_term(plain[:, d, :], 1, d)
+
         root_sums = [bank(ROOT_BANKS[b], [P, P]) for b in range(R_BLOCKS)]
         for d in range(D):
-            term = root_term(0, d, 0, U)
+            if d < D - 1:
+                term = root_term(0, d, 0, U)
+            else:
+                term = keep.tile([P, U], F32, name="first_third")
+                nc.vector.tensor_tensor(term[:], plain_first[:], gates2[:, d, :], MULT)
             for b in range(R_BLOCKS):
                 turn(root_sums[b][:], term, b, d, D - 1)
-        first_rows = keep.tile([P, U], F32, name="first_rows")
         for b in range(R_BLOCKS):
             summed = keep.tile([P, P], F32, name="summed%d" % b)
             nc.scalar.copy(out=summed[:], in_=root_sums[b][:])
             back = bank(ROOT_BACK_BANKS[b], [P, P])
             nc.tensor.transpose(back[:], summed[:], ident[:])
-            nc.scalar.copy(out=first_rows[:, block(b)], in_=back[:])
-        nc.scalar.dma_start(out[0:P, :], first_rows[:])
+            first_rows = keep.tile([P, P], F32, name="first_rows%d" % b)
+            nc.scalar.copy(out=first_rows[:], in_=back[:])
+            nc.scalar.dma_start(out[0:P, block(b)], first_rows[:])
 
-        terms = keep.tile([P, D, U], F32, name="terms")
-        nc.vector.tensor_tensor(terms[:, 0:2, :], plain[:, 0:2, :], gates2[:, 0:2, :], MULT)
-        nc.vector.tensor_tensor(terms[:, 2, :], plain[:, 2, :], gates2[:, 2, :], MULT)
+        last_third = root_term(1, D - 1, 0, U)
+        terms = keep.tile([P, D - 1, U], F32, name="terms")
+        for d in range(D - 1):
+            nc.vector.tensor_tensor(terms[:, d, :], plain[:, d, :], gates2[:, d, :], MULT)
         root_part = keep.tile([P, U], F32, name="root_part")
         for b in range(R_BLOCKS):
-            nc.vector.tensor_tensor(root_part[:, block(b)], terms[:, 0, block(b)], terms[:, 1, block(b)], ADD)
+            nc.vector.tensor_tensor(root_part[:, block(b)], terms[:, 0, block(b)], last_third[:, block(b)], ADD)
         for b in range(R_BLOCKS):
             last_rows = keep.tile([P, P], F32, name="last_rows%d" % b)
-            nc.vector.tensor_tensor(last_rows[:], root_part[:, block(b)], terms[:, 2, block(b)], ADD)
+            nc.vector.tensor_tensor(last_rows[:], root_part[:, block(b)], terms[:, 1, block(b)], ADD)
             nc.sync.dma_start(out[P : 2 * P, block(b)], last_rows[:])

@@ -37,7 +37,7 @@ SHARED_BACK_BANK = 4
 OWN_BACK_BANK = 2
 G_BANKS = (0, 1, 6, 7)
 G_SECOND_BANKS = (4, 5)
-MERGE = (False, False)
+MERGE = (False, True)
 ROOT_BANKS = (2, 3)
 ROOT_BACK_BANKS = (6, 7)
 
@@ -303,8 +303,7 @@ def tile_picked_hop2_gelu_e_kernel(
         own_back = {}
         for b in reversed(own):
             pairs = keep.tile([P, 2, P, 2], BF16, name="pairs%d" % b)
-            rounding = nc.vector.tensor_copy if b == OWN - 1 else nc.scalar.copy
-            rounding(out=pairs[:], in_=own_sums[b][:].rearrange("v (u e) p -> v u p e", e=2))
+            nc.scalar.copy(out=pairs[:], in_=own_sums[b][:].rearrange("v (u e) p -> v u p e", e=2))
             own_back[b] = bank(OWN_BACK_BANK + b, [P, 2, P])
             for u in range(2):
                 nc.tensor.transpose(

@@ -30,8 +30,9 @@ M_TILES = N // P
 BLOCKS = V // P
 OWN = 2
 R_BLOCKS = U // P
+VECTOR_GROUPS = (72, 32)
 TERM_BUFFERS = 4
-H_BANKS = {1: 4, 2: 6, 3: 4}
+H_BANKS = {1: (2, 4), 2: (6, 7), 3: (5, 4)}
 TURN_BANKS = (2, 6)
 SHARED_BACK_BANK = 4
 OWN_BACK_BANK = 2
@@ -86,51 +87,49 @@ def tile_picked_hop2_gelu_e_kernel(
         for j in (0, 1, 3):
             planes[j] = load_plane(j)
 
-        word_row = keep.tile([P, 2 * S], U32, name="word_row")
-        words = word_row[:].rearrange("p (u c) -> p u c", u=2)
-        halves = word_row[:].bitcast(BF16)
         rest = S - PIECE
-
-        def half_words(j, e0, count):
-            first = 2 * (j // 2 * S + e0)
-            return halves[:, first + j % 2 : first + 2 * count : 2]
+        word_row = keep.tile([P, 2 * rest], U32, name="word_row")
+        halves = word_row[:].bitcast(BF16)
+        staged = keep.tile([P, PACK, PIECE], BF16, name="staged")
+        first_woven = keep.tile([P, PIECE, PACK], BF16, name="first_woven", align_bytes=64)
 
         def gather_half(j, e0, count):
-            nc.vector.tensor_copy(out=half_words(j, e0, count), in_=planes[j][:].indirect(entries(offs_t, e0, count)))
-
-        gather_half(2, 0, S)
-        gather_half(0, 0, rest)
-        gather_half(1, 0, rest)
-        rounded = [keep.tile([P, T], BF16, name="rounded%d" % j) for j in range(2)]
-        nc.gpsimd.tensor_copy(out=rounded[0][:], in_=planes[0][:])
-        nc.gpsimd.tensor_copy(out=rounded[1][:, 0 : T // 2], in_=planes[1][:, 0 : T // 2])
-        nc.scalar.copy(out=rounded[1][:, T // 2 : T], in_=planes[1][:, T // 2 : T])
-        for j in range(2):
-            nc.scalar.activation(
-                half_words(j, rest, PIECE), rounded[j][:].indirect(entries(offs_t, rest, PIECE)), COPY
+            first = 2 * (j // 2 * rest + e0 - PIECE)
+            nc.vector.tensor_copy(
+                out=halves[:, first + j % 2 : first + 2 * count : 2],
+                in_=planes[j][:].indirect(entries(offs_t, e0, count)),
             )
-        for e0 in range(0, S, PIECE):
+
+        def gather_first(j):
+            nc.scalar.activation(staged[:, j, :], planes[j][:].indirect(entries(offs_t, 0, PIECE)), COPY)
+
+        def place_first(j0, j1):
+            nc.scalar.copy(out=first_woven[:, :, j0:j1], in_=staged[:, j0:j1, :].rearrange("p j c -> p c j"))
+
+        for j in (2, 0, 1):
+            gather_half(j, PIECE, rest)
+            gather_first(j)
+        place_first(0, PACK - 1)
+        gather_first(PACK - 1)
+        place_first(PACK - 1, PACK)
+        for e0 in range(PIECE, S, PIECE):
             gather_half(3, e0, PIECE)
 
         w_rows = w1.rearrange("(p j) c -> p j c", j=PACK)
-        w1_codes = keep.tile([P, H], U32, name="w1_codes", align_bytes=64)
+        w1_codes = [keep.tile([P, 2 * P], U32, name="w1_codes", align_bytes=64)]
         w1_bytes = keep.tile([P, H], U8, name="w1_bytes", align_bytes=64)
 
-        w_wide = keep.tile([P, PACK, 2 * H], F32, name="w_wide", align_bytes=64)
-        w_raw = w_wide[:, :, 0:H]
-        w_cols = w_raw.rearrange("p j (m f) -> p m j f", f=PACK)
-
-        def load_w1(half):
-            rows = slice(2 * half, 2 * half + 2)
-            nc.sync.dma_start(w_raw[:, rows, :], w_rows[:, rows, :])
+        w_raw = keep.tile([P, PACK, H], F32, name="w_raw")
+        w_cols = w_raw[:].rearrange("p j (m f) -> p m j f", f=PACK)
 
         def quantize_w1(grouped, c0, width):
             nc.vector.quantize_mx(
-                out=w1_codes[:, c0 : c0 + width].bitcast(FP8X4), scales=w1_bytes[:, c0 : c0 + width], in_=grouped
+                out=w1_codes[c0 // (2 * P)][:, c0 % (2 * P) : c0 % (2 * P) + width].bitcast(FP8X4),
+                scales=w1_bytes[:, c0 : c0 + width],
+                in_=grouped,
             )
 
-        load_w1(0)
-        load_w1(1)
+        nc.sync.dma_start(w_raw[:], w_rows)
         pos = [load_list("pos%d" % d, src) for d, src in enumerate((pos1, pos2, pos3))]
         own_width = OWN * P
         own_gates = keep.tile([P, D - 1, own_width], F32, name="own_gates")
@@ -152,11 +151,14 @@ def tile_picked_hop2_gelu_e_kernel(
         gates2 = keep.tile([P, D, U], F32, name="gates2")
         nc.sync.dma_start(gates2[:], gate2.rearrange("d p r -> p d r"))
 
-        w_first = keep.tile([P, P * PACK], BF16, name="w_first", align_bytes=64)
-        first_view = w_first[:].rearrange("p (m j) -> p m j", j=PACK)
-        nc.gpsimd.tensor_copy(out=first_view[:, :, 0:2], in_=w_cols[:, :, 0:2, 0])
+        w_pairs = [keep.tile([P, 2, P, PACK], BF16, name="w_pair", tag="w_pair%d" % u, align_bytes=64) for u in range(2)]
 
-        x_codes = keep.tile([P, S], U32, name="x_codes", align_bytes=64)
+        def round_w1(copy, u, groups):
+            copy(
+                out=w_pairs[u][:, :, groups, :].rearrange("p e m j -> p m j e"),
+                in_=w_cols[:, groups, :, 2 * u : 2 * u + 2],
+            )
+
         x_bytes = keep.tile([P, S], U8, name="x_bytes", align_bytes=64)
         h = [keep.tile([P, S], F32, name="h%d" % t) for t in range(H_TILES)]
 
@@ -164,9 +166,9 @@ def tile_picked_hop2_gelu_e_kernel(
             acc = bank(n, [P, width])
             nc.tensor.matmul_mx(
                 out=acc[:],
-                lhsT=w1_codes[:, block(t)].bitcast(FP8X4),
+                lhsT=w1_codes[t // 2][:, block(t % 2)].bitcast(FP8X4),
                 lhsT_scale=w1_bytes[:, block(t)],
-                rhs=x_codes[:, c0 : c0 + width].bitcast(FP8X4),
+                rhs=x_codes[c0 // BANK][:, c0 % BANK : c0 % BANK + width].bitcast(FP8X4),
                 rhs_scale=x_bytes[:, c0 : c0 + width],
                 start=True,
                 stop=True,
@@ -176,33 +178,33 @@ def tile_picked_hop2_gelu_e_kernel(
         def gelu(t, c0, acc):
             nc.scalar.activation(h[t][:, c0 : c0 + acc.shape[1]], acc[:], GELU)
 
-        woven = []
-        for e0 in range(0, S, PIECE):
-            if e0 == S - PIECE:
-                nc.scalar.copy(out=first_view[:, :, 2:PACK], in_=w_cols[:, :, 2:PACK, 0])
-                tile = w_wide[:, 2, H : 2 * H].bitcast(BF16)
-            else:
-                tile = keep.tile([P, PIECE * PACK], BF16, name="woven", tag="woven%d" % e0, align_bytes=64)[:]
-            nc.scalar.copy(
+        woven = [first_woven[:].rearrange("p c j -> p (c j)")]
+        for e0 in range(0, rest, PIECE):
+            tile = keep.tile([P, PIECE * PACK], BF16, name="woven", tag="woven%d" % e0, align_bytes=64)[:]
+            weave = nc.scalar.copy if e0 == rest - PIECE else nc.gpsimd.tensor_copy
+            weave(
                 out=tile.bitcast(U32).rearrange("p (c u) -> p c u", u=2),
-                in_=words[:, :, e0 : e0 + PIECE].rearrange("p u c -> p c u"),
+                in_=word_row[:].rearrange("p (u c) -> p c u", u=2)[:, e0 : e0 + PIECE, :],
             )
             woven.append(tile)
+        for u in range(2):
+            round_w1(nc.vector.tensor_copy, u, slice(0, VECTOR_GROUPS[u]))
+            round_w1(nc.scalar.copy, u, slice(VECTOR_GROUPS[u], P))
+        for e in range(2):
+            quantize_w1(w_pairs[0][:, e, :, :].rearrange("p m j -> p (m j)"), e * P, P)
+        x_codes = [
+            keep.tile([P, BANK], U32, name="x_codes", tag=tag, align_bytes=64) for tag in ("x_codes", "w_pair0")
+        ]
         for n, e0 in enumerate(range(0, S, PIECE)):
-            cols = slice(e0, e0 + PIECE)
-            nc.vector.quantize_mx(out=x_codes[:, cols].bitcast(FP8X4), scales=x_bytes[:, cols], in_=woven[n])
-            if n == 0:
-                quantize_w1(w_first[:], 0, P)
+            nc.vector.quantize_mx(
+                out=x_codes[e0 // BANK][:, e0 % BANK : e0 % BANK + PIECE].bitcast(FP8X4),
+                scales=x_bytes[:, e0 : e0 + PIECE],
+                in_=woven[n],
+            )
             gelu(0, e0, product(0, e0, PIECE, n))
 
-        w_second = keep.tile([P, P * PACK], BF16, name="w_second", align_bytes=64)
-        nc.vector.tensor_copy(out=w_second[:].rearrange("p (m j) -> p m j", j=PACK), in_=w_cols[:, :, :, 1])
-        w_high = keep.tile([P, 2 * P * PACK], BF16, name="w_high", tag="w_high", align_bytes=64)
-        nc.vector.tensor_copy(
-            out=w_high[:].rearrange("p (e m j) -> p m j e", e=2, j=PACK), in_=w_cols[:, :, :, 2:PACK]
-        )
-        quantize_w1(w_second[:], P, P)
-        quantize_w1(w_high[:], 2 * P, 2 * P)
+        w1_codes.append(keep.tile([P, 2 * P], U32, name="w1_codes", tag="woven%d" % (rest - PIECE), align_bytes=64))
+        quantize_w1(w_pairs[1][:].rearrange("p e m j -> p (e m j)"), 2 * P, 2 * P)
 
         g = [keep.tile([P, V], F32, name="g%d" % m) for m in range(M_TILES)]
 
@@ -226,13 +228,13 @@ def tile_picked_hop2_gelu_e_kernel(
         own = range(OWN)
         shared = range(BLOCKS - OWN)
         shared_width = V - own_width
-        held = keep.tile([P, H_TILES * V + (D - 1) * own_width], F32, name="held", tag="w_second", align_bytes=64)
+        held = keep.tile([P, H_TILES * V + (D - 1) * own_width], F32, name="held", tag="w_pair1", align_bytes=64)
         third = held[:, 0 : H_TILES * V].rearrange("p (t v) -> p t v", t=H_TILES)
         own_sums = [bank(b, [P, H_TILES, P]) for b in own]
         turned = {}
 
         def products(t):
-            return [product(t, c0, BANK, H_BANKS[t] + c0 // BANK) for c0 in range(0, S, BANK)]
+            return [product(t, c0, BANK, H_BANKS[t][c0 // BANK]) for c0 in range(0, S, BANK)]
 
         def gelus(t, accs):
             for half, acc in enumerate(accs):

@@ -151,7 +151,9 @@ def tile_picked_hop2_gelu_e_kernel(
         gates2 = keep.tile([P, D, U], F32, name="gates2")
         nc.sync.dma_start(gates2[:], gate2.rearrange("d p r -> p d r"))
 
-        w_pairs = [keep.tile([P, 2, P, PACK], BF16, name="w_pair", tag="w_pair%d" % u, align_bytes=64) for u in range(2)]
+        low_rows = keep.tile([P, 6, P * PACK], BF16, name="low_rows", align_bytes=64)
+        high_rows = keep.tile([P, 2, P * PACK], BF16, name="high_rows", tag="w_pair1", align_bytes=64)
+        w_pairs = [rows.rearrange("p e (m j) -> p e m j", j=PACK) for rows in (low_rows[:, 0:6:5, :], high_rows[:])]
 
         def round_w1(copy, u, groups):
             copy(
@@ -180,7 +182,11 @@ def tile_picked_hop2_gelu_e_kernel(
 
         woven = [first_woven[:].rearrange("p c j -> p (c j)")]
         for e0 in range(0, rest, PIECE):
-            tile = keep.tile([P, PIECE * PACK], BF16, name="woven", tag="woven%d" % e0, align_bytes=64)[:]
+            if e0 == 0:
+                tile = keep.tile([P, PIECE * PACK], BF16, name="woven", align_bytes=64)[:]
+            else:
+                row = 2 * e0 // PIECE - 1
+                tile = low_rows[:, row : row + 2, :].rearrange("p r c -> p (r c)")
             weave = nc.scalar.copy if e0 == rest - PIECE else nc.gpsimd.tensor_copy
             weave(
                 out=tile.bitcast(U32).rearrange("p (c u) -> p c u", u=2),
@@ -190,11 +196,8 @@ def tile_picked_hop2_gelu_e_kernel(
         for u in range(2):
             round_w1(nc.vector.tensor_copy, u, slice(0, VECTOR_GROUPS[u]))
             round_w1(nc.scalar.copy, u, slice(VECTOR_GROUPS[u], P))
-        for e in range(2):
-            quantize_w1(w_pairs[0][:, e, :, :].rearrange("p m j -> p (m j)"), e * P, P)
-        x_codes = [
-            keep.tile([P, BANK], U32, name="x_codes", tag=tag, align_bytes=64) for tag in ("x_codes", "w_pair0")
-        ]
+        quantize_w1(low_rows[:, 0, :], 0, P)
+        x_codes = [keep.tile([P, BANK], U32, name="x_codes%d" % half, align_bytes=64) for half in range(2)]
         for n, e0 in enumerate(range(0, S, PIECE)):
             nc.vector.quantize_mx(
                 out=x_codes[e0 // BANK][:, e0 % BANK : e0 % BANK + PIECE].bitcast(FP8X4),
@@ -203,8 +206,9 @@ def tile_picked_hop2_gelu_e_kernel(
             )
             gelu(0, e0, product(0, e0, PIECE, n))
 
-        w1_codes.append(keep.tile([P, 2 * P], U32, name="w1_codes", tag="woven%d" % (rest - PIECE), align_bytes=64))
-        quantize_w1(w_pairs[1][:].rearrange("p e m j -> p (e m j)"), 2 * P, 2 * P)
+        quantize_w1(low_rows[:, 5, :], P, P)
+        w1_codes.append(keep.tile([P, 2 * P], U32, name="high_codes", align_bytes=64))
+        quantize_w1(high_rows[:].rearrange("p e c -> p (e c)"), 2 * P, 2 * P)
 
         g = [keep.tile([P, V], F32, name="g%d" % m) for m in range(M_TILES)]
 

@@ -31,16 +31,14 @@ BLOCKS = V // P
 OWN = 2
 R_BLOCKS = U // P
 VECTOR_GROUPS = (72, 32)
-TERM_BUFFERS = 4
-H_BANKS = {1: (2, 4), 2: (6, 7), 3: (5, 4)}
+WHOLE_TILE = 1
+H_BANKS = {1: (4, 5), 2: (6, 7), 3: (4, 5)}
 TURN_BANKS = (2, 6)
+THIRD_BANK = 0
 SHARED_BACK_BANK = 4
-OWN_BACK_BANK = 2
-G_BANKS = (0, 1, 6, 7)
-G_SECOND_BANKS = (4, 5)
-MERGE = (False, True)
 ROOT_BANKS = (2, 3)
-ROOT_BACK_BANKS = (6, 7)
+ROOT_BACK_BANKS = (4, 5)
+G_BANKS = (0, 2, 6)
 
 
 def tile_picked_hop2_gelu_e_kernel(
@@ -50,7 +48,6 @@ def tile_picked_hop2_gelu_e_kernel(
 
     with ExitStack() as ctx:
         keep = ctx.enter_context(tc.tile_pool(name="keep", bufs=1))
-        picked = ctx.enter_context(tc.tile_pool(name="picked", bufs=TERM_BUFFERS))
         psum = ctx.enter_context(tc.psum_pool(name="psum", bufs=1))
 
         def bank(n, shape):
@@ -136,9 +133,9 @@ def tile_picked_hop2_gelu_e_kernel(
         nc.sync.dma_start(own_gates[:], gate[0 : D - 1, :, 0:own_width].rearrange("d p v -> p d v"))
         last_gates = keep.tile([P, V], F32, name="last_gates")
         nc.sync.dma_start(last_gates[:], gate[D - 1])
-        gate_cols = [keep.tile([P, BLOCKS - OWN], F32, name="gate_cols%d" % d) for d in range(D - 1)]
+        gate_cols = [keep.tile([P, BLOCKS - OWN], F32, name="gate_cols%d" % d) for d in range(D)]
         with nc.allow_non_contiguous_dma(reason="one gate a partition"):
-            for d in range(D - 1):
+            for d in range(D):
                 nc.sync.dma_start(gate_cols[d][:], gate[d, 0, own_width:V].rearrange("(b p) -> p b", p=P))
         w2_codes = keep.tile([P, N], U32, name="w2_codes", align_bytes=64)
         nc.sync.dma_start(w2_codes[:].bitcast(I32), w2_words[0].rearrange("p n t -> p (n t)").bitcast(I32))
@@ -211,31 +208,21 @@ def tile_picked_hop2_gelu_e_kernel(
         quantize_w1(high_rows[:].rearrange("p e c -> p (e c)"), 2 * P, 2 * P)
 
         g = [keep.tile([P, V], F32, name="g%d" % m) for m in range(M_TILES)]
-
-        def turn(acc, term, b, d, last):
-            nc.tensor.matmul(acc, term[:, block(b)], ident[:], start=(d == 0), stop=(d == last), is_transpose=True)
-
         z_codes = keep.tile([P, V], U32, name="z_codes", align_bytes=64)
         z_bytes = keep.tile([P, V], U8, name="z_bytes", align_bytes=64)
 
-        def second_layer(acc, m, cols):
-            nc.tensor.matmul_mx(
-                out=acc,
-                lhsT=w2_codes[:, block(m)].bitcast(FP8X4),
-                lhsT_scale=w2_bytes[:, block(m)],
-                rhs=z_codes[:, cols].bitcast(FP8X4),
-                rhs_scale=z_bytes[:, cols],
-                start=True,
-                stop=True,
-            )
-
-        own = range(OWN)
         shared = range(BLOCKS - OWN)
         shared_width = V - own_width
-        held = keep.tile([P, H_TILES * V + (D - 1) * own_width], F32, name="held", tag="w_pair1", align_bytes=64)
+        held = keep.tile([P, H_TILES * V + 2 * (D - 1) * own_width], F32, name="held", tag="w_pair1", align_bytes=64)
         third = held[:, 0 : H_TILES * V].rearrange("p (t v) -> p t v", t=H_TILES)
-        own_sums = [bank(b, [P, H_TILES, P]) for b in own]
+        later_terms = keep.tile([P, 2 * (D - 1) * own_width], F32, name="later_terms")
+        own_terms = [
+            rows.rearrange("p (d e v) -> p d e v", d=D - 1, e=2) for rows in (held[:, H_TILES * V :], later_terms[:])
+        ]
+        two = keep.tile([P, H_TILES, own_width], F32, name="two")
         turned = {}
+        nc.gpsimd.memset(third[:, WHOLE_TILE, own_width:V], 0.0)
+        turned_third = bank(THIRD_BANK, [P, BLOCKS - OWN, P])
 
         def products(t):
             return [product(t, c0, BANK, H_BANKS[t][c0 // BANK]) for c0 in range(0, S, BANK)]
@@ -246,31 +233,31 @@ def tile_picked_hop2_gelu_e_kernel(
 
         def vector_terms(t):
             for d in range(D - 1):
-                if t == 0:
-                    term = held[:, H_TILES * V + d * own_width : H_TILES * V + (d + 1) * own_width]
-                else:
-                    term = picked.tile([P, own_width], F32, name="term")[:]
-                nc.vector.tensor_tensor(term, h[t][:].indirect(entries(pos[d], 0, own_width)), own_gates[:, d, :], MULT)
-                for b in own:
-                    turn(own_sums[b][:, t, :], term, b, d, D - 1)
-            cuts = (0, own_width, V) if t == H_TILES - 1 else (0, V)
-            for v0, v1 in zip(cuts, cuts[1:]):
                 nc.vector.tensor_tensor(
-                    third[:, t, v0:v1], h[t][:].indirect(entries(pos[D - 1], v0, v1 - v0)), last_gates[:, v0:v1], MULT
+                    own_terms[t // 2][:, d, t % 2, :],
+                    h[t][:].indirect(entries(pos[d], 0, own_width)),
+                    own_gates[:, d, :],
+                    MULT,
                 )
-                if v0 == 0:
-                    for b in own:
-                        turn(own_sums[b][:, t, :], third[:, t, :], b, D - 1, D - 1)
+            width = own_width if t == WHOLE_TILE else V
+            nc.vector.tensor_tensor(
+                third[:, t, 0:width], h[t][:].indirect(entries(pos[D - 1], 0, width)), last_gates[:, 0:width], MULT
+            )
+            if t % 2 == 1:
+                nc.vector.tensor_tensor(
+                    two[:, t - 1 : t + 1, :], own_terms[t // 2][:, 0, :, :], own_terms[t // 2][:, 1, :, :], ADD
+                )
 
         def scalar_terms(t):
             if t % 2 == 0:
                 for b in shared:
                     turned[t // 2, b] = bank(TURN_BANKS[t // 2] + b, [P, D - 1, 2, P])
-            for d in range(D - 1):
+            for d in range(D if t == WHOLE_TILE else D - 1):
                 raw = keep.tile([P, shared_width], F32, name="raw%d_%d" % (t, d))
                 nc.scalar.activation(raw[:], h[t][:].indirect(entries(pos[d], own_width, shared_width)), COPY)
                 for b in shared:
-                    nc.tensor.transpose(turned[t // 2, b][:, d, t % 2, :], raw[:, block(b)], ident[:])
+                    dst = turned[t // 2, b][:, d, t % 2, :] if d < D - 1 else turned_third[:, b, :]
+                    nc.tensor.transpose(dst, raw[:, block(b)], ident[:])
 
         second, next_tile = products(1), products(2)
         scalar_terms(0)
@@ -289,59 +276,67 @@ def tile_picked_hop2_gelu_e_kernel(
         shared_back = [bank(SHARED_BACK_BANK + b, [P, H_TILES, P]) for b in shared]
         for pair in range(2):
             for b in shared:
-                first = keep.tile([P, 2, P], F32, name="first%d_%d" % (pair, b))
-                nc.scalar.activation(first[:], turned[pair, b][:, 0, :, :], COPY, scale=gate_cols[0][:, b : b + 1])
-                if MERGE[pair]:
-                    both = keep.tile([P, 2, P], F32, name="both%d_%d" % (pair, b))
-                    nc.vector.scalar_tensor_tensor(
-                        both[:], turned[pair, b][:, 1, :, :], gate_cols[1][:, b : b + 1], first[:], MULT, ADD
+                gated = keep.tile([P, D - 1, 2, P], F32, name="gated%d_%d" % (pair, b))
+                for d in range(D - 1):
+                    nc.scalar.activation(
+                        gated[:, d, :, :], turned[pair, b][:, d, :, :], COPY, scale=gate_cols[d][:, b : b + 1]
                     )
-                    for e in range(2):
-                        nc.tensor.transpose(shared_back[b][:, 2 * pair + e, :], both[:, e, :], ident[:])
-                else:
-                    second = keep.tile([P, 2, P], F32, name="second%d_%d" % (pair, b))
-                    nc.scalar.activation(second[:], turned[pair, b][:, 1, :, :], COPY, scale=gate_cols[1][:, b : b + 1])
-                    for e in range(2):
-                        for d, gated in enumerate((first, second)):
-                            turn(shared_back[b][:, 2 * pair + e, :], gated[:, e, :], 0, d, 1)
+                for e in range(2):
+                    terms = [gated[:, d, e, :] for d in range(D - 1)]
+                    if 2 * pair + e == WHOLE_TILE:
+                        extra = keep.tile([P, P], F32, name="extra%d" % b)
+                        nc.scalar.activation(extra[:], turned_third[:, b, :], COPY, scale=gate_cols[D - 1][:, b : b + 1])
+                        terms.append(extra[:])
+                    for d, term in enumerate(terms):
+                        nc.tensor.matmul(
+                            shared_back[b][:, 2 * pair + e, :],
+                            term,
+                            ident[:],
+                            start=(d == 0),
+                            stop=(d == len(terms) - 1),
+                            is_transpose=True,
+                        )
 
-        z_in = [keep.tile([P, P * PACK], BF16, name="z_in%d" % b, align_bytes=64) for b in range(BLOCKS)]
-        own_back = {}
-        for b in reversed(own):
-            pairs = keep.tile([P, 2, P, 2], BF16, name="pairs%d" % b)
-            nc.scalar.copy(out=pairs[:], in_=own_sums[b][:].rearrange("v (u e) p -> v u p e", e=2))
-            own_back[b] = bank(OWN_BACK_BANK + b, [P, 2, P])
-            for u in range(2):
-                nc.tensor.transpose(
-                    own_back[b][:, u, :], pairs[:, u, :, :].rearrange("v p e -> v (p e)").bitcast(F32), ident[:]
-                )
-        for b in reversed(own):
-            nc.scalar.copy(
-                out=z_in[b][:].bitcast(F32).rearrange("p (v u) -> p v u", u=2),
-                in_=own_back[b][:].rearrange("p u v -> p v u"),
-            )
-
-        for b in shared:
+        def add_third(name, partial, cols):
+            z_in = keep.tile([P, (cols.stop - cols.start) * PACK], BF16, name=name, align_bytes=64)
             nc.vector.tensor_tensor(
-                z_in[OWN + b][:].rearrange("p (c i j) -> p c j i", i=LINE, j=PACK),
-                shared_back[b][:].rearrange("p j (c i) -> p c j i", i=LINE),
-                third[:, :, block(OWN + b)].rearrange("p j (c i) -> p c j i", i=LINE),
+                z_in[:].rearrange("p (c i j) -> p c j i", i=LINE, j=PACK),
+                partial.rearrange("p j (c i) -> p c j i", i=LINE),
+                third[:, :, cols].rearrange("p j (c i) -> p c j i", i=LINE),
                 ADD,
             )
-        early_g = bank(G_SECOND_BANKS[0], [P, V])
-        for b in (2, 3, 1, 0):
-            nc.vector.quantize_mx(out=z_codes[:, block(b)].bitcast(FP8X4), scales=z_bytes[:, block(b)], in_=z_in[b][:])
-            acc = bank(G_BANKS[b], [P, P])
-            second_layer(acc[:], 0, block(b))
-            nc.scalar.activation(g[0][:, block(b)], acc[:], RELU)
-            if b == 3:
-                second_layer(early_g[:, own_width:V], 1, slice(own_width, V))
-            if b == 1:
-                second_layer(early_g[:, block(b)], 1, block(b))
-        last_g = bank(G_SECOND_BANKS[1], [P, P])
-        second_layer(last_g[:], 1, block(0))
-        nc.scalar.activation(g[1][:, block(0)], last_g[:], RELU)
-        nc.vector.tensor_scalar_max(g[1][:, P:V], early_g[:, P:V], 0.0)
+            return z_in
+
+        def second_layer(z_in, cols, first_bank):
+            nc.vector.quantize_mx(out=z_codes[:, cols].bitcast(FP8X4), scales=z_bytes[:, cols], in_=z_in[:])
+            accs = []
+            for m in range(M_TILES):
+                acc = bank(first_bank + m, [P, cols.stop - cols.start])
+                nc.tensor.matmul_mx(
+                    out=acc[:],
+                    lhsT=w2_codes[:, block(m)].bitcast(FP8X4),
+                    lhsT_scale=w2_bytes[:, block(m)],
+                    rhs=z_codes[:, cols].bitcast(FP8X4),
+                    rhs_scale=z_bytes[:, cols],
+                    start=True,
+                    stop=True,
+                )
+                accs.append(acc)
+            return accs
+
+        parts = [slice(0, own_width)] + [block(OWN + b) for b in shared]
+        own_in = add_third("own_in", two[:], parts[0])
+        ins = [own_in] + [add_third("z_in%d" % b, shared_back[b][:], parts[1 + b]) for b in shared]
+        for n, cols in enumerate(parts):
+            accs = second_layer(ins[n], cols, G_BANKS[n])
+            nc.scalar.activation(g[0][:, cols], accs[0][:], RELU)
+            if n < len(parts) - 1:
+                nc.scalar.activation(g[1][:, cols], accs[1][:], RELU)
+            else:
+                nc.vector.tensor_scalar_max(g[1][:, cols], accs[1][:], 0.0)
+
+        def turn(acc, term, b, d, last):
+            nc.tensor.matmul(acc, term[:, block(b)], ident[:], start=(d == 0), stop=(d == last), is_transpose=True)
 
         def root_term(m, d, r0, width):
             term = keep.tile([P, width], F32, name="root_term%d_%d_%d" % (m, d, r0))

@@ -36,9 +36,10 @@ H_BANKS = {1: (4, 5), 2: (6, 7), 3: (4, 5)}
 TURN_BANKS = (2, 6)
 THIRD_BANK = 0
 SHARED_BACK_BANK = 4
-ROOT_BANKS = (2, 3)
-ROOT_BACK_BANKS = (4, 5)
-G_BANKS = (0, 2, 6)
+ROOT_BANKS = (4, 5)
+ROOT_BACK_BANKS = (6, 7)
+OWN_G_BANKS = (7, 6)
+SHARED_G_BANK = 0
 
 
 def tile_picked_hop2_gelu_e_kernel(
@@ -208,7 +209,6 @@ def tile_picked_hop2_gelu_e_kernel(
         quantize_w1(high_rows[:].rearrange("p e c -> p (e c)"), 2 * P, 2 * P)
 
         g = [keep.tile([P, V], F32, name="g%d" % m) for m in range(M_TILES)]
-        z_codes = keep.tile([P, V], U32, name="z_codes", align_bytes=64)
         z_bytes = keep.tile([P, V], U8, name="z_bytes", align_bytes=64)
 
         shared = range(BLOCKS - OWN)
@@ -267,35 +267,39 @@ def tile_picked_hop2_gelu_e_kernel(
         vector_terms(0)
         scalar_terms(1)
         gelus(3, last)
+        shared_back = [bank(SHARED_BACK_BANK + b, [P, H_TILES, P]) for b in shared]
+
+        def gate_and_turn_back(pair, b):
+            gated = keep.tile([P, D - 1, 2, P], F32, name="gated%d_%d" % (pair, b), align_bytes=64)
+            for d in range(D - 1):
+                nc.scalar.activation(
+                    gated[:, d, :, :], turned[pair, b][:, d, :, :], COPY, scale=gate_cols[d][:, b : b + 1]
+                )
+            for e in range(2):
+                terms = [gated[:, d, e, :] for d in range(D - 1)]
+                if 2 * pair + e == WHOLE_TILE:
+                    extra = keep.tile([P, P], F32, name="extra%d" % b)
+                    nc.scalar.activation(extra[:], turned_third[:, b, :], COPY, scale=gate_cols[D - 1][:, b : b + 1])
+                    terms.append(extra[:])
+                for d, term in enumerate(terms):
+                    nc.tensor.matmul(
+                        shared_back[b][:, 2 * pair + e, :],
+                        term,
+                        ident[:],
+                        start=(d == 0),
+                        stop=(d == len(terms) - 1),
+                        is_transpose=True,
+                    )
+
         vector_terms(1)
+        gate_and_turn_back(0, 0)
         scalar_terms(2)
         vector_terms(2)
         scalar_terms(3)
         vector_terms(3)
-
-        shared_back = [bank(SHARED_BACK_BANK + b, [P, H_TILES, P]) for b in shared]
-        for pair in range(2):
-            for b in shared:
-                gated = keep.tile([P, D - 1, 2, P], F32, name="gated%d_%d" % (pair, b))
-                for d in range(D - 1):
-                    nc.scalar.activation(
-                        gated[:, d, :, :], turned[pair, b][:, d, :, :], COPY, scale=gate_cols[d][:, b : b + 1]
-                    )
-                for e in range(2):
-                    terms = [gated[:, d, e, :] for d in range(D - 1)]
-                    if 2 * pair + e == WHOLE_TILE:
-                        extra = keep.tile([P, P], F32, name="extra%d" % b)
-                        nc.scalar.activation(extra[:], turned_third[:, b, :], COPY, scale=gate_cols[D - 1][:, b : b + 1])
-                        terms.append(extra[:])
-                    for d, term in enumerate(terms):
-                        nc.tensor.matmul(
-                            shared_back[b][:, 2 * pair + e, :],
-                            term,
-                            ident[:],
-                            start=(d == 0),
-                            stop=(d == len(terms) - 1),
-                            is_transpose=True,
-                        )
+        gate_and_turn_back(0, 1)
+        for b in shared:
+            gate_and_turn_back(1, b)
 
         def add_third(name, partial, cols):
             z_in = keep.tile([P, (cols.stop - cols.start) * PACK], BF16, name=name, align_bytes=64)
@@ -307,33 +311,37 @@ def tile_picked_hop2_gelu_e_kernel(
             )
             return z_in
 
-        def second_layer(z_in, cols, first_bank):
-            nc.vector.quantize_mx(out=z_codes[:, cols].bitcast(FP8X4), scales=z_bytes[:, cols], in_=z_in[:])
-            accs = []
-            for m in range(M_TILES):
-                acc = bank(first_bank + m, [P, cols.stop - cols.start])
-                nc.tensor.matmul_mx(
-                    out=acc[:],
-                    lhsT=w2_codes[:, block(m)].bitcast(FP8X4),
-                    lhsT_scale=w2_bytes[:, block(m)],
-                    rhs=z_codes[:, cols].bitcast(FP8X4),
-                    rhs_scale=z_bytes[:, cols],
-                    start=True,
-                    stop=True,
-                )
-                accs.append(acc)
-            return accs
+        def quantize_z(codes, z_in, cols):
+            nc.vector.quantize_mx(out=codes.bitcast(FP8X4), scales=z_bytes[:, cols], in_=z_in[:])
 
-        parts = [slice(0, own_width)] + [block(OWN + b) for b in shared]
-        own_in = add_third("own_in", two[:], parts[0])
-        ins = [own_in] + [add_third("z_in%d" % b, shared_back[b][:], parts[1 + b]) for b in shared]
-        for n, cols in enumerate(parts):
-            accs = second_layer(ins[n], cols, G_BANKS[n])
-            nc.scalar.activation(g[0][:, cols], accs[0][:], RELU)
-            if n < len(parts) - 1:
-                nc.scalar.activation(g[1][:, cols], accs[1][:], RELU)
+        def second_layer(m, codes, cols, n):
+            acc = bank(n, [P, cols.stop - cols.start])
+            nc.tensor.matmul_mx(
+                out=acc[:],
+                lhsT=w2_codes[:, block(m)].bitcast(FP8X4),
+                lhsT_scale=w2_bytes[:, block(m)],
+                rhs=codes.bitcast(FP8X4),
+                rhs_scale=z_bytes[:, cols],
+                start=True,
+                stop=True,
+            )
+            if (m, cols.stop) == (M_TILES - 1, V):
+                nc.vector.tensor_scalar_max(g[m][:, cols], acc[:], 0.0)
             else:
-                nc.vector.tensor_scalar_max(g[1][:, cols], accs[1][:], 0.0)
+                nc.scalar.activation(g[m][:, cols], acc[:], RELU)
+
+        own_cols = slice(0, own_width)
+        own_in = add_third("own_in", two[:], own_cols)
+        shared_in = [add_third("z_in%d" % b, shared_back[b][:], block(OWN + b)) for b in shared]
+        own_codes = keep.tile([P, own_width], U32, name="own_codes", tag="gated1_0", align_bytes=64)
+        shared_codes = keep.tile([P, shared_width], U32, name="shared_codes", tag="gated1_1", align_bytes=64)
+        quantize_z(own_codes[:], own_in, own_cols)
+        for m in range(M_TILES):
+            second_layer(m, own_codes[:], own_cols, OWN_G_BANKS[m])
+        for b in shared:
+            quantize_z(shared_codes[:, block(b)], shared_in[b], block(OWN + b))
+            for m in range(M_TILES):
+                second_layer(m, shared_codes[:, block(b)], block(OWN + b), SHARED_G_BANK + 2 * b + m)
 
         def turn(acc, term, b, d, last):
             nc.tensor.matmul(acc, term[:, block(b)], ident[:], start=(d == 0), stop=(d == last), is_transpose=True)

@@ -231,6 +231,11 @@ def tile_picked_hop2_gelu_e_kernel(
             for half, acc in enumerate(accs):
                 gelu(t, half * BANK, acc)
 
+        def third_term(t, v0, v1):
+            nc.vector.tensor_tensor(
+                third[:, t, v0:v1], h[t][:].indirect(entries(pos[D - 1], v0, v1 - v0)), last_gates[:, v0:v1], MULT
+            )
+
         def vector_terms(t):
             for d in range(D - 1):
                 nc.vector.tensor_tensor(
@@ -239,20 +244,19 @@ def tile_picked_hop2_gelu_e_kernel(
                     own_gates[:, d, :],
                     MULT,
                 )
-            width = own_width if t == WHOLE_TILE else V
-            nc.vector.tensor_tensor(
-                third[:, t, 0:width], h[t][:].indirect(entries(pos[D - 1], 0, width)), last_gates[:, 0:width], MULT
-            )
+            third_term(t, 0, V if t % 2 == 0 else own_width)
             if t % 2 == 1:
                 nc.vector.tensor_tensor(
                     two[:, t - 1 : t + 1, :], own_terms[t // 2][:, 0, :, :], own_terms[t // 2][:, 1, :, :], ADD
                 )
+            if t == H_TILES - 1:
+                third_term(t, own_width, V)
 
-        def scalar_terms(t):
-            if t % 2 == 0:
+        def scalar_terms(t, first_list=0, end_list=D):
+            if t % 2 == 0 and first_list == 0:
                 for b in shared:
                     turned[t // 2, b] = bank(TURN_BANKS[t // 2] + b, [P, D - 1, 2, P])
-            for d in range(D if t == WHOLE_TILE else D - 1):
+            for d in range(first_list, min(end_list, D if t == WHOLE_TILE else D - 1)):
                 raw = keep.tile([P, shared_width], F32, name="raw%d_%d" % (t, d))
                 nc.scalar.activation(raw[:], h[t][:].indirect(entries(pos[d], own_width, shared_width)), COPY)
                 for b in shared:
@@ -260,8 +264,9 @@ def tile_picked_hop2_gelu_e_kernel(
                     nc.tensor.transpose(dst, raw[:, block(b)], ident[:])
 
         second, next_tile = products(1), products(2)
-        scalar_terms(0)
+        scalar_terms(0, 0, 1)
         gelus(1, second)
+        scalar_terms(0, 1)
         gelus(2, next_tile)
         last = products(3)
         vector_terms(0)
@@ -275,21 +280,20 @@ def tile_picked_hop2_gelu_e_kernel(
                 nc.scalar.activation(
                     gated[:, d, :, :], turned[pair, b][:, d, :, :], COPY, scale=gate_cols[d][:, b : b + 1]
                 )
-            for e in range(2):
-                terms = [gated[:, d, e, :] for d in range(D - 1)]
-                if 2 * pair + e == WHOLE_TILE:
-                    extra = keep.tile([P, P], F32, name="extra%d" % b)
-                    nc.scalar.activation(extra[:], turned_third[:, b, :], COPY, scale=gate_cols[D - 1][:, b : b + 1])
-                    terms.append(extra[:])
-                for d, term in enumerate(terms):
-                    nc.tensor.matmul(
-                        shared_back[b][:, 2 * pair + e, :],
-                        term,
-                        ident[:],
-                        start=(d == 0),
-                        stop=(d == len(terms) - 1),
-                        is_transpose=True,
-                    )
+            terms = [(e, gated[:, d, e, :]) for d in range(D - 1) for e in range(2)]
+            if pair == WHOLE_TILE // 2:
+                extra = keep.tile([P, P], F32, name="extra%d" % b)
+                nc.scalar.activation(extra[:], turned_third[:, b, :], COPY, scale=gate_cols[D - 1][:, b : b + 1])
+                terms.append((WHOLE_TILE % 2, extra[:]))
+            for n, (e, term) in enumerate(terms):
+                nc.tensor.matmul(
+                    shared_back[b][:, 2 * pair + e, :],
+                    term,
+                    ident[:],
+                    start=(n == 0),
+                    stop=(n == len(terms) - 1),
+                    is_transpose=True,
+                )
 
         vector_terms(1)
         gate_and_turn_back(0, 0)
@@ -331,11 +335,12 @@ def tile_picked_hop2_gelu_e_kernel(
                 nc.scalar.activation(g[m][:, cols], acc[:], RELU)
 
         own_cols = slice(0, own_width)
-        own_in = add_third("own_in", two[:], own_cols)
+        own_in = [add_third("own_in%d" % b, two[:, :, block(b)], block(b)) for b in range(OWN)]
         shared_in = [add_third("z_in%d" % b, shared_back[b][:], block(OWN + b)) for b in shared]
-        own_codes = keep.tile([P, own_width], U32, name="own_codes", tag="gated1_0", align_bytes=64)
+        own_codes = keep.tile([P, own_width], U32, name="own_codes", align_bytes=64)
         shared_codes = keep.tile([P, shared_width], U32, name="shared_codes", tag="gated1_1", align_bytes=64)
-        quantize_z(own_codes[:], own_in, own_cols)
+        for b in range(OWN):
+            quantize_z(own_codes[:, block(b)], own_in[b], block(b))
         for m in range(M_TILES):
             second_layer(m, own_codes[:], own_cols, OWN_G_BANKS[m])
         for b in shared:

@@ -36,6 +36,7 @@ H_BANKS = {1: (4, 5), 2: (6, 7), 3: (4, 5)}
 TURN_BANKS = (2, 6)
 THIRD_BANK = 0
 SHARED_BACK_BANK = 4
+ROOT_PLAIN_BANK = 0
 ROOT_BANKS = (4, 5)
 ROOT_BACK_BANKS = (6, 7)
 OWN_G_BANKS = (7, 6)
@@ -146,6 +147,9 @@ def tile_picked_hop2_gelu_e_kernel(
                 w2_scales[0, 4 * quad : 4 * quad + 4, :].bitcast(I32),
             )
         nxt = [load_list("nxt%d" % d, src) for d, src in enumerate((nxt1, nxt2, nxt3))]
+        root_cols = keep.tile([P, R_BLOCKS], F32, name="root_cols")
+        with nc.allow_non_contiguous_dma(reason="one gate a partition"):
+            nc.sync.dma_start(root_cols[:], gate2[D - 1, 0, :].rearrange("(b p) -> p b", p=P))
         gates2 = keep.tile([P, D, U], F32, name="gates2")
         nc.sync.dma_start(gates2[:], gate2.rearrange("d p r -> p d r"))
 
@@ -368,24 +372,28 @@ def tile_picked_hop2_gelu_e_kernel(
             plain_term(plain[:, d, :], 1, d)
 
         root_sums = [bank(ROOT_BANKS[b], [P, P]) for b in range(R_BLOCKS)]
-        for d in range(D):
-            if d < D - 1:
-                term = root_term(0, d, 0, U)
-            else:
-                term = keep.tile([P, U], F32, name="first_third")
-                nc.vector.tensor_tensor(term[:], plain_first[:], gates2[:, d, :], MULT)
+        plain_turned = bank(ROOT_PLAIN_BANK, [P, R_BLOCKS, P])
+        for d in range(D - 1):
+            term = root_term(0, d, 0, U)
             for b in range(R_BLOCKS):
-                turn(root_sums[b][:], term, b, d, D - 1)
+                turn(root_sums[b][:], term, b, d, D - 2)
+            if d == 0:
+                for b in range(R_BLOCKS):
+                    nc.tensor.transpose(plain_turned[:, b, :], plain_first[:, block(b)], ident[:])
+        last_third = root_term(1, D - 1, 0, U)
+        root_gated = keep.tile([P, R_BLOCKS, P], F32, name="root_gated")
         for b in range(R_BLOCKS):
+            nc.scalar.activation(root_gated[:, b, :], plain_turned[:, b, :], COPY, scale=root_cols[:, b : b + 1])
+        for b, copy in enumerate((nc.scalar.copy, nc.vector.tensor_copy)):
             summed = keep.tile([P, P], F32, name="summed%d" % b)
-            nc.scalar.copy(out=summed[:], in_=root_sums[b][:])
+            copy(out=summed[:], in_=root_sums[b][:])
             back = bank(ROOT_BACK_BANKS[b], [P, P])
-            nc.tensor.transpose(back[:], summed[:], ident[:])
+            turn(back[:], root_gated[:, b, :], 0, 0, 1)
+            turn(back[:], summed, 0, 1, 1)
             first_rows = keep.tile([P, P], F32, name="first_rows%d" % b)
             nc.scalar.copy(out=first_rows[:], in_=back[:])
             nc.scalar.dma_start(out[0:P, block(b)], first_rows[:])
 
-        last_third = root_term(1, D - 1, 0, U)
         terms = keep.tile([P, D - 1, U], F32, name="terms")
         for d in range(D - 1):
             nc.vector.tensor_tensor(terms[:, d, :], plain[:, d, :], gates2[:, d, :], MULT)

@@ -384,9 +384,9 @@ def tile_picked_hop2_gelu_e_kernel(
         root_gated = keep.tile([P, R_BLOCKS, P], F32, name="root_gated")
         for b in range(R_BLOCKS):
             nc.scalar.activation(root_gated[:, b, :], plain_turned[:, b, :], COPY, scale=root_cols[:, b : b + 1])
-        for b, copy in enumerate((nc.scalar.copy, nc.vector.tensor_copy)):
+        for b in range(R_BLOCKS):
             summed = keep.tile([P, P], F32, name="summed%d" % b)
-            copy(out=summed[:], in_=root_sums[b][:])
+            nc.scalar.copy(out=summed[:], in_=root_sums[b][:])
             back = bank(ROOT_BACK_BANKS[b], [P, P])
             turn(back[:], root_gated[:, b, :], 0, 0, 1)
             turn(back[:], summed, 0, 1, 1)

@@ -333,10 +333,7 @@ def tile_picked_hop2_gelu_e_kernel(
                 start=True,
                 stop=True,
             )
-            if (m, cols.stop) == (M_TILES - 1, V):
-                nc.vector.tensor_scalar_max(g[m][:, cols], acc[:], 0.0)
-            else:
-                nc.scalar.activation(g[m][:, cols], acc[:], RELU)
+            nc.scalar.activation(g[m][:, cols], acc[:], RELU)
 
         own_cols = slice(0, own_width)
         own_in = [add_third("own_in%d" % b, two[:, :, block(b)], block(b)) for b in range(OWN)]
@@ -349,8 +346,8 @@ def tile_picked_hop2_gelu_e_kernel(
             second_layer(m, own_codes[:], own_cols, OWN_G_BANKS[m])
         for b in shared:
             quantize_z(shared_codes[:, block(b)], shared_in[b], block(OWN + b))
-            for m in range(M_TILES):
-                second_layer(m, shared_codes[:, block(b)], block(OWN + b), SHARED_G_BANK + 2 * b + m)
+            second_layer(0, shared_codes[:, block(b)], block(OWN + b), SHARED_G_BANK + 1 + b)
+        second_layer(1, shared_codes[:], slice(own_width, V), SHARED_G_BANK + 3)
 
         def turn(acc, term, b, d, last):
             nc.tensor.matmul(acc, term[:, block(b)], ident[:], start=(d == 0), stop=(d == last), is_transpose=True)

@@ -28,19 +28,20 @@ BANK = 512
 H_TILES = H // P
 M_TILES = N // P
 BLOCKS = V // P
-OWN = 2
 R_BLOCKS = U // P
+OWN = 2
 VECTOR_GROUPS = (72, 32)
 WHOLE_TILE = 1
+
 H_BANKS = {1: (4, 5), 2: (6, 7), 3: (4, 5)}
 TURN_BANKS = (2, 6)
 THIRD_BANK = 0
-SHARED_BACK_BANK = 4
-ROOT_PLAIN_BANK = 0
-ROOT_BANKS = (4, 5)
-ROOT_BACK_BANKS = (6, 7)
+BACK_BANK = 4
 OWN_G_BANKS = (7, 6)
-SHARED_G_BANK = 0
+SHARED_G_BANKS = (1, 2, 3)
+ROOT_TURN_BANK = 0
+ROOT_SUM_BANKS = (4, 5)
+ROOT_BACK_BANKS = (6, 7)
 
 
 def tile_picked_hop2_gelu_e_kernel(
@@ -66,6 +67,9 @@ def tile_picked_hop2_gelu_e_kernel(
         def block(b):
             return slice(b * P, (b + 1) * P)
 
+        def turn(acc, term, n, last):
+            nc.tensor.matmul(acc, term, ident[:], start=(n == 0), stop=(n == last), is_transpose=True)
+
         ident = keep.tile([P, P], F32, name="ident")
         make_identity(nc, ident[:])
         warm = keep.tile([P, 2], F32, name="warm")
@@ -86,7 +90,9 @@ def tile_picked_hop2_gelu_e_kernel(
         for j in (0, 1, 3):
             planes[j] = load_plane(j)
 
-        rest = S - PIECE
+        rest = PIECE
+        low_rows = keep.tile([P, 6, P * PACK], BF16, name="low_rows", align_bytes=64)
+        direct = low_rows[:, 1:5, :].rearrange("p r c -> p (r c)")
         word_row = keep.tile([P, 2 * rest], U32, name="word_row")
         halves = word_row[:].bitcast(BF16)
         staged = keep.tile([P, PACK, PIECE], BF16, name="staged")
@@ -99,6 +105,12 @@ def tile_picked_hop2_gelu_e_kernel(
                 in_=planes[j][:].indirect(entries(offs_t, e0, count)),
             )
 
+        def gather_direct(j, e0, count):
+            first = (e0 - 2 * PIECE) * PACK
+            nc.vector.tensor_copy(
+                out=direct[:, first + j : first + count * PACK : PACK], in_=planes[j][:].indirect(entries(offs_t, e0, count))
+            )
+
         def gather_first(j):
             nc.scalar.activation(staged[:, j, :], planes[j][:].indirect(entries(offs_t, 0, PIECE)), COPY)
 
@@ -107,12 +119,13 @@ def tile_picked_hop2_gelu_e_kernel(
 
         for j in (2, 0, 1):
             gather_half(j, PIECE, rest)
+            gather_direct(j, 2 * PIECE, 2 * PIECE)
             gather_first(j)
         place_first(0, PACK - 1)
         gather_first(PACK - 1)
         place_first(PACK - 1, PACK)
-        for e0 in range(PIECE, S, PIECE):
-            gather_half(3, e0, PIECE)
+        gather_half(PACK - 1, PIECE, rest)
+        gather_direct(PACK - 1, 2 * PIECE, 2 * PIECE)
 
         w_rows = w1.rearrange("(p j) c -> p j c", j=PACK)
         w1_codes = [keep.tile([P, 2 * P], U32, name="w1_codes", align_bytes=64)]
@@ -153,7 +166,6 @@ def tile_picked_hop2_gelu_e_kernel(
         gates2 = keep.tile([P, D, U], F32, name="gates2")
         nc.sync.dma_start(gates2[:], gate2.rearrange("d p r -> p d r"))
 
-        low_rows = keep.tile([P, 6, P * PACK], BF16, name="low_rows", align_bytes=64)
         high_rows = keep.tile([P, 2, P * PACK], BF16, name="high_rows", tag="w_pair1", align_bytes=64)
         w_pairs = [rows.rearrange("p e (m j) -> p e m j", j=PACK) for rows in (low_rows[:, 0:6:5, :], high_rows[:])]
 
@@ -182,19 +194,13 @@ def tile_picked_hop2_gelu_e_kernel(
         def gelu(t, c0, acc):
             nc.scalar.activation(h[t][:, c0 : c0 + acc.shape[1]], acc[:], GELU)
 
-        woven = [first_woven[:].rearrange("p c j -> p (c j)")]
-        for e0 in range(0, rest, PIECE):
-            if e0 == 0:
-                tile = keep.tile([P, PIECE * PACK], BF16, name="woven", align_bytes=64)[:]
-            else:
-                row = 2 * e0 // PIECE - 1
-                tile = low_rows[:, row : row + 2, :].rearrange("p r c -> p (r c)")
-            weave = nc.scalar.copy if e0 == rest - PIECE else nc.gpsimd.tensor_copy
-            weave(
-                out=tile.bitcast(U32).rearrange("p (c u) -> p c u", u=2),
-                in_=word_row[:].rearrange("p (u c) -> p c u", u=2)[:, e0 : e0 + PIECE, :],
-            )
-            woven.append(tile)
+        second_woven = keep.tile([P, PIECE * PACK], BF16, name="woven", align_bytes=64)
+        nc.gpsimd.tensor_copy(
+            out=second_woven[:].bitcast(U32).rearrange("p (c u) -> p c u", u=2),
+            in_=word_row[:].rearrange("p (u c) -> p c u", u=2),
+        )
+        woven = [first_woven[:].rearrange("p c j -> p (c j)"), second_woven[:]]
+        woven.extend(direct[:, n * PIECE * PACK : (n + 1) * PIECE * PACK] for n in range(2))
         for u in range(2):
             round_w1(nc.vector.tensor_copy, u, slice(0, VECTOR_GROUPS[u]))
             round_w1(nc.scalar.copy, u, slice(VECTOR_GROUPS[u], P))
@@ -231,8 +237,8 @@ def tile_picked_hop2_gelu_e_kernel(
         def products(t):
             return [product(t, c0, BANK, H_BANKS[t][c0 // BANK]) for c0 in range(0, S, BANK)]
 
-        def gelus(t, accs):
-            for half, acc in enumerate(accs):
+        def gelus(t, halves_of_tile):
+            for half, acc in enumerate(halves_of_tile):
                 gelu(t, half * BANK, acc)
 
         def third_term(t, v0, v1):
@@ -248,7 +254,7 @@ def tile_picked_hop2_gelu_e_kernel(
                     own_gates[:, d, :],
                     MULT,
                 )
-            third_term(t, 0, V if t % 2 == 0 else own_width)
+            third_term(t, 0, own_width if t in (WHOLE_TILE, H_TILES - 1) else V)
             if t % 2 == 1:
                 nc.vector.tensor_tensor(
                     two[:, t - 1 : t + 1, :], own_terms[t // 2][:, 0, :, :], own_terms[t // 2][:, 1, :, :], ADD
@@ -256,27 +262,27 @@ def tile_picked_hop2_gelu_e_kernel(
             if t == H_TILES - 1:
                 third_term(t, own_width, V)
 
-        def scalar_terms(t, first_list=0, end_list=D):
-            if t % 2 == 0 and first_list == 0:
-                for b in shared:
-                    turned[t // 2, b] = bank(TURN_BANKS[t // 2] + b, [P, D - 1, 2, P])
-            for d in range(first_list, min(end_list, D if t == WHOLE_TILE else D - 1)):
+        def scalar_terms(t, neighbours):
+            for d in neighbours:
+                if t % 2 == 0 and d == 0:
+                    for b in shared:
+                        turned[t // 2, b] = bank(TURN_BANKS[t // 2] + b, [P, D - 1, 2, P])
                 raw = keep.tile([P, shared_width], F32, name="raw%d_%d" % (t, d))
                 nc.scalar.activation(raw[:], h[t][:].indirect(entries(pos[d], own_width, shared_width)), COPY)
                 for b in shared:
                     dst = turned[t // 2, b][:, d, t % 2, :] if d < D - 1 else turned_third[:, b, :]
                     nc.tensor.transpose(dst, raw[:, block(b)], ident[:])
 
-        second, next_tile = products(1), products(2)
-        scalar_terms(0, 0, 1)
-        gelus(1, second)
-        scalar_terms(0, 1)
-        gelus(2, next_tile)
-        last = products(3)
+        accs = {t: products(t) for t in (1, 2)}
+        scalar_terms(0, [0])
+        gelus(1, accs[1])
+        scalar_terms(0, [1])
+        gelus(2, accs[2])
+        accs[3] = products(3)
         vector_terms(0)
-        scalar_terms(1)
-        gelus(3, last)
-        shared_back = [bank(SHARED_BACK_BANK + b, [P, H_TILES, P]) for b in shared]
+        scalar_terms(WHOLE_TILE, range(D))
+        gelus(3, accs[3])
+        shared_back = [bank(BACK_BANK + b, [P, H_TILES, P]) for b in shared]
 
         def gate_and_turn_back(pair, b):
             gated = keep.tile([P, D - 1, 2, P], F32, name="gated%d_%d" % (pair, b), align_bytes=64)
@@ -290,21 +296,13 @@ def tile_picked_hop2_gelu_e_kernel(
                 nc.scalar.activation(extra[:], turned_third[:, b, :], COPY, scale=gate_cols[D - 1][:, b : b + 1])
                 terms.append((WHOLE_TILE % 2, extra[:]))
             for n, (e, term) in enumerate(terms):
-                nc.tensor.matmul(
-                    shared_back[b][:, 2 * pair + e, :],
-                    term,
-                    ident[:],
-                    start=(n == 0),
-                    stop=(n == len(terms) - 1),
-                    is_transpose=True,
-                )
+                turn(shared_back[b][:, 2 * pair + e, :], term, n, len(terms) - 1)
 
         vector_terms(1)
         gate_and_turn_back(0, 0)
-        scalar_terms(2)
-        vector_terms(2)
-        scalar_terms(3)
-        vector_terms(3)
+        for t in (2, 3):
+            scalar_terms(t, range(D - 1))
+            vector_terms(t)
         gate_and_turn_back(0, 1)
         for b in shared:
             gate_and_turn_back(1, b)
@@ -335,7 +333,6 @@ def tile_picked_hop2_gelu_e_kernel(
             )
             nc.scalar.activation(g[m][:, cols], acc[:], RELU)
 
-        own_cols = slice(0, own_width)
         own_in = [add_third("own_in%d" % b, two[:, :, block(b)], block(b)) for b in range(OWN)]
         shared_in = [add_third("z_in%d" % b, shared_back[b][:], block(OWN + b)) for b in shared]
         own_codes = keep.tile([P, own_width], U32, name="own_codes", align_bytes=64)
@@ -343,20 +340,15 @@ def tile_picked_hop2_gelu_e_kernel(
         for b in range(OWN):
             quantize_z(own_codes[:, block(b)], own_in[b], block(b))
         for m in range(M_TILES):
-            second_layer(m, own_codes[:], own_cols, OWN_G_BANKS[m])
+            second_layer(m, own_codes[:], slice(0, own_width), OWN_G_BANKS[m])
         for b in shared:
             quantize_z(shared_codes[:, block(b)], shared_in[b], block(OWN + b))
-            second_layer(0, shared_codes[:, block(b)], block(OWN + b), SHARED_G_BANK + 1 + b)
-        second_layer(1, shared_codes[:], slice(own_width, V), SHARED_G_BANK + 3)
+            second_layer(0, shared_codes[:, block(b)], block(OWN + b), SHARED_G_BANKS[b])
+        second_layer(1, shared_codes[:], slice(own_width, V), SHARED_G_BANKS[2])
 
-        def turn(acc, term, b, d, last):
-            nc.tensor.matmul(acc, term[:, block(b)], ident[:], start=(d == 0), stop=(d == last), is_transpose=True)
-
-        def root_term(m, d, r0, width):
-            term = keep.tile([P, width], F32, name="root_term%d_%d_%d" % (m, d, r0))
-            nc.vector.tensor_tensor(
-                term[:], g[m][:].indirect(entries(nxt[d], r0, width)), gates2[:, d, r0 : r0 + width], MULT
-            )
+        def root_term(m, d):
+            term = keep.tile([P, U], F32, name="root_term%d_%d" % (m, d))
+            nc.vector.tensor_tensor(term[:], g[m][:].indirect(nxt[d][:]), gates2[:, d, :], MULT)
             return term
 
         def plain_term(dst, m, d):
@@ -368,16 +360,16 @@ def tile_picked_hop2_gelu_e_kernel(
         for d in range(D - 1):
             plain_term(plain[:, d, :], 1, d)
 
-        root_sums = [bank(ROOT_BANKS[b], [P, P]) for b in range(R_BLOCKS)]
-        plain_turned = bank(ROOT_PLAIN_BANK, [P, R_BLOCKS, P])
+        root_sums = [bank(ROOT_SUM_BANKS[b], [P, P]) for b in range(R_BLOCKS)]
+        plain_turned = bank(ROOT_TURN_BANK, [P, R_BLOCKS, P])
         for d in range(D - 1):
-            term = root_term(0, d, 0, U)
+            term = root_term(0, d)
             for b in range(R_BLOCKS):
-                turn(root_sums[b][:], term, b, d, D - 2)
+                turn(root_sums[b][:], term[:, block(b)], d, D - 2)
             if d == 0:
                 for b in range(R_BLOCKS):
                     nc.tensor.transpose(plain_turned[:, b, :], plain_first[:, block(b)], ident[:])
-        last_third = root_term(1, D - 1, 0, U)
+        last_third = root_term(1, D - 1)
         root_gated = keep.tile([P, R_BLOCKS, P], F32, name="root_gated")
         for b in range(R_BLOCKS):
             nc.scalar.activation(root_gated[:, b, :], plain_turned[:, b, :], COPY, scale=root_cols[:, b : b + 1])
@@ -385,19 +377,19 @@ def tile_picked_hop2_gelu_e_kernel(
             summed = keep.tile([P, P], F32, name="summed%d" % b)
             nc.scalar.copy(out=summed[:], in_=root_sums[b][:])
             back = bank(ROOT_BACK_BANKS[b], [P, P])
-            turn(back[:], root_gated[:, b, :], 0, 0, 1)
-            turn(back[:], summed, 0, 1, 1)
+            for n, term in enumerate((root_gated[:, b, :], summed[:])):
+                turn(back[:], term, n, 1)
             first_rows = keep.tile([P, P], F32, name="first_rows%d" % b)
             nc.scalar.copy(out=first_rows[:], in_=back[:])
             nc.scalar.dma_start(out[0:P, block(b)], first_rows[:])
 
-        terms = keep.tile([P, D - 1, U], F32, name="terms")
+        gated_plain = keep.tile([P, D - 1, U], F32, name="gated_plain")
         for d in range(D - 1):
-            nc.vector.tensor_tensor(terms[:, d, :], plain[:, d, :], gates2[:, d, :], MULT)
+            nc.vector.tensor_tensor(gated_plain[:, d, :], plain[:, d, :], gates2[:, d, :], MULT)
         root_part = keep.tile([P, U], F32, name="root_part")
         for b in range(R_BLOCKS):
-            nc.vector.tensor_tensor(root_part[:, block(b)], terms[:, 0, block(b)], last_third[:, block(b)], ADD)
+            nc.vector.tensor_tensor(root_part[:, block(b)], gated_plain[:, 0, block(b)], last_third[:, block(b)], ADD)
         for b in range(R_BLOCKS):
             last_rows = keep.tile([P, P], F32, name="last_rows%d" % b)
-            nc.vector.tensor_tensor(last_rows[:], root_part[:, block(b)], terms[:, 1, block(b)], ADD)
+            nc.vector.tensor_tensor(last_rows[:], root_part[:, block(b)], gated_plain[:, 1, block(b)], ADD)
             nc.sync.dma_start(out[P : 2 * P, block(b)], last_rows[:])

@@ -30,7 +30,7 @@ M_TILES = N // P
 BLOCKS = V // P
 R_BLOCKS = U // P
 OWN = 2
-VECTOR_GROUPS = (72, 32)
+VECTOR_GROUPS = (64, 32)
 WHOLE_TILE = 1
 
 H_BANKS = {1: (4, 5), 2: (6, 7), 3: (4, 5)}
@@ -91,8 +91,8 @@ def tile_picked_hop2_gelu_e_kernel(
             planes[j] = load_plane(j)
 
         rest = PIECE
-        low_rows = keep.tile([P, 6, P * PACK], BF16, name="low_rows", align_bytes=64)
-        direct = low_rows[:, 1:5, :].rearrange("p r c -> p (r c)")
+        low_rows = keep.tile([P, 8, P * PACK], BF16, name="low_rows", align_bytes=64)
+        direct = low_rows[:, 3:7, :].rearrange("p r c -> p (r c)")
         word_row = keep.tile([P, 2 * rest], U32, name="word_row")
         halves = word_row[:].bitcast(BF16)
         staged = keep.tile([P, PACK, PIECE], BF16, name="staged")
@@ -167,7 +167,7 @@ def tile_picked_hop2_gelu_e_kernel(
         nc.sync.dma_start(gates2[:], gate2.rearrange("d p r -> p d r"))
 
         high_rows = keep.tile([P, 2, P * PACK], BF16, name="high_rows", tag="w_pair1", align_bytes=64)
-        w_pairs = [rows.rearrange("p e (m j) -> p e m j", j=PACK) for rows in (low_rows[:, 0:6:5, :], high_rows[:])]
+        w_pairs = [rows.rearrange("p e (m j) -> p e m j", j=PACK) for rows in (low_rows[:, 0:8:7, :], high_rows[:])]
 
         def round_w1(copy, u, groups):
             copy(
@@ -194,12 +194,12 @@ def tile_picked_hop2_gelu_e_kernel(
         def gelu(t, c0, acc):
             nc.scalar.activation(h[t][:, c0 : c0 + acc.shape[1]], acc[:], GELU)
 
-        second_woven = keep.tile([P, PIECE * PACK], BF16, name="woven", align_bytes=64)
+        second_woven = low_rows[:, 1:3, :].rearrange("p r c -> p (r c)")
         nc.gpsimd.tensor_copy(
-            out=second_woven[:].bitcast(U32).rearrange("p (c u) -> p c u", u=2),
+            out=second_woven.bitcast(U32).rearrange("p (c u) -> p c u", u=2),
             in_=word_row[:].rearrange("p (u c) -> p c u", u=2),
         )
-        woven = [first_woven[:].rearrange("p c j -> p (c j)"), second_woven[:]]
+        woven = [first_woven[:].rearrange("p c j -> p (c j)"), second_woven]
         woven.extend(direct[:, n * PIECE * PACK : (n + 1) * PIECE * PACK] for n in range(2))
         for u in range(2):
             round_w1(nc.vector.tensor_copy, u, slice(0, VECTOR_GROUPS[u]))
@@ -214,7 +214,7 @@ def tile_picked_hop2_gelu_e_kernel(
             )
             gelu(0, e0, product(0, e0, PIECE, n))
 
-        quantize_w1(low_rows[:, 5, :], P, P)
+        quantize_w1(low_rows[:, 7, :], P, P)
         w1_codes.append(keep.tile([P, 2 * P], U32, name="high_codes", align_bytes=64))
         quantize_w1(high_rows[:].rearrange("p e c -> p (e c)"), 2 * P, 2 * P)
 

@@ -90,25 +90,24 @@ def tile_picked_hop2_gelu_e_kernel(
         for j in (0, 1, 3):
             planes[j] = load_plane(j)
 
-        rest = PIECE
+        paired = 2 * PIECE
         low_rows = keep.tile([P, 8, P * PACK], BF16, name="low_rows", align_bytes=64)
-        direct = low_rows[:, 3:7, :].rearrange("p r c -> p (r c)")
-        word_row = keep.tile([P, 2 * rest], U32, name="word_row")
+        direct = low_rows[:, 5:7, :].rearrange("p r c -> p (r c)")
+        word_row = keep.tile([P, 2 * paired], U32, name="word_row")
         halves = word_row[:].bitcast(BF16)
         staged = keep.tile([P, PACK, PIECE], BF16, name="staged")
         first_woven = keep.tile([P, PIECE, PACK], BF16, name="first_woven", align_bytes=64)
 
         def gather_half(j, e0, count):
-            first = 2 * (j // 2 * rest + e0 - PIECE)
+            first = 2 * (j // 2 * paired + e0 - PIECE)
             nc.vector.tensor_copy(
                 out=halves[:, first + j % 2 : first + 2 * count : 2],
                 in_=planes[j][:].indirect(entries(offs_t, e0, count)),
             )
 
-        def gather_direct(j, e0, count):
-            first = (e0 - 2 * PIECE) * PACK
+        def gather_direct(j):
             nc.vector.tensor_copy(
-                out=direct[:, first + j : first + count * PACK : PACK], in_=planes[j][:].indirect(entries(offs_t, e0, count))
+                out=direct[:, j : PIECE * PACK : PACK], in_=planes[j][:].indirect(entries(offs_t, S - PIECE, PIECE))
             )
 
         def gather_first(j):
@@ -118,14 +117,15 @@ def tile_picked_hop2_gelu_e_kernel(
             nc.scalar.copy(out=first_woven[:, :, j0:j1], in_=staged[:, j0:j1, :].rearrange("p j c -> p c j"))
 
         for j in (2, 0, 1):
-            gather_half(j, PIECE, rest)
-            gather_direct(j, 2 * PIECE, 2 * PIECE)
+            gather_half(j, PIECE, paired)
+            gather_direct(j)
             gather_first(j)
         place_first(0, PACK - 1)
         gather_first(PACK - 1)
         place_first(PACK - 1, PACK)
-        gather_half(PACK - 1, PIECE, rest)
-        gather_direct(PACK - 1, 2 * PIECE, 2 * PIECE)
+        for e0 in range(PIECE, S - PIECE, PIECE):
+            gather_half(PACK - 1, e0, PIECE)
+        gather_direct(PACK - 1)
 
         w_rows = w1.rearrange("(p j) c -> p j c", j=PACK)
         w1_codes = [keep.tile([P, 2 * P], U32, name="w1_codes", align_bytes=64)]
@@ -194,13 +194,14 @@ def tile_picked_hop2_gelu_e_kernel(
         def gelu(t, c0, acc):
             nc.scalar.activation(h[t][:, c0 : c0 + acc.shape[1]], acc[:], GELU)
 
-        second_woven = low_rows[:, 1:3, :].rearrange("p r c -> p (r c)")
-        nc.gpsimd.tensor_copy(
-            out=second_woven.bitcast(U32).rearrange("p (c u) -> p c u", u=2),
-            in_=word_row[:].rearrange("p (u c) -> p c u", u=2),
-        )
-        woven = [first_woven[:].rearrange("p c j -> p (c j)"), second_woven]
-        woven.extend(direct[:, n * PIECE * PACK : (n + 1) * PIECE * PACK] for n in range(2))
+        woven = [first_woven[:].rearrange("p c j -> p (c j)")]
+        for n in range(paired // PIECE):
+            woven.append(low_rows[:, 2 * n + 1 : 2 * n + 3, :].rearrange("p r c -> p (r c)"))
+            nc.gpsimd.tensor_copy(
+                out=woven[-1].bitcast(U32).rearrange("p (c u) -> p c u", u=2),
+                in_=word_row[:].rearrange("p (u c) -> p c u", u=2)[:, n * PIECE : (n + 1) * PIECE, :],
+            )
+        woven.append(direct)
         for u in range(2):
             round_w1(nc.vector.tensor_copy, u, slice(0, VECTOR_GROUPS[u]))
             round_w1(nc.scalar.copy, u, slice(VECTOR_GROUPS[u], P))

from contextlib import ExitStack

import concourse.mybir as mybir
from concourse.masks import make_identity

K, T, S, D, V, H, N, U = 512, 2048, 1024, 3, 512, 512, 256, 256
FLOPS = 2 * K * H * S + 2 * H * N * V

F32 = mybir.dt.float32
BF16 = mybir.dt.bfloat16
I32 = mybir.dt.int32
U32 = mybir.dt.uint32
U16 = mybir.dt.uint16
U8 = mybir.dt.uint8
FP8X4 = mybir.dt.float8_e4m3fn_x4
MULT = mybir.AluOpType.mult
ADD = mybir.AluOpType.add
GELU = mybir.ActivationFunctionType.Gelu_apprx_tanh
COPY = mybir.ActivationFunctionType.Copy
RELU = mybir.ActivationFunctionType.Relu

P = 128
PACK = 4
PER_COLUMN = 16
LINE = 4
PIECE = 256
BANK = 512
H_TILES = H // P
M_TILES = N // P
BLOCKS = V // P
R_BLOCKS = U // P
OWN = 2
VECTOR_GROUPS = (64, 32)
WHOLE_TILE = 1

H_BANKS = {1: (4, 5), 2: (6, 7), 3: (4, 5)}
TURN_BANKS = (2, 6)
THIRD_BANK = 0
BACK_BANK = 4
OWN_G_BANKS = (7, 6)
SHARED_G_BANKS = (1, 2, 3)
ROOT_TURN_BANK = 0
ROOT_SUM_BANKS = (4, 5)
ROOT_BACK_BANKS = (6, 7)


def tile_picked_hop2_gelu_e_kernel(
    tc, xT, w1, w2_words, w2_scales, gate, gate2, offs, pos1, pos2, pos3, nxt1, nxt2, nxt3, out
):
    nc = tc.nc

    with ExitStack() as ctx:
        keep = ctx.enter_context(tc.tile_pool(name="keep", bufs=1))
        psum = ctx.enter_context(tc.psum_pool(name="psum", bufs=1))

        def bank(n, shape):
            return psum.tile(shape, F32, name="bank", tag="bank%d" % n)

        def load_list(name, src):
            tile = keep.tile(list(src.shape), U16, name=name)
            nc.sync.dma_start(tile[:], src)
            return tile

        def entries(list_tile, first, count):
            return list_tile[:, first // PER_COLUMN : (first + count) // PER_COLUMN]

        def block(b):
            return slice(b * P, (b + 1) * P)

        def turn(acc, term, n, last):
            nc.tensor.matmul(acc, term, ident[:], start=(n == 0), stop=(n == last), is_transpose=True)

        ident = keep.tile([P, P], F32, name="ident")
        make_identity(nc, ident[:])
        warm = keep.tile([P, 2], F32, name="warm")
        nc.vector.memset(warm[:, 0:1], 0.0)
        nc.scalar.activation(warm[:, 1:2], warm[:, 0:1], GELU)
        w2_bytes = keep.tile([P, N], U8, name="w2_bytes", align_bytes=64)
        nc.gpsimd.memset(w2_bytes[:], 0)

        x_rows = xT.rearrange("(p j) c -> p j c", j=PACK)

        def load_plane(j):
            plane = keep.tile([P, T], F32, name="plane%d" % j)
            nc.sync.dma_start(plane[:], x_rows[:, j, :])
            return plane

        planes = {2: load_plane(2)}
        offs_t = load_list("offs_t", offs)
        for j in (0, 1, 3):
            planes[j] = load_plane(j)

        paired = 2 * PIECE
        low_rows = keep.tile([P, 8, P * PACK], BF16, name="low_rows", align_bytes=64)
        direct = low_rows[:, 5:7, :].rearrange("p r c -> p (r c)")
        word_row = keep.tile([P, 2 * paired], U32, name="word_row")
        halves = word_row[:].bitcast(BF16)
        staged = keep.tile([P, PACK, PIECE], BF16, name="staged")
        first_woven = keep.tile([P, PIECE, PACK], BF16, name="first_woven", align_bytes=64)

        def gather_half(j, e0, count):
            first = 2 * (j // 2 * paired + e0 - PIECE)
            nc.vector.tensor_copy(
                out=halves[:, first + j % 2 : first + 2 * count : 2],
                in_=planes[j][:].indirect(entries(offs_t, e0, count)),
            )

        def gather_direct(j):
            nc.vector.tensor_copy(
                out=direct[:, j : PIECE * PACK : PACK], in_=planes[j][:].indirect(entries(offs_t, S - PIECE, PIECE))
            )

        def gather_first(j):
            nc.scalar.activation(staged[:, j, :], planes[j][:].indirect(entries(offs_t, 0, PIECE)), COPY)

        def place_first(j0, j1):
            nc.scalar.copy(out=first_woven[:, :, j0:j1], in_=staged[:, j0:j1, :].rearrange("p j c -> p c j"))

        for j in (2, 0, 1):
            gather_half(j, PIECE, paired)
            gather_direct(j)
            gather_first(j)
        place_first(0, PACK - 1)
        gather_first(PACK - 1)
        place_first(PACK - 1, PACK)
        for e0 in range(PIECE, S - PIECE, PIECE):
            gather_half(PACK - 1, e0, PIECE)
        gather_direct(PACK - 1)

        w_rows = w1.rearrange("(p j) c -> p j c", j=PACK)
        w1_codes = [keep.tile([P, 2 * P], U32, name="w1_codes", align_bytes=64)]
        w1_bytes = keep.tile([P, H], U8, name="w1_bytes", align_bytes=64)

        w_raw = keep.tile([P, PACK, H], F32, name="w_raw")
        w_cols = w_raw[:].rearrange("p j (m f) -> p m j f", f=PACK)

        def quantize_w1(grouped, c0, width):
            nc.vector.quantize_mx(
                out=w1_codes[c0 // (2 * P)][:, c0 % (2 * P) : c0 % (2 * P) + width].bitcast(FP8X4),
                scales=w1_bytes[:, c0 : c0 + width],
                in_=grouped,
            )

        nc.sync.dma_start(w_raw[:], w_rows)
        pos = [load_list("pos%d" % d, src) for d, src in enumerate((pos1, pos2, pos3))]
        own_width = OWN * P
        own_gates = keep.tile([P, D - 1, own_width], F32, name="own_gates")
        nc.sync.dma_start(own_gates[:], gate[0 : D - 1, :, 0:own_width].rearrange("d p v -> p d v"))
        last_gates = keep.tile([P, V], F32, name="last_gates")
        nc.sync.dma_start(last_gates[:], gate[D - 1])
        gate_cols = [keep.tile([P, BLOCKS - OWN], F32, name="gate_cols%d" % d) for d in range(D)]
        with nc.allow_non_contiguous_dma(reason="one gate a partition"):
            for d in range(D):
                nc.sync.dma_start(gate_cols[d][:], gate[d, 0, own_width:V].rearrange("(b p) -> p b", p=P))
        w2_codes = keep.tile([P, N], U32, name="w2_codes", align_bytes=64)
        nc.sync.dma_start(w2_codes[:].bitcast(I32), w2_words[0].rearrange("p n t -> p (n t)").bitcast(I32))
        for quad in range(4):
            nc.sync.dma_start(
                w2_bytes[32 * quad : 32 * quad + 4, :].bitcast(I32),
                w2_scales[0, 4 * quad : 4 * quad + 4, :].bitcast(I32),
            )
        nxt = [load_list("nxt%d" % d, src) for d, src in enumerate((nxt1, nxt2, nxt3))]
        root_cols = keep.tile([P, R_BLOCKS], F32, name="root_cols")
        with nc.allow_non_contiguous_dma(reason="one gate a partition"):
            nc.sync.dma_start(root_cols[:], gate2[D - 1, 0, :].rearrange("(b p) -> p b", p=P))
        gates2 = keep.tile([P, D, U], F32, name="gates2")
        nc.sync.dma_start(gates2[:], gate2.rearrange("d p r -> p d r"))

        high_rows = keep.tile([P, 2, P * PACK], BF16, name="high_rows", tag="w_pair1", align_bytes=64)
        w_pairs = [rows.rearrange("p e (m j) -> p e m j", j=PACK) for rows in (low_rows[:, 0:8:7, :], high_rows[:])]

        def round_w1(copy, u, groups):
            copy(
                out=w_pairs[u][:, :, groups, :].rearrange("p e m j -> p m j e"),
                in_=w_cols[:, groups, :, 2 * u : 2 * u + 2],
            )

        x_bytes = keep.tile([P, S], U8, name="x_bytes", align_bytes=64)
        h = [keep.tile([P, S], F32, name="h%d" % t) for t in range(H_TILES)]

        def product(t, c0, width, n):
            acc = bank(n, [P, width])
            nc.tensor.matmul_mx(
                out=acc[:],
                lhsT=w1_codes[t // 2][:, block(t % 2)].bitcast(FP8X4),
                lhsT_scale=w1_bytes[:, block(t)],
                rhs=x_codes[c0 // BANK][:, c0 % BANK : c0 % BANK + width].bitcast(FP8X4),
                rhs_scale=x_bytes[:, c0 : c0 + width],
                start=True,
                stop=True,
            )
            return acc

        def gelu(t, c0, acc):
            nc.scalar.activation(h[t][:, c0 : c0 + acc.shape[1]], acc[:], GELU)

        woven = [first_woven[:].rearrange("p c j -> p (c j)")]
        for n in range(paired // PIECE):
            woven.append(low_rows[:, 2 * n + 1 : 2 * n + 3, :].rearrange("p r c -> p (r c)"))
            nc.gpsimd.tensor_copy(
                out=woven[-1].bitcast(U32).rearrange("p (c u) -> p c u", u=2),
                in_=word_row[:].rearrange("p (u c) -> p c u", u=2)[:, n * PIECE : (n + 1) * PIECE, :],
            )
        woven.append(direct)
        for u in range(2):
            round_w1(nc.vector.tensor_copy, u, slice(0, VECTOR_GROUPS[u]))
            round_w1(nc.scalar.copy, u, slice(VECTOR_GROUPS[u], P))
        quantize_w1(low_rows[:, 0, :], 0, P)
        x_codes = [keep.tile([P, BANK], U32, name="x_codes%d" % half, align_bytes=64) for half in range(2)]
        for n, e0 in enumerate(range(0, S, PIECE)):
            nc.vector.quantize_mx(
                out=x_codes[e0 // BANK][:, e0 % BANK : e0 % BANK + PIECE].bitcast(FP8X4),
                scales=x_bytes[:, e0 : e0 + PIECE],
                in_=woven[n],
            )
            gelu(0, e0, product(0, e0, PIECE, n))

        quantize_w1(low_rows[:, 7, :], P, P)
        w1_codes.append(keep.tile([P, 2 * P], U32, name="high_codes", align_bytes=64))
        quantize_w1(high_rows[:].rearrange("p e c -> p (e c)"), 2 * P, 2 * P)

        g = [keep.tile([P, V], F32, name="g%d" % m) for m in range(M_TILES)]
        z_bytes = keep.tile([P, V], U8, name="z_bytes", align_bytes=64)

        shared = range(BLOCKS - OWN)
        shared_width = V - own_width
        held = keep.tile([P, H_TILES * V + 2 * (D - 1) * own_width], F32, name="held", tag="w_pair1", align_bytes=64)
        third = held[:, 0 : H_TILES * V].rearrange("p (t v) -> p t v", t=H_TILES)
        later_terms = keep.tile([P, 2 * (D - 1) * own_width], F32, name="later_terms")
        own_terms = [
            rows.rearrange("p (d e v) -> p d e v", d=D - 1, e=2) for rows in (held[:, H_TILES * V :], later_terms[:])
        ]
        two = keep.tile([P, H_TILES, own_width], F32, name="two")
        turned = {}
        nc.gpsimd.memset(third[:, WHOLE_TILE, own_width:V], 0.0)
        turned_third = bank(THIRD_BANK, [P, BLOCKS - OWN, P])

        def products(t):
            return [product(t, c0, BANK, H_BANKS[t][c0 // BANK]) for c0 in range(0, S, BANK)]

        def gelus(t, halves_of_tile):
            for half, acc in enumerate(halves_of_tile):
                gelu(t, half * BANK, acc)

        def third_term(t, v0, v1):
            nc.vector.tensor_tensor(
                third[:, t, v0:v1], h[t][:].indirect(entries(pos[D - 1], v0, v1 - v0)), last_gates[:, v0:v1], MULT
            )

        def vector_terms(t):
            for d in range(D - 1):
                nc.vector.tensor_tensor(
                    own_terms[t // 2][:, d, t % 2, :],
                    h[t][:].indirect(entries(pos[d], 0, own_width)),
                    own_gates[:, d, :],
                    MULT,
                )
            third_term(t, 0, own_width if t in (WHOLE_TILE, H_TILES - 1) else V)
            if t % 2 == 1:
                nc.vector.tensor_tensor(
                    two[:, t - 1 : t + 1, :], own_terms[t // 2][:, 0, :, :], own_terms[t // 2][:, 1, :, :], ADD
                )
            if t == H_TILES - 1:
                third_term(t, own_width, V)

        def scalar_terms(t, neighbours):
            for d in neighbours:
                if t % 2 == 0 and d == 0:
                    for b in shared:
                        turned[t // 2, b] = bank(TURN_BANKS[t // 2] + b, [P, D - 1, 2, P])
                raw = keep.tile([P, shared_width], F32, name="raw%d_%d" % (t, d))
                nc.scalar.activation(raw[:], h[t][:].indirect(entries(pos[d], own_width, shared_width)), COPY)
                for b in shared:
                    dst = turned[t // 2, b][:, d, t % 2, :] if d < D - 1 else turned_third[:, b, :]
                    nc.tensor.transpose(dst, raw[:, block(b)], ident[:])

        accs = {t: products(t) for t in (1, 2)}
        scalar_terms(0, [0])
        gelus(1, accs[1])
        scalar_terms(0, [1])
        gelus(2, accs[2])
        accs[3] = products(3)
        vector_terms(0)
        scalar_terms(WHOLE_TILE, range(D))
        gelus(3, accs[3])
        shared_back = [bank(BACK_BANK + b, [P, H_TILES, P]) for b in shared]

        def gate_and_turn_back(pair, b):
            gated = keep.tile([P, D - 1, 2, P], F32, name="gated%d_%d" % (pair, b), align_bytes=64)
            for d in range(D - 1):
                nc.scalar.activation(
                    gated[:, d, :, :], turned[pair, b][:, d, :, :], COPY, scale=gate_cols[d][:, b : b + 1]
                )
            terms = [(e, gated[:, d, e, :]) for d in range(D - 1) for e in range(2)]
            if pair == WHOLE_TILE // 2:
                extra = keep.tile([P, P], F32, name="extra%d" % b)
                nc.scalar.activation(extra[:], turned_third[:, b, :], COPY, scale=gate_cols[D - 1][:, b : b + 1])
                terms.append((WHOLE_TILE % 2, extra[:]))
            for n, (e, term) in enumerate(terms):
                turn(shared_back[b][:, 2 * pair + e, :], term, n, len(terms) - 1)

        vector_terms(1)
        gate_and_turn_back(0, 0)
        for t in (2, 3):
            scalar_terms(t, range(D - 1))
            vector_terms(t)
        gate_and_turn_back(0, 1)
        for b in shared:
            gate_and_turn_back(1, b)

        def add_third(name, partial, cols):
            z_in = keep.tile([P, (cols.stop - cols.start) * PACK], BF16, name=name, align_bytes=64)
            nc.vector.tensor_tensor(
                z_in[:].rearrange("p (c i j) -> p c j i", i=LINE, j=PACK),
                partial.rearrange("p j (c i) -> p c j i", i=LINE),
                third[:, :, cols].rearrange("p j (c i) -> p c j i", i=LINE),
                ADD,
            )
            return z_in

        def quantize_z(codes, z_in, cols):
            nc.vector.quantize_mx(out=codes.bitcast(FP8X4), scales=z_bytes[:, cols], in_=z_in[:])

        def second_layer(m, codes, cols, n):
            acc = bank(n, [P, cols.stop - cols.start])
            nc.tensor.matmul_mx(
                out=acc[:],
                lhsT=w2_codes[:, block(m)].bitcast(FP8X4),
                lhsT_scale=w2_bytes[:, block(m)],
                rhs=codes.bitcast(FP8X4),
                rhs_scale=z_bytes[:, cols],
                start=True,
                stop=True,
            )
            nc.scalar.activation(g[m][:, cols], acc[:], RELU)

        own_in = [add_third("own_in%d" % b, two[:, :, block(b)], block(b)) for b in range(OWN)]
        shared_in = [add_third("z_in%d" % b, shared_back[b][:], block(OWN + b)) for b in shared]
        own_codes = keep.tile([P, own_width], U32, name="own_codes", align_bytes=64)
        shared_codes = keep.tile([P, shared_width], U32, name="shared_codes", tag="gated1_1", align_bytes=64)
        for b in range(OWN):
            quantize_z(own_codes[:, block(b)], own_in[b], block(b))
        for m in range(M_TILES):
            second_layer(m, own_codes[:], slice(0, own_width), OWN_G_BANKS[m])
        for b in shared:
            quantize_z(shared_codes[:, block(b)], shared_in[b], block(OWN + b))
            second_layer(0, shared_codes[:, block(b)], block(OWN + b), SHARED_G_BANKS[b])
        second_layer(1, shared_codes[:], slice(own_width, V), SHARED_G_BANKS[2])

        def root_term(m, d):
            term = keep.tile([P, U], F32, name="root_term%d_%d" % (m, d))
            nc.vector.tensor_tensor(term[:], g[m][:].indirect(nxt[d][:]), gates2[:, d, :], MULT)
            return term

        def plain_term(dst, m, d):
            nc.scalar.activation(dst, g[m][:].indirect(nxt[d][:]), COPY)

        plain_first = keep.tile([P, U], F32, name="plain_first")
        plain_term(plain_first[:], 0, D - 1)
        plain = keep.tile([P, D - 1, U], F32, name="plain")
        for d in range(D - 1):
            plain_term(plain[:, d, :], 1, d)

        root_sums = [bank(ROOT_SUM_BANKS[b], [P, P]) for b in range(R_BLOCKS)]
        plain_turned = bank(ROOT_TURN_BANK, [P, R_BLOCKS, P])
        for d in range(D - 1):
            term = root_term(0, d)
            for b in range(R_BLOCKS):
                turn(root_sums[b][:], term[:, block(b)], d, D - 2)
            if d == 0:
                for b in range(R_BLOCKS):
                    nc.tensor.transpose(plain_turned[:, b, :], plain_first[:, block(b)], ident[:])
        last_third = root_term(1, D - 1)
        root_gated = keep.tile([P, R_BLOCKS, P], F32, name="root_gated")
        for b in range(R_BLOCKS):
            nc.scalar.activation(root_gated[:, b, :], plain_turned[:, b, :], COPY, scale=root_cols[:, b : b + 1])
        for b in range(R_BLOCKS):
            summed = keep.tile([P, P], F32, name="summed%d" % b)
            nc.scalar.copy(out=summed[:], in_=root_sums[b][:])
            back = bank(ROOT_BACK_BANKS[b], [P, P])
            for n, term in enumerate((root_gated[:, b, :], summed[:])):
                turn(back[:], term, n, 1)
            first_rows = keep.tile([P, P], F32, name="first_rows%d" % b)
            nc.scalar.copy(out=first_rows[:], in_=back[:])
            nc.scalar.dma_start(out[0:P, block(b)], first_rows[:])

        gated_plain = keep.tile([P, D - 1, U], F32, name="gated_plain")
        for d in range(D - 1):
            nc.vector.tensor_tensor(gated_plain[:, d, :], plain[:, d, :], gates2[:, d, :], MULT)
        root_part = keep.tile([P, U], F32, name="root_part")
        for b in range(R_BLOCKS):
            nc.vector.tensor_tensor(root_part[:, block(b)], gated_plain[:, 0, block(b)], last_third[:, block(b)], ADD)
        for b in range(R_BLOCKS):
            last_rows = keep.tile([P, P], F32, name="last_rows%d" % b)
            nc.vector.tensor_tensor(last_rows[:], root_part[:, block(b)], gated_plain[:, 1, block(b)], ADD)
            nc.sync.dma_start(out[P : 2 * P, block(b)], last_rows[:])
